import numpy as np
import ml_dtypes


def mxq(x, axis, fmt="e4m3"):
    dtype, down = {"e4m3": (ml_dtypes.float8_e4m3fn, 7), "e5m2": (ml_dtypes.float8_e5m2, 14)}[fmt]
    v = np.moveaxis(np.asarray(x, np.float32).astype(ml_dtypes.bfloat16).astype(np.float64), axis, -1)
    blocks = v.reshape(v.shape[:-1] + (-1, 32))
    amax = np.abs(blocks).max(-1, keepdims=True)
    byte = np.maximum(np.where(amax > 0, np.frexp(amax)[1] - 1 + 127, 0) - down, 1)
    scale = np.exp2(byte - 127.0)
    codes = (blocks / scale).astype(np.float32).astype(dtype).astype(np.float64)
    return np.moveaxis((codes * scale).reshape(v.shape), -1, axis)


WIDE = False


def mx_kscale(k):
    if not WIDE:
        return np.ones(k)
    levels = np.array([10, -10, 5, -5, 0])
    if k % 512:
        return np.exp2(np.random.permutation(np.resize(levels, k // 32))).repeat(32)
    a = np.empty((k // 512, 16))
    for p in range(k // 512):
        a[p, :8] = np.random.permutation(np.resize(levels, 8))
        for g in range(8):
            far = levels[np.abs(levels - a[p, g]) >= 10]
            a[p, g + 8] = far[np.random.randint(len(far))]
    return np.exp2(a.ravel()).repeat(32)


BF16 = ml_dtypes.bfloat16


def bf(x):
    return np.asarray(x, np.float32).astype(BF16)


def f64(x):
    return np.asarray(x).astype(np.float64)


E2M1 = np.array([0.0, 0.5, 1.0, 1.5, 2.0, 3.0, 4.0, 6.0, -0.0, -0.5, -1.0, -1.5, -2.0, -3.0, -4.0, -6.0])


def pack_weight(w, fmt):
    k, n = w.shape
    w = f64(bf(w)).reshape(k // 32, 32, n)
    amax = np.abs(w).max(1)
    if fmt == "e4m3":
        byte = np.frexp(amax)[1] - 1 + 127 - 7
    else:
        mant, ex = np.frexp(amax / 6.0)
        byte = np.where(mant > 0.5, ex, ex - 1) + 127
    byte = np.clip(np.where(amax > 0, byte, 1), 1, 254)
    scaled = (w * np.exp2(127.0 - byte)[:, None, :]).reshape(k, n).astype(np.float32)
    by_word = np.ascontiguousarray(scaled.reshape(k // 512, 128, 4, n).transpose(0, 1, 3, 2))
    if fmt == "e4m3":
        words = by_word.astype(ml_dtypes.float8_e4m3fn).view(np.uint8)
    else:
        c = by_word.astype(ml_dtypes.float4_e2m1fn).view(np.uint8) & 0xF
        words = c[..., 0::2] | (c[..., 1::2] << 4)
    return np.ascontiguousarray(words), np.ascontiguousarray(byte.astype(np.uint8).reshape(k // 512, 16, n))


def unpack_weight(words, scales, fmt):
    g, p, n, _ = words.shape
    if fmt == "e4m3":
        vals = np.ascontiguousarray(words).view(ml_dtypes.float8_e4m3fn).astype(np.float64)
    else:
        nib = np.empty((g, p, n, 4), np.uint8)
        nib[..., 0::2] = words & 0xF
        nib[..., 1::2] = words >> 4
        vals = E2M1[nib]
    vals = vals * np.repeat(np.exp2(scales.astype(np.float64) - 127.0), 8, axis=1)[..., None]
    return vals.transpose(0, 1, 3, 2).reshape(g * 512, n)
def pack4(w):
    words, scales = pack_weight(w, "e2m1")
    return words.reshape(words.shape[0], 128, -1), scales


def unpack4(words, scales):
    return unpack_weight(words.reshape(words.shape[0], 128, -1, 2), scales, "e2m1")


N, D, E, SKIP = 1024, 512, 512, 512


def sigmoid(v):
    return 1.0 / (1.0 + np.exp(-v))


def draw0():
    sy, ss, t = mx_kscale(D), mx_kscale(E), mx_kscale(D)
    y = np.random.standard_normal((N, D)) * sy
    side = np.random.standard_normal((N, E)) * ss
    x = np.random.standard_normal((N, D))
    w_m = np.random.standard_normal((D, 2 * D)) / np.sqrt(D) / sy[:, None]
    w_s = np.random.standard_normal((E, 2 * D)) / np.sqrt(E) / ss[:, None]
    g = (1.0 + 0.1 * np.random.standard_normal(D)) * t
    w_o = 2.0 * np.random.standard_normal((D, D + SKIP)) / np.sqrt(D) / t[:, None]
    w_m_words, w_m_scales = pack4(w_m)
    w_s_words, w_s_scales = pack4(w_s)
    w_o_words, w_o_scales = pack4(w_o)
    return {"y": bf(y), "side": bf(side), "x": bf(x), "w_m_words": w_m_words, "w_m_scales": w_m_scales, "w_s_words": w_s_words, "w_s_scales": w_s_scales, "g": bf(g), "w_o_words": w_o_words, "w_o_scales": w_o_scales}


def core(y, side, x, w_m_words, w_m_scales, w_s_words, w_s_scales, g, w_o_words, w_o_scales):
    d = x.shape[-1]
    z = (mxq(f64(y), 1, "e4m3") @ unpack4(w_m_words, w_m_scales)) + (mxq(f64(side), 1, "e4m3") @ unpack4(w_s_words, w_s_scales))
    a = z[:, :d]
    c = z[:, d:]
    u = sigmoid(a) * np.tanh(c) * f64(g)[None, :]
    o = mxq(u, 1, "e4m3") @ unpack4(w_o_words, w_o_scales)
    xnew = (f64(x) + o[:, :d]) / np.sqrt(2.0)
    skip = o[:, d:]
    return xnew, skip


def e4m3fn_bytes(y):
    return np.clip(np.asarray(y, np.float64), -448.0, 448.0).astype(np.float32).astype(ml_dtypes.float8_e4m3fn).view(np.uint8)


def e4m3fn_values(b):
    return np.asarray(b, np.uint8).view(ml_dtypes.float8_e4m3fn).astype(np.float64)


def setup_inputs():
    d = draw0()
    x0 = np.asarray(d['y']).astype(np.float64)
    s = (np.max(np.abs(x0), axis=(0,), keepdims=True) / 448.0).astype(np.float32)
    out = {}
    for k, v in d.items():
        if k == 'y':
            out['y_bytes'] = e4m3fn_bytes(x0 / s.astype(np.float64))
            out['y_scale'] = s
        else:
            out[k] = v
    return out


def reference(y_bytes, y_scale, side, x, w_m_words, w_m_scales, w_s_words, w_s_scales, g, w_o_words, w_o_scales):
    return core(e4m3fn_values(y_bytes) * y_scale.astype(np.float64), side, x, w_m_words, w_m_scales, w_s_words, w_s_scales, g, w_o_words, w_o_scales)

@@ -1,0 +1,279 @@
+from contextlib import ExitStack
+
+import concourse.mybir as mybir
+from concourse.masks import make_identity
+
+N, D, E = 1024, 512, 512
+FLOPS = 2 * N * (D + E + D) * 2 * D
+
+F32 = mybir.dt.float32
+BF16 = mybir.dt.bfloat16
+U8 = mybir.dt.uint8
+U32 = mybir.dt.uint32
+I32 = mybir.dt.int32
+FP8 = mybir.dt.float8_e4m3fn
+FP8X4 = mybir.dt.float8_e4m3fn_x4
+FP4X4 = mybir.dt.float4_e2m1fn_x4
+MULT = mybir.AluOpType.mult
+ADD = mybir.AluOpType.add
+ACT = mybir.ActivationFunctionType
+
+P = 128
+TILES = N // P
+RSQRT2 = 0.5 ** 0.5
+EARLY = 2
+
+
+def tile_csdigatedsideinforesidual_w4_kernel(tc, y_bytes, y_scale, side, x, w_m_words, w_m_scales, w_s_words, w_s_scales, g, w_o_words, w_o_scales, out_0, out_1):
+    nc = tc.nc
+    with ExitStack() as ctx:
+        keep = ctx.enter_context(tc.tile_pool(name="keep", bufs=1))
+        work = ctx.enter_context(tc.tile_pool(name="work", bufs=4))
+        psum = ctx.enter_context(tc.psum_pool(name="psum", bufs=1))
+        ctx.enter_context(tc.manual_schedule())
+
+        y_v = y_bytes.rearrange("(p i) k -> p i k", i=TILES)
+        side_v = side.rearrange("(p i) k -> p i k", i=TILES)
+        x_v = x.rearrange("(p i) k -> p i k", i=TILES)
+        xnew_v = out_0.rearrange("(p i) k -> p i k", i=TILES)
+        skip_v = out_1.rearrange("(p i) k -> p i k", i=TILES)
+
+        ys_part = keep.tile([P, 4], F32, name="ys_part")
+        g_part = keep.tile([P, 4], BF16, name="g_part")
+        ys_all = keep.tile([P, D], F32, name="ys_all", align_bytes=64)
+        y_raw = keep.tile([P, TILES, D], U8, name="y_raw", align_bytes=64)
+        side_sb = keep.tile([P, TILES, E], BF16, name="side_sb", align_bytes=64)
+        x_sb = keep.tile([P, TILES, D], BF16, name="x_sb", align_bytes=64)
+        xs_sb = keep.tile([P, TILES, D], F32, name="xs_sb", align_bytes=64)
+        ident = keep.tile([P, P], F32, name="ident")
+        zeros = keep.tile([P, D], BF16, name="zeros", align_bytes=64)
+        warm = keep.tile([P, 1], F32, name="warm")
+        wm = keep.tile([P, 4 * D], U8, name="wm", align_bytes=64)
+        ws = keep.tile([P, 4 * D], U8, name="ws", align_bytes=64)
+        wo = keep.tile([P, 4 * D], U8, name="wo", align_bytes=64)
+        wm_sc = keep.tile([P, 2 * D], U8, name="wm_sc", align_bytes=64)
+        ws_sc = keep.tile([P, 2 * D], U8, name="ws_sc", align_bytes=64)
+        wo_sc = keep.tile([P, 2 * D], U8, name="wo_sc", align_bytes=64)
+
+        def load_scales(tile, dram):
+            for q in range(4):
+                nc.sync.dma_start(out=tile[32 * q : 32 * q + 4, :].bitcast(I32), in_=dram[0, 4 * q : 4 * q + 4, :].bitcast(I32))
+
+        def load_rows(tile, view, lo, hi):
+            nc.sync.dma_start(out=tile[:, lo:hi, :], in_=view[:, lo:hi, :])
+
+        nc.gpsimd.memset(zeros[:].bitcast(I32), 0)
+        make_identity(nc, ident[:])
+        nc.gpsimd.dma_start(out=side_sb[:, 2:4, :], in_=side_v[:, 2:4, :])
+        for t in (wm_sc, ws_sc, warm, wo_sc):
+            nc.vector.memset(t[:].bitcast(I32), 0)
+        nc.scalar.activation(out=warm[:], in_=warm[:], func=ACT.Sigmoid)
+
+        nc.sync.dma_start(out=ys_part[:], in_=y_scale.rearrange("o (p t) -> p (o t)", t=4))
+        load_rows(y_raw, y_v, 0, 4)
+        load_rows(side_sb, side_v, 0, 2)
+        load_scales(wm_sc, w_m_scales)
+        load_scales(ws_sc, w_s_scales)
+        nc.sync.dma_start(out=wm[:], in_=w_m_words[0])
+        nc.sync.dma_start(out=ws[:], in_=w_s_words[0])
+        load_rows(y_raw, y_v, 4, 8)
+        load_rows(side_sb, side_v, 4, 8)
+        nc.sync.dma_start(out=g_part[:], in_=g.rearrange("(p t) -> p t", t=4))
+        load_rows(x_sb, x_v, 0, 4)
+        load_scales(wo_sc, w_o_scales)
+        nc.sync.dma_start(out=wo[:], in_=w_o_words[0])
+        load_rows(x_sb, x_v, 4, 8)
+
+        warm_bank = psum.tile([P, D], F32, tag="bank", name="warm_bank", bufs=8)
+
+        def warm_up(n):
+            for k in range(n):
+                nc.tensor.matmul(warm_bank[:], lhsT=zeros[:, 0:P], rhs=zeros[:], start=True, stop=True)
+
+        st = {}
+
+        def spread_scales():
+            bank = psum.tile([P, 4, P], F32, tag="bank", name="ysb", bufs=8)
+            for t in range(4):
+                nc.tensor.transpose(bank[:, t, :], ys_part[:, t : t + 1].to_broadcast([P, P]), ident[:])
+            nc.scalar.copy(out=ys_all[:].rearrange("p (n t) -> p n t", t=4), in_=bank[:].rearrange("p t n -> p n t"))
+
+        def yprod(i):
+            yb = work.tile([P, D], BF16, tag="yb", name="yb", bufs=6, align_bytes=64)
+            if i < EARLY:
+                nc.vector.tensor_copy(out=yb[:], in_=y_raw[:, i, :].bitcast(FP8))
+            else:
+                nc.vector.tensor_tensor(out=yb[:], in0=y_raw[:, i, :].bitcast(FP8), in1=ys_all[:], op=MULT)
+            st["yb", i] = yb
+
+        def turn(i):
+            yw = st["yb", i][:].bitcast(F32)
+            sw = side_sb[:, i, :].bitcast(F32)
+            bank = psum.tile([P, 4, P], F32, tag="bank", name="tb", bufs=8)
+            sbank = psum.tile([P, 4, P], F32, tag="bank", name="tsb", bufs=8) if i < EARLY else bank
+            for u in range(2):
+                nc.tensor.transpose(bank[:, u, :], yw[:, u : D // 2 : 2], ident[:])
+            for u in range(2):
+                nc.tensor.transpose(sbank[:, 2 + u, :], sw[:, u : D // 2 : 2], ident[:])
+            st["tb", i] = (bank, sbank)
+            st["grp", i] = work.tile([P, 2, P, 4], BF16, tag="grp", name="grp", bufs=6, align_bytes=64)
+
+        def evac(i):
+            bank, sbank = st["tb", i]
+            lo = 1 if i < EARLY else 0
+            gw = st["grp", i][:].rearrange("p o r j -> p (o r j)").bitcast(F32)
+            nc.scalar.copy(
+                out=gw.rearrange("p (o r u) -> p o r u", o=2, u=2)[:, lo:],
+                in_=sbank[:].rearrange("p (o u) r -> p o r u", o=2)[:, lo:],
+            )
+
+        def evac_y(i):
+            if i < EARLY:
+                bank, sbank = st["tb", i]
+                yt = bank[:, 0:2, :].rearrange("p u r -> p (u r)").bitcast(BF16)
+                nc.vector.tensor_tensor(
+                    out=st["grp", i][:, 0].rearrange("p r (u e) -> p r u e", e=2),
+                    in0=yt.rearrange("p (u r e) -> p r u e", u=2, e=2),
+                    in1=ys_part[:].rearrange("p (u e) -> p u e", e=2).unsqueeze(1).to_broadcast([P, P, 2, 2]),
+                    op=MULT,
+                )
+
+        def quant(i):
+            codes = work.tile([P, 2 * P], U32, tag="codes", name="codes", align_bytes=64)
+            scales = work.tile([P, 2 * P], U8, tag="scales", name="scales", align_bytes=64)
+            nc.vector.quantize_mx(out=codes[:].bitcast(FP8X4), scales=scales[:], in_=st["grp", i][:].rearrange("p o r j -> p (o r j)"))
+            st["q", i] = (codes, scales)
+
+        def mm_z(i, h):
+            codes, scales = st["q", i]
+            bank = psum.tile([P, D], F32, tag="bank", name="zb", bufs=8)
+            for o, (w, sc) in enumerate(((wm, wm_sc), (ws, ws_sc))):
+                nc.tensor.matmul_mx(
+                    out=bank[:],
+                    lhsT=codes[:, o * P : (o + 1) * P].bitcast(FP8X4),
+                    lhsT_scale=scales[:, o * P : (o + 1) * P],
+                    rhs=w[:, 2 * D * h : 2 * D * (h + 1)].bitcast(FP4X4),
+                    rhs_scale=sc[:, D * h : D * (h + 1)],
+                    start=(o == 0),
+                    stop=(o == 1),
+                )
+            st["z", h, i] = bank
+
+        def act(i, h):
+            name, func = (("sg", ACT.Sigmoid), ("th", ACT.Tanh))[h]
+            r = work.tile([P, 4, P], F32, tag=name, name=name, align_bytes=64)
+            nc.scalar.activation(out=r[:], in_=st["z", h, i][:].rearrange("p (m t) -> p t m", t=4), func=func)
+            st[name, i] = r
+
+        def uprod(i):
+            u = work.tile([P, 4, P], F32, tag="u", name="u", align_bytes=64)
+            nc.vector.tensor_tensor(out=u[:], in0=st["sg", i][:], in1=st["th", i][:], op=MULT)
+            st["u", i] = u
+
+        def turn_u(i):
+            bank = psum.tile([P, 4, P], F32, tag="bank", name="ut", bufs=8)
+            for t in range(4):
+                nc.tensor.transpose(bank[:, t, :], st["u", i][:, t, :], ident[:])
+            st["ut", i] = bank
+
+        def gain(i):
+            ug = work.tile([P, P, 4], BF16, tag="ug", name="ug", align_bytes=64)
+            nc.vector.tensor_tensor(
+                out=ug[:],
+                in0=st["ut", i][:].rearrange("p t r -> p r t"),
+                in1=g_part[:].unsqueeze(1).to_broadcast([P, P, 4]),
+                op=MULT,
+            )
+            st["ug", i] = ug
+
+        def quant_u(i):
+            codes = work.tile([P, P], U32, tag="ucodes", name="ucodes", bufs=6, align_bytes=64)
+            scales = work.tile([P, P], U8, tag="uscales", name="uscales", bufs=6, align_bytes=64)
+            nc.vector.quantize_mx(out=codes[:].bitcast(FP8X4), scales=scales[:], in_=st["ug", i][:].rearrange("p r t -> p (r t)"))
+            st["uq", i] = (codes, scales)
+
+        def mm_o(i, h):
+            codes, scales = st["uq", i]
+            bank = psum.tile([P, D], F32, tag="bank", name="ob", bufs=8)
+            nc.tensor.matmul_mx(
+                out=bank[:],
+                lhsT=codes[:].bitcast(FP8X4),
+                lhsT_scale=scales[:],
+                rhs=wo[:, 2 * D * h : 2 * D * (h + 1)].bitcast(FP4X4),
+                rhs_scale=wo_sc[:, D * h : D * (h + 1)],
+                start=True,
+                stop=True,
+            )
+            st["o", h, i] = bank
+
+        def scale_x(i):
+            nc.scalar.activation(out=xs_sb[:, i, :], in_=x_sb[:, i, :], func=ACT.Copy, scale=RSQRT2)
+
+        def skip(i):
+            r = work.tile([P, D], F32, tag="sk", name="sk", align_bytes=64)
+            nc.scalar.copy(out=r[:], in_=st["o", 1, i][:])
+            nc.sync.dma_start(out=skip_v[:, i, :], in_=r[:])
+
+        def xnew(i):
+            r = work.tile([P, D], F32, tag="xn", name="xn", align_bytes=64)
+            nc.vector.scalar_tensor_tensor(out=r[:], in0=st["o", 0, i][:], scalar=RSQRT2, in1=xs_sb[:, i, :], op0=MULT, op1=ADD)
+            nc.sync.dma_start(out=xnew_v[:, i, :], in_=r[:])
+
+        warm_up(3)
+        spread_scales()
+        warm_up(1)
+        yprod(0)
+        yprod(1)
+        turn(0)
+        yprod(2)
+        turn(1)
+        evac(0)
+        evac_y(0)
+        turn(2)
+        warm_up(2)
+        yprod(3)
+        quant(0)
+        evac(1)
+        evac_y(1)
+        done = {(yprod, 0), (yprod, 1), (yprod, 2), (yprod, 3), (turn, 0), (turn, 1), (turn, 2), (evac, 0), (evac, 1), (quant, 0)}
+        order = (
+            (mm_z, -1, 1),
+            (mm_z, -1, 0),
+            (quant, -2),
+            (turn, -4),
+            (skip, 4),
+            (turn_u, 1),
+            (turn, -5),
+            (xnew, 4),
+            (uprod, 0),
+            (quant_u, 2),
+            (quant, -3),
+            (act, -1, 1),
+            (turn_u, 0),
+            (mm_z, -2, 0),
+            (act, -1, 0),
+            (evac, -4),
+            (scale_x, 0),
+            (evac, -5),
+            (yprod, -7),
+            (xnew, 3),
+            (gain, 1),
+            (gain, 0),
+            (mm_z, -2, 1),
+            (quant_u, 1),
+            (act, -2, 0),
+            (mm_o, 3, 1),
+            (act, -2, 1),
+            (mm_o, 2, 0),
+            (skip, 3),
+            (uprod, -1),
+            (mm_o, 2, 1),
+            (scale_x, 1),
+            (yprod, -6),
+            (mm_o, 1, 0),
+        )
+        for s in range(-5, 8):
+            for stage, lag, *args in order:
+                i = 2 * s - lag
+                if 0 <= i < TILES and (stage, i) not in done:
+                    stage(i, *args)

@@ -20,16 +20,16 @@ ACT = mybir.ActivationFunctionType
 
 P = 128
 TILES = N // P
+HALF = TILES // 2
 RSQRT2 = 0.5 ** 0.5
-EARLY = 2
 
 
 def tile_csdigatedsideinforesidual_w4_kernel(tc, y_bytes, y_scale, side, x, w_m_words, w_m_scales, w_s_words, w_s_scales, g, w_o_words, w_o_scales, out_0, out_1):
     nc = tc.nc
     with ExitStack() as ctx:
         keep = ctx.enter_context(tc.tile_pool(name="keep", bufs=1))
-        work = ctx.enter_context(tc.tile_pool(name="work", bufs=4))
-        psum = ctx.enter_context(tc.psum_pool(name="psum", bufs=1))
+        work = ctx.enter_context(tc.tile_pool(name="work", bufs=TILES))
+        psum = ctx.enter_context(tc.psum_pool(name="psum", bufs=8))
         ctx.enter_context(tc.manual_schedule())
 
         y_v = y_bytes.rearrange("(p i) k -> p i k", i=TILES)
@@ -41,10 +41,9 @@ def tile_csdigatedsideinforesidual_w4_kernel(tc, y_bytes, y_scale, side, x, w_m_
         ys_part = keep.tile([P, 4], F32, name="ys_part")
         g_part = keep.tile([P, 4], BF16, name="g_part")
         ys_all = keep.tile([P, D], F32, name="ys_all", align_bytes=64)
-        y_raw = keep.tile([P, TILES, D], U8, name="y_raw", align_bytes=64)
-        side_sb = keep.tile([P, TILES, E], BF16, name="side_sb", align_bytes=64)
-        x_sb = keep.tile([P, TILES, D], BF16, name="x_sb", align_bytes=64)
-        xs_sb = keep.tile([P, TILES, D], F32, name="xs_sb", align_bytes=64)
+        y_raw = [keep.tile([P, HALF, D], U8, name="y_raw%d" % h, align_bytes=64) for h in range(2)]
+        side_sb = [keep.tile([P, HALF, E], BF16, name="side_sb%d" % h, align_bytes=64) for h in range(2)]
+        x_sb = [keep.tile([P, HALF, D], BF16, name="x_sb%d" % h, align_bytes=64) for h in range(2)]
         ident = keep.tile([P, P], F32, name="ident")
         zeros = keep.tile([P, D], BF16, name="zeros", align_bytes=64)
         warm = keep.tile([P, 1], F32, name="warm")
@@ -59,84 +58,97 @@ def tile_csdigatedsideinforesidual_w4_kernel(tc, y_bytes, y_scale, side, x, w_m_
             for q in range(4):
                 nc.sync.dma_start(out=tile[32 * q : 32 * q + 4, :].bitcast(I32), in_=dram[0, 4 * q : 4 * q + 4, :].bitcast(I32))
 
-        def load_rows(tile, view, lo, hi):
-            nc.sync.dma_start(out=tile[:, lo:hi, :], in_=view[:, lo:hi, :])
+        def load_half(tiles, view, h):
+            nc.sync.dma_start(out=tiles[h][:], in_=view[:, HALF * h : HALF * (h + 1), :])
 
         nc.gpsimd.memset(zeros[:].bitcast(I32), 0)
         make_identity(nc, ident[:])
-        nc.gpsimd.dma_start(out=side_sb[:, 2:4, :], in_=side_v[:, 2:4, :])
         for t in (wm_sc, ws_sc, warm, wo_sc):
             nc.vector.memset(t[:].bitcast(I32), 0)
         nc.scalar.activation(out=warm[:], in_=warm[:], func=ACT.Sigmoid)
 
         nc.sync.dma_start(out=ys_part[:], in_=y_scale.rearrange("o (p t) -> p (o t)", t=4))
-        load_rows(y_raw, y_v, 0, 4)
-        load_rows(side_sb, side_v, 0, 2)
+        load_half(y_raw, y_v, 0)
+        load_half(side_sb, side_v, 0)
         load_scales(wm_sc, w_m_scales)
-        load_scales(ws_sc, w_s_scales)
         nc.sync.dma_start(out=wm[:], in_=w_m_words[0])
         nc.sync.dma_start(out=ws[:], in_=w_s_words[0])
-        load_rows(y_raw, y_v, 4, 8)
-        load_rows(side_sb, side_v, 4, 8)
+        load_scales(ws_sc, w_s_scales)
+        load_half(y_raw, y_v, 1)
+        load_half(side_sb, side_v, 1)
         nc.sync.dma_start(out=g_part[:], in_=g.rearrange("(p t) -> p t", t=4))
-        load_rows(x_sb, x_v, 0, 4)
+        load_half(x_sb, x_v, 0)
         load_scales(wo_sc, w_o_scales)
         nc.sync.dma_start(out=wo[:], in_=w_o_words[0])
-        load_rows(x_sb, x_v, 4, 8)
-
-        warm_bank = psum.tile([P, D], F32, tag="bank", name="warm_bank", bufs=8)
+        load_half(x_sb, x_v, 1)
 
         def warm_up(n):
+            bank = psum.tile([P, D], F32, tag="bank", name="warm_bank")
             for k in range(n):
-                nc.tensor.matmul(warm_bank[:], lhsT=zeros[:, 0:P], rhs=zeros[:], start=True, stop=True)
+                nc.tensor.matmul(bank[:], lhsT=zeros[:, 0:P], rhs=zeros[:], start=True, stop=True)
 
         st = {}
 
-        def spread_scales():
-            bank = psum.tile([P, 4, P], F32, tag="bank", name="ysb", bufs=8)
+        def spread_turn():
+            bank = psum.tile([P, 4, P], F32, tag="bank", name="ysb")
             for t in range(4):
                 nc.tensor.transpose(bank[:, t, :], ys_part[:, t : t + 1].to_broadcast([P, P]), ident[:])
-            nc.scalar.copy(out=ys_all[:].rearrange("p (n t) -> p n t", t=4), in_=bank[:].rearrange("p t n -> p n t"))
+            st["ysb"] = bank
+
+        def spread_copy():
+            nc.scalar.copy(out=ys_all[:].rearrange("p (n t) -> p n t", t=4), in_=st["ysb"][:].rearrange("p t n -> p n t"))
+
+        def y_codes(i):
+            return y_raw[i // HALF][:, i % HALF, :].bitcast(FP8)
+
+        def side_words(i):
+            return side_sb[i // HALF][:, i % HALF, :].bitcast(F32)
+
+        def widen(i):
+            yb = work.tile([P, D], BF16, tag="yb", name="yb", align_bytes=64)
+            nc.vector.tensor_copy(out=yb[:], in_=y_codes(i))
+            st["yb", i] = yb
+            st["grp", i] = work.tile([P, 2, P, 4], BF16, tag="grp", name="grp", align_bytes=64)
 
         def yprod(i):
-            yb = work.tile([P, D], BF16, tag="yb", name="yb", bufs=6, align_bytes=64)
-            if i < EARLY:
-                nc.vector.tensor_copy(out=yb[:], in_=y_raw[:, i, :].bitcast(FP8))
-            else:
-                nc.vector.tensor_tensor(out=yb[:], in0=y_raw[:, i, :].bitcast(FP8), in1=ys_all[:], op=MULT)
+            yb = work.tile([P, D], BF16, tag="yb", name="yb", align_bytes=64)
+            nc.vector.tensor_tensor(out=yb[:], in0=y_codes(i), in1=ys_all[:], op=MULT)
             st["yb", i] = yb
+            st["grp", i] = work.tile([P, 2, P, 4], BF16, tag="grp", name="grp", align_bytes=64)
+
+        def turn_two(first, second):
+            bank = psum.tile([P, 2, 2, P], F32, tag="bank", name="tb")
+            for o, words in enumerate((first, second)):
+                for u in range(2):
+                    nc.tensor.transpose(bank[:, o, u, :], words[:, u : D // 2 : 2], ident[:])
+            return bank
+
+        def turn_y(i):
+            st["ty", i] = turn_two(st["yb", i][:].bitcast(F32), st["yb", i + 1][:].bitcast(F32))
+
+        def turn_side(i):
+            st["ts", i] = turn_two(side_words(i), side_words(i + 1))
 
         def turn(i):
-            yw = st["yb", i][:].bitcast(F32)
-            sw = side_sb[:, i, :].bitcast(F32)
-            bank = psum.tile([P, 4, P], F32, tag="bank", name="tb", bufs=8)
-            sbank = psum.tile([P, 4, P], F32, tag="bank", name="tsb", bufs=8) if i < EARLY else bank
-            for u in range(2):
-                nc.tensor.transpose(bank[:, u, :], yw[:, u : D // 2 : 2], ident[:])
-            for u in range(2):
-                nc.tensor.transpose(sbank[:, 2 + u, :], sw[:, u : D // 2 : 2], ident[:])
-            st["tb", i] = (bank, sbank)
-            st["grp", i] = work.tile([P, 2, P, 4], BF16, tag="grp", name="grp", bufs=6, align_bytes=64)
+            st["tb", i] = turn_two(st["yb", i][:].bitcast(F32), side_words(i))
+
+        def grp_words(i):
+            return st["grp", i][:].rearrange("p o r j -> p (o r j)").bitcast(F32).rearrange("p (o r u) -> p o r u", o=2, u=2)
 
         def evac(i):
-            bank, sbank = st["tb", i]
-            lo = 1 if i < EARLY else 0
-            gw = st["grp", i][:].rearrange("p o r j -> p (o r j)").bitcast(F32)
-            nc.scalar.copy(
-                out=gw.rearrange("p (o r u) -> p o r u", o=2, u=2)[:, lo:],
-                in_=sbank[:].rearrange("p (o u) r -> p o r u", o=2)[:, lo:],
-            )
+            nc.scalar.copy(out=grp_words(i), in_=st["tb", i][:].rearrange("p o u r -> p o r u"))
+
+        def evac_side(i):
+            nc.scalar.copy(out=grp_words(i)[:, 1], in_=st["ts", i - i % 2][:, i % 2].rearrange("p u r -> p r u"))
 
         def evac_y(i):
-            if i < EARLY:
-                bank, sbank = st["tb", i]
-                yt = bank[:, 0:2, :].rearrange("p u r -> p (u r)").bitcast(BF16)
-                nc.vector.tensor_tensor(
-                    out=st["grp", i][:, 0].rearrange("p r (u e) -> p r u e", e=2),
-                    in0=yt.rearrange("p (u r e) -> p r u e", u=2, e=2),
-                    in1=ys_part[:].rearrange("p (u e) -> p u e", e=2).unsqueeze(1).to_broadcast([P, P, 2, 2]),
-                    op=MULT,
-                )
+            yt = st["ty", i - i % 2][:, i % 2].rearrange("p u r -> p (u r)").bitcast(BF16)
+            nc.vector.tensor_tensor(
+                out=st["grp", i][:, 0].rearrange("p r (u e) -> p r u e", e=2),
+                in0=yt.rearrange("p (u r e) -> p r u e", u=2, e=2),
+                in1=ys_part[:].rearrange("p (u e) -> p u e", e=2).unsqueeze(1).to_broadcast([P, P, 2, 2]),
+                op=MULT,
+            )
 
         def quant(i):
             codes = work.tile([P, 2 * P], U32, tag="codes", name="codes", align_bytes=64)
@@ -146,7 +158,7 @@ def tile_csdigatedsideinforesidual_w4_kernel(tc, y_bytes, y_scale, side, x, w_m_
 
         def mm_z(i, h):
             codes, scales = st["q", i]
-            bank = psum.tile([P, D], F32, tag="bank", name="zb", bufs=8)
+            bank = psum.tile([P, D], F32, tag="bank", name="zb")
             for o, (w, sc) in enumerate(((wm, wm_sc), (ws, ws_sc))):
                 nc.tensor.matmul_mx(
                     out=bank[:],
@@ -171,7 +183,7 @@ def tile_csdigatedsideinforesidual_w4_kernel(tc, y_bytes, y_scale, side, x, w_m_
             st["u", i] = u
 
         def turn_u(i):
-            bank = psum.tile([P, 4, P], F32, tag="bank", name="ut", bufs=8)
+            bank = psum.tile([P, 4, P], F32, tag="bank", name="ut")
             for t in range(4):
                 nc.tensor.transpose(bank[:, t, :], st["u", i][:, t, :], ident[:])
             st["ut", i] = bank
@@ -187,14 +199,14 @@ def tile_csdigatedsideinforesidual_w4_kernel(tc, y_bytes, y_scale, side, x, w_m_
             st["ug", i] = ug
 
         def quant_u(i):
-            codes = work.tile([P, P], U32, tag="ucodes", name="ucodes", bufs=6, align_bytes=64)
-            scales = work.tile([P, P], U8, tag="uscales", name="uscales", bufs=6, align_bytes=64)
+            codes = work.tile([P, P], U32, tag="ucodes", name="ucodes", align_bytes=64)
+            scales = work.tile([P, P], U8, tag="uscales", name="uscales", align_bytes=64)
             nc.vector.quantize_mx(out=codes[:].bitcast(FP8X4), scales=scales[:], in_=st["ug", i][:].rearrange("p r t -> p (r t)"))
             st["uq", i] = (codes, scales)
 
         def mm_o(i, h):
             codes, scales = st["uq", i]
-            bank = psum.tile([P, D], F32, tag="bank", name="ob", bufs=8)
+            bank = psum.tile([P, D], F32, tag="bank", name="ob")
             nc.tensor.matmul_mx(
                 out=bank[:],
                 lhsT=codes[:].bitcast(FP8X4),
@@ -207,7 +219,9 @@ def tile_csdigatedsideinforesidual_w4_kernel(tc, y_bytes, y_scale, side, x, w_m_
             st["o", h, i] = bank
 
         def scale_x(i):
-            nc.scalar.activation(out=xs_sb[:, i, :], in_=x_sb[:, i, :], func=ACT.Copy, scale=RSQRT2)
+            xs = work.tile([P, D], F32, tag="xs", name="xs", align_bytes=64)
+            nc.scalar.activation(out=xs[:], in_=x_sb[i // HALF][:, i % HALF, :], func=ACT.Copy, scale=RSQRT2)
+            st["xs", i] = xs
 
         def skip(i):
             r = work.tile([P, D], F32, tag="sk", name="sk", align_bytes=64)
@@ -216,64 +230,62 @@ def tile_csdigatedsideinforesidual_w4_kernel(tc, y_bytes, y_scale, side, x, w_m_
 
         def xnew(i):
             r = work.tile([P, D], F32, tag="xn", name="xn", align_bytes=64)
-            nc.vector.scalar_tensor_tensor(out=r[:], in0=st["o", 0, i][:], scalar=RSQRT2, in1=xs_sb[:, i, :], op0=MULT, op1=ADD)
+            nc.vector.scalar_tensor_tensor(out=r[:], in0=st["o", 0, i][:], scalar=RSQRT2, in1=st["xs", i][:], op0=MULT, op1=ADD)
             nc.sync.dma_start(out=xnew_v[:, i, :], in_=r[:])
 
+        def both(stage, i):
+            stage(i, 0)
+            stage(i, 1)
+
+        def on(stage, i, lo=0):
+            if lo <= i < TILES:
+                stage(i)
+
+        def z(i):
+            both(mm_z, i)
+
+        def a(i):
+            both(act, i)
+
+        def o(i):
+            both(mm_o, i)
+
         warm_up(3)
-        spread_scales()
-        warm_up(1)
-        yprod(0)
-        yprod(1)
-        turn(0)
-        yprod(2)
-        turn(1)
-        evac(0)
-        evac_y(0)
-        turn(2)
+        spread_turn()
+        spread_copy()
         warm_up(2)
-        yprod(3)
-        quant(0)
-        evac(1)
+        for i in range(HALF):
+            widen(i)
+        turn_y(0)
+        turn_side(0)
+        warm_up(2)
+        turn_y(2)
+        turn_side(2)
+        evac_y(0)
         evac_y(1)
-        done = {(yprod, 0), (yprod, 1), (yprod, 2), (yprod, 3), (turn, 0), (turn, 1), (turn, 2), (evac, 0), (evac, 1), (quant, 0)}
-        order = (
-            (mm_z, -1, 1),
-            (mm_z, -1, 0),
-            (quant, -2),
-            (turn, -4),
-            (skip, 4),
-            (turn_u, 1),
-            (turn, -5),
-            (xnew, 4),
-            (uprod, 0),
-            (quant_u, 2),
-            (quant, -3),
-            (act, -1, 1),
-            (turn_u, 0),
-            (mm_z, -2, 0),
-            (act, -1, 0),
-            (evac, -4),
-            (scale_x, 0),
-            (evac, -5),
-            (yprod, -7),
-            (xnew, 3),
-            (gain, 1),
-            (gain, 0),
-            (mm_z, -2, 1),
-            (quant_u, 1),
-            (act, -2, 0),
-            (mm_o, 3, 1),
-            (act, -2, 1),
-            (mm_o, 2, 0),
-            (skip, 3),
-            (uprod, -1),
-            (mm_o, 2, 1),
-            (scale_x, 1),
-            (yprod, -6),
-            (mm_o, 1, 0),
-        )
-        for s in range(-5, 8):
-            for stage, lag, *args in order:
-                i = 2 * s - lag
-                if 0 <= i < TILES and (stage, i) not in done:
-                    stage(i, *args)
+        evac_side(0)
+        evac_side(1)
+        quant(0)
+        quant(1)
+        evac_side(2)
+        evac_side(3)
+        evac_y(2)
+        evac_y(3)
+        quant(2)
+        quant(3)
+        TL, OL, F, XL = 2, 4, 3, 2
+        for s in range(TILES + OL):
+            on(z, s)
+            on(uprod, s - 1)
+            on(quant_u, s - TL - 1)
+            on(evac, s + F - 1, HALF)
+            on(o, s - OL)
+            on(a, s)
+            on(yprod, s + 4, HALF)
+            on(quant, s + 1, HALF)
+            on(turn_u, s - TL)
+            on(turn, s + F, HALF)
+            on(xnew, s - OL)
+            on(skip, s - OL)
+            on(gain, s - TL)
+            on(scale_x, s - XL)

@@ -40,7 +40,7 @@ def tile_csdigatedsideinforesidual_w4_kernel(tc, y_bytes, y_scale, side, x, w_m_
 
         ys_part = keep.tile([P, 4], F32, name="ys_part")
         g_part = keep.tile([P, 4], BF16, name="g_part")
-        ys_all = keep.tile([P, D], F32, name="ys_all", align_bytes=64)
+        ones = keep.tile([P, 1], F32, name="ones")
         y_raw = [keep.tile([P, HALF, D], U8, name="y_raw%d" % h, align_bytes=64) for h in range(2)]
         side_sb = [keep.tile([P, HALF, E], BF16, name="side_sb%d" % h, align_bytes=64) for h in range(2)]
         x_sb = [keep.tile([P, HALF, D], BF16, name="x_sb%d" % h, align_bytes=64) for h in range(2)]
@@ -65,11 +65,12 @@ def tile_csdigatedsideinforesidual_w4_kernel(tc, y_bytes, y_scale, side, x, w_m_
         make_identity(nc, ident[:])
         for t in (wm_sc, ws_sc, warm, wo_sc):
             nc.vector.memset(t[:].bitcast(I32), 0)
+        nc.vector.memset(ones[:], 1.0)
         nc.scalar.activation(out=warm[:], in_=warm[:], func=ACT.Sigmoid)
 
-        nc.sync.dma_start(out=ys_part[:], in_=y_scale.rearrange("o (p t) -> p (o t)", t=4))
         load_half(y_raw, y_v, 0)
         load_half(side_sb, side_v, 0)
+        nc.sync.dma_start(out=ys_part[:], in_=y_scale.rearrange("o (p t) -> p (o t)", t=4))
         load_scales(wm_sc, w_m_scales)
         nc.sync.dma_start(out=wm[:], in_=w_m_words[0])
         nc.sync.dma_start(out=ws[:], in_=w_s_words[0])
@@ -89,81 +90,60 @@ def tile_csdigatedsideinforesidual_w4_kernel(tc, y_bytes, y_scale, side, x, w_m_
 
         st = {}
 
-        def spread_turn():
-            bank = psum.tile([P, 4, P], F32, tag="bank", name="ysb")
-            for t in range(4):
-                nc.tensor.transpose(bank[:, t, :], ys_part[:, t : t + 1].to_broadcast([P, P]), ident[:])
-            st["ysb"] = bank
+        def widen(q):
+            yb = work.tile([P, 2, 2, P, 2], BF16, tag="yb", name="yb", bufs=HALF, align_bytes=64)
+            codes = y_raw[q // 2][:, 2 * (q % 2) : 2 * (q % 2) + 2, :].bitcast(FP8)
+            nc.vector.tensor_scalar(out=yb[:].rearrange("p u j m e -> p (j m) u e"), in0=codes.rearrange("p j (m u e) -> p (j m) u e", u=2, e=2), scalar1=ones[:], scalar2=None, op0=MULT)
+            st["yb", q] = yb
+            st["grp", q] = work.tile([P, 2, 2 * P, 4], BF16, tag="grp", name="grp", bufs=HALF, align_bytes=64)
 
-        def spread_copy():
-            nc.scalar.copy(out=ys_all[:].rearrange("p (n t) -> p n t", t=4), in_=st["ysb"][:].rearrange("p t n -> p n t"))
-
-        def y_codes(i):
-            return y_raw[i // HALF][:, i % HALF, :].bitcast(FP8)
-
-        def side_words(i):
-            return side_sb[i // HALF][:, i % HALF, :].bitcast(F32)
-
-        def widen(i):
-            yb = work.tile([P, D], BF16, tag="yb", name="yb", align_bytes=64)
-            nc.vector.tensor_copy(out=yb[:], in_=y_codes(i))
-            st["yb", i] = yb
-            st["grp", i] = work.tile([P, 2, P, 4], BF16, tag="grp", name="grp", align_bytes=64)
-
-        def yprod(i):
-            yb = work.tile([P, D], BF16, tag="yb", name="yb", align_bytes=64)
-            nc.vector.tensor_tensor(out=yb[:], in0=y_codes(i), in1=ys_all[:], op=MULT)
-            st["yb", i] = yb
-            st["grp", i] = work.tile([P, 2, P, 4], BF16, tag="grp", name="grp", align_bytes=64)
-
-        def turn_two(first, second):
-            bank = psum.tile([P, 2, 2, P], F32, tag="bank", name="tb")
-            for o, words in enumerate((first, second)):
+        def turn_y(q):
+            bank = psum.tile([P, 2, 2, P], F32, tag="bank", name="ty")
+            words = st["yb", q][:].rearrange("p j u m e -> p (j u m e)").bitcast(F32)
+            for j in range(2):
                 for u in range(2):
-                    nc.tensor.transpose(bank[:, o, u, :], words[:, u : D // 2 : 2], ident[:])
-            return bank
+                    nc.tensor.transpose(bank[:, u, j, :], words[:, (2 * u + j) * P : (2 * u + j + 1) * P], ident[:])
+            st["ty", q] = bank
 
-        def turn_y(i):
-            st["ty", i] = turn_two(st["yb", i][:].bitcast(F32), st["yb", i + 1][:].bitcast(F32))
+        def turn_side(q):
+            bank = psum.tile([P, 2, 2, P], F32, tag="bank", name="ts")
+            for j in range(2):
+                words = side_sb[q // 2][:, 2 * (q % 2) + j, :].bitcast(F32)
+                for u in range(2):
+                    nc.tensor.transpose(bank[:, u, j, :], words[:, u : D // 2 : 2], ident[:])
+            st["ts", q] = bank
 
-        def turn_side(i):
-            st["ts", i] = turn_two(side_words(i), side_words(i + 1))
+        def evac_side(q):
+            words = st["grp", q][:, 1].rearrange("p r t -> p (r t)").bitcast(F32)
+            nc.scalar.copy(out=words.rearrange("p (r u) -> p r u", u=2), in_=st["ts", q][:].rearrange("p u j r -> p (j r) u"))
 
-        def turn(i):
-            st["tb", i] = turn_two(st["yb", i][:].bitcast(F32), side_words(i))
-
-        def grp_words(i):
-            return st["grp", i][:].rearrange("p o r j -> p (o r j)").bitcast(F32).rearrange("p (o r u) -> p o r u", o=2, u=2)
-
-        def evac(i):
-            nc.scalar.copy(out=grp_words(i), in_=st["tb", i][:].rearrange("p o u r -> p o r u"))
-
-        def evac_side(i):
-            nc.scalar.copy(out=grp_words(i)[:, 1], in_=st["ts", i - i % 2][:, i % 2].rearrange("p u r -> p r u"))
-
-        def evac_y(i):
-            yt = st["ty", i - i % 2][:, i % 2].rearrange("p u r -> p (u r)").bitcast(BF16)
+        def evac_y(q, lo=0, hi=2):
+            n = (hi - lo) * P
+            yt = st["ty", q][:].rearrange("p u j r -> p (u j r)").bitcast(BF16).rearrange("p (u r e) -> p r u e", u=2, e=2)
             nc.vector.tensor_tensor(
-                out=st["grp", i][:, 0].rearrange("p r (u e) -> p r u e", e=2),
-                in0=yt.rearrange("p (u r e) -> p r u e", u=2, e=2),
-                in1=ys_part[:].rearrange("p (u e) -> p u e", e=2).unsqueeze(1).to_broadcast([P, P, 2, 2]),
+                out=st["grp", q][:, 0, lo * P : hi * P].rearrange("p r (u e) -> p r u e", e=2),
+                in0=yt[:, lo * P : hi * P],
+                in1=ys_part[:].rearrange("p (u e) -> p u e", e=2).unsqueeze(1).to_broadcast([P, n, 2, 2]),
                 op=MULT,
             )
 
-        def quant(i):
-            codes = work.tile([P, 2 * P], U32, tag="codes", name="codes", align_bytes=64)
-            scales = work.tile([P, 2 * P], U8, tag="scales", name="scales", align_bytes=64)
-            nc.vector.quantize_mx(out=codes[:].bitcast(FP8X4), scales=scales[:], in_=st["grp", i][:].rearrange("p o r j -> p (o r j)"))
-            st["q", i] = (codes, scales)
+        def quant(q, lo=0, hi=4):
+            if ("q", q) not in st:
+                codes = work.tile([P, 4 * P], U32, tag="codes", name="codes", bufs=HALF, align_bytes=64)
+                scales = work.tile([P, 4 * P], U8, tag="scales", name="scales", bufs=HALF, align_bytes=64)
+                st["q", q] = (codes, scales)
+            codes, scales = st["q", q]
+            grp = st["grp", q][:].rearrange("p o r t -> p (o r t)")
+            nc.vector.quantize_mx(out=codes[:, lo * P : hi * P].bitcast(FP8X4), scales=scales[:, lo * P : hi * P], in_=grp[:, lo * D : hi * D])
 
         def mm_z(i, h):
-            codes, scales = st["q", i]
+            codes, scales = st["q", i // 2]
             bank = psum.tile([P, D], F32, tag="bank", name="zb")
             for o, (w, sc) in enumerate(((wm, wm_sc), (ws, ws_sc))):
                 nc.tensor.matmul_mx(
                     out=bank[:],
-                    lhsT=codes[:, o * P : (o + 1) * P].bitcast(FP8X4),
-                    lhsT_scale=scales[:, o * P : (o + 1) * P],
+                    lhsT=codes[:, (2 * o + i % 2) * P : (2 * o + i % 2 + 1) * P].bitcast(FP8X4),
+                    lhsT_scale=scales[:, (2 * o + i % 2) * P : (2 * o + i % 2 + 1) * P],
                     rhs=w[:, 2 * D * h : 2 * D * (h + 1)].bitcast(FP4X4),
                     rhs_scale=sc[:, D * h : D * (h + 1)],
                     start=(o == 0),
@@ -177,9 +157,18 @@ def tile_csdigatedsideinforesidual_w4_kernel(tc, y_bytes, y_scale, side, x, w_m_
             nc.scalar.activation(out=r[:], in_=st["z", h, i][:].rearrange("p (m t) -> p t m", t=4), func=func)
             st[name, i] = r
 
+        def flat(tile):
+            if tile.dtype == F32:
+                return tile[:]
+            return tile[:, 0].rearrange("p r t -> p (r t)").bitcast(F32).rearrange("p (t m) -> p t m", t=4)
+
         def uprod(i):
-            u = work.tile([P, 4, P], F32, tag="u", name="u", align_bytes=64)
-            nc.vector.tensor_tensor(out=u[:], in0=st["sg", i][:], in1=st["th", i][:], op=MULT)
+            if i in (1, 2, 3, 4, 5, 6):
+                u = flat(st[behind[i]]) if i in behind else work.tile([P, 4, P], F32, tag="u", name="u", align_bytes=64)[:]
+                nc.gpsimd.tensor_tensor(out=u, in0=st["sg", i][:], in1=st["th", i][:], op=MULT)
+            else:
+                u = work.tile([P, 4, P], F32, tag="u", name="u", align_bytes=64)[:]
+                nc.vector.tensor_tensor(out=u, in0=st["sg", i][:], in1=st["th", i][:], op=MULT)
             st["u", i] = u
 
         def turn_u(i):
@@ -189,9 +178,9 @@ def tile_csdigatedsideinforesidual_w4_kernel(tc, y_bytes, y_scale, side, x, w_m_
             st["ut", i] = bank
 
         def gain(i):
-            ug = work.tile([P, P, 4], BF16, tag="ug", name="ug", align_bytes=64)
+            ug = work.tile([P, 4, P], F32, tag="ug", name="ug", align_bytes=64)
             nc.vector.tensor_tensor(
-                out=ug[:],
+                out=ug[:, 0:2].rearrange("p a b -> p (a b)").bitcast(BF16).rearrange("p (r t) -> p r t", t=4),
                 in0=st["ut", i][:].rearrange("p t r -> p r t"),
                 in1=g_part[:].unsqueeze(1).to_broadcast([P, P, 4]),
                 op=MULT,
@@ -201,7 +190,7 @@ def tile_csdigatedsideinforesidual_w4_kernel(tc, y_bytes, y_scale, side, x, w_m_
         def quant_u(i):
             codes = work.tile([P, P], U32, tag="ucodes", name="ucodes", align_bytes=64)
             scales = work.tile([P, P], U8, tag="uscales", name="uscales", align_bytes=64)
-            nc.vector.quantize_mx(out=codes[:].bitcast(FP8X4), scales=scales[:], in_=st["ug", i][:].rearrange("p r t -> p (r t)"))
+            nc.vector.quantize_mx(out=codes[:].bitcast(FP8X4), scales=scales[:], in_=st["ug", i][:, 0:2].rearrange("p a b -> p (a b)").bitcast(BF16))
             st["uq", i] = (codes, scales)
 
         def mm_o(i, h):
@@ -237,10 +226,6 @@ def tile_csdigatedsideinforesidual_w4_kernel(tc, y_bytes, y_scale, side, x, w_m_
             stage(i, 0)
             stage(i, 1)
 
-        def on(stage, i, lo=0):
-            if lo <= i < TILES:
-                stage(i)
-
         def z(i):
             both(mm_z, i)
 
@@ -250,42 +235,113 @@ def tile_csdigatedsideinforesidual_w4_kernel(tc, y_bytes, y_scale, side, x, w_m_
         def o(i):
             both(mm_o, i)
 
-        warm_up(3)
-        spread_turn()
-        spread_copy()
-        warm_up(2)
-        for i in range(HALF):
-            widen(i)
+        behind = {1: ("sg", 0), 2: ("grp", 2), 4: ("ug", 2), 6: ("ug", 3)}
+        warm_up(5)
+        widen(0)
+        widen(1)
         turn_y(0)
         turn_side(0)
+        turn_side(1)
+        turn_y(1)
         warm_up(2)
-        turn_y(2)
-        turn_side(2)
-        evac_y(0)
-        evac_y(1)
+        evac_y(0, 0, 1)
         evac_side(0)
+        evac_y(0, 1, 2)
+        quant(0, 0, 1)
+        quant(0, 2, 4)
+        quant(0, 1, 2)
         evac_side(1)
-        quant(0)
+        evac_y(1)
+        widen(2)
         quant(1)
+        z(0)
+        z(1)
+        a(0)
+        a(1)
+        uprod(0)
+        widen(3)
+        uprod(1)
+        turn_side(2)
+        turn_y(2)
+        turn_u(0)
         evac_side(2)
-        evac_side(3)
+        gain(0)
         evac_y(2)
-        evac_y(3)
+        scale_x(0)
+        quant_u(0)
         quant(2)
+        z(2)
+        z(3)
+        o(0)
+        a(2)
+        a(3)
+        uprod(2)
+        uprod(3)
+        turn_y(3)
+        turn_side(3)
+        turn_u(1)
+        turn_u(2)
+        xnew(0)
+        scale_x(1)
+        skip(0)
+        evac_y(3)
+        evac_side(3)
+        gain(1)
+        gain(2)
         quant(3)
-        TL, OL, F, XL = 2, 4, 3, 2
-        for s in range(TILES + OL):
-            on(z, s)
-            on(uprod, s - 1)
-            on(quant_u, s - TL - 1)
-            on(evac, s + F - 1, HALF)
-            on(o, s - OL)
-            on(a, s)
-            on(yprod, s + 4, HALF)
-            on(quant, s + 1, HALF)
-            on(turn_u, s - TL)
-            on(turn, s + F, HALF)
-            on(xnew, s - OL)
-            on(skip, s - OL)
-            on(gain, s - TL)
-            on(scale_x, s - XL)
+        quant_u(1)
+        quant_u(2)
+        z(4)
+        z(5)
+        scale_x(2)
+        a(4)
+        a(5)
+        uprod(4)
+        uprod(5)
+        turn_u(3)
+        gain(3)
+        o(1)
+        o(2)
+        z(6)
+        scale_x(3)
+        xnew(1)
+        xnew(2)
+        skip(1)
+        a(6)
+        skip(2)
+        quant_u(3)
+        uprod(6)
+        turn_u(4)
+        turn_u(5)
+        gain(4)
+        z(7)
+        o(3)
+        a(7)
+        gain(5)
+        xnew(3)
+        quant_u(4)
+        quant_u(5)
+        scale_x(4)
+        skip(3)
+        turn_u(6)
+        uprod(7)
+        o(4)
+        o(5)
+        turn_u(7)
+        gain(6)
+        scale_x(5)
+        xnew(4)
+        skip(4)
+        quant_u(6)
+        gain(7)
+        scale_x(6)
+        xnew(5)
+        skip(5)
+        o(6)
+        quant_u(7)
+        scale_x(7)
+        xnew(6)
+        skip(6)
+        o(7)
+        xnew(7)
+        skip(7)

@@ -157,18 +157,9 @@ def tile_csdigatedsideinforesidual_w4_kernel(tc, y_bytes, y_scale, side, x, w_m_
             nc.scalar.activation(out=r[:], in_=st["z", h, i][:].rearrange("p (m t) -> p t m", t=4), func=func)
             st[name, i] = r
 
-        def flat(tile):
-            if tile.dtype == F32:
-                return tile[:]
-            return tile[:, 0].rearrange("p r t -> p (r t)").bitcast(F32).rearrange("p (t m) -> p t m", t=4)
-
         def uprod(i):
-            if i in (1, 2, 3, 4, 5, 6):
-                u = flat(st[behind[i]]) if i in behind else work.tile([P, 4, P], F32, tag="u", name="u", align_bytes=64)[:]
-                nc.gpsimd.tensor_tensor(out=u, in0=st["sg", i][:], in1=st["th", i][:], op=MULT)
-            else:
-                u = work.tile([P, 4, P], F32, tag="u", name="u", align_bytes=64)[:]
-                nc.vector.tensor_tensor(out=u, in0=st["sg", i][:], in1=st["th", i][:], op=MULT)
+            u = work.tile([P, 4, P], F32, tag="u", name="u", align_bytes=64)[:]
+            nc.vector.tensor_tensor(out=u, in0=st["sg", i][:], in1=st["th", i][:], op=MULT)
             st["u", i] = u
 
         def turn_u(i):
@@ -178,9 +169,9 @@ def tile_csdigatedsideinforesidual_w4_kernel(tc, y_bytes, y_scale, side, x, w_m_
             st["ut", i] = bank
 
         def gain(i):
-            ug = work.tile([P, 4, P], F32, tag="ug", name="ug", align_bytes=64)
+            ug = work.tile([P, P, 4], BF16, tag="ug", name="ug", align_bytes=64)
             nc.vector.tensor_tensor(
-                out=ug[:, 0:2].rearrange("p a b -> p (a b)").bitcast(BF16).rearrange("p (r t) -> p r t", t=4),
+                out=ug[:],
                 in0=st["ut", i][:].rearrange("p t r -> p r t"),
                 in1=g_part[:].unsqueeze(1).to_broadcast([P, P, 4]),
                 op=MULT,
@@ -190,7 +181,7 @@ def tile_csdigatedsideinforesidual_w4_kernel(tc, y_bytes, y_scale, side, x, w_m_
         def quant_u(i):
             codes = work.tile([P, P], U32, tag="ucodes", name="ucodes", align_bytes=64)
             scales = work.tile([P, P], U8, tag="uscales", name="uscales", align_bytes=64)
-            nc.vector.quantize_mx(out=codes[:].bitcast(FP8X4), scales=scales[:], in_=st["ug", i][:, 0:2].rearrange("p a b -> p (a b)").bitcast(BF16))
+            nc.vector.quantize_mx(out=codes[:].bitcast(FP8X4), scales=scales[:], in_=st["ug", i][:].rearrange("p r t -> p (r t)"))
             st["uq", i] = (codes, scales)
 
         def mm_o(i, h):
@@ -233,9 +224,9 @@ def tile_csdigatedsideinforesidual_w4_kernel(tc, y_bytes, y_scale, side, x, w_m_
             both(act, i)
 
         def o(i):
-            both(mm_o, i)
+            mm_o(i, 1)
+            mm_o(i, 0)
 
-        behind = {1: ("sg", 0), 2: ("grp", 2), 4: ("ug", 2), 6: ("ug", 3)}
         warm_up(5)
         widen(0)
         widen(1)
@@ -276,72 +267,73 @@ def tile_csdigatedsideinforesidual_w4_kernel(tc, y_bytes, y_scale, side, x, w_m_
         a(2)
         a(3)
         uprod(2)
-        uprod(3)
         turn_y(3)
         turn_side(3)
         turn_u(1)
         turn_u(2)
+        skip(0)
+        uprod(3)
         xnew(0)
         scale_x(1)
-        skip(0)
-        evac_y(3)
         evac_side(3)
+        evac_y(3)
         gain(1)
         gain(2)
-        quant(3)
         quant_u(1)
-        quant_u(2)
         z(4)
         z(5)
+        o(1)
         scale_x(2)
         a(4)
         a(5)
         uprod(4)
-        uprod(5)
+        quant(3)
+        quant_u(2)
         turn_u(3)
-        gain(3)
-        o(1)
-        o(2)
-        z(6)
-        scale_x(3)
-        xnew(1)
-        xnew(2)
+        turn_u(4)
         skip(1)
+        uprod(5)
+        xnew(1)
+        gain(3)
+        gain(4)
+        quant_u(3)
+        z(6)
+        o(2)
+        z(7)
+        scale_x(3)
+        scale_x(4)
         a(6)
         skip(2)
-        quant_u(3)
-        uprod(6)
-        turn_u(4)
-        turn_u(5)
-        gain(4)
-        z(7)
-        o(3)
         a(7)
-        gain(5)
-        xnew(3)
+        xnew(2)
         quant_u(4)
-        quant_u(5)
-        scale_x(4)
-        skip(3)
+        uprod(6)
+        o(3)
+        turn_u(5)
         turn_u(6)
+        skip(3)
+        scale_x(5)
+        xnew(3)
         uprod(7)
+        gain(5)
         o(4)
-        o(5)
         turn_u(7)
         gain(6)
-        scale_x(5)
-        xnew(4)
+        quant_u(5)
         skip(4)
-        quant_u(6)
-        gain(7)
         scale_x(6)
-        xnew(5)
+        scale_x(7)
+        xnew(4)
+        quant_u(6)
+        o(5)
+        gain(7)
         skip(5)
         o(6)
+        xnew(5)
         quant_u(7)
-        scale_x(7)
-        xnew(6)
         skip(6)
-        o(7)
+        mm_o(7, 0)
+        mm_o(7, 1)
+        xnew(6)
         xnew(7)
         skip(7)

@@ -40,6 +40,7 @@ def tile_csdigatedsideinforesidual_w4_kernel(tc, y_bytes, y_scale, side, x, w_m_
 
         ys_part = keep.tile([P, 4], F32, name="ys_part")
         g_part = keep.tile([P, 4], BF16, name="g_part")
+        ys_all = keep.tile([P, D], F32, name="ys_all", align_bytes=64)
         ones = keep.tile([P, 1], F32, name="ones")
         y_raw = [keep.tile([P, HALF, D], U8, name="y_raw%d" % h, align_bytes=64) for h in range(2)]
         side_sb = [keep.tile([P, HALF, E], BF16, name="side_sb%d" % h, align_bytes=64) for h in range(2)]
@@ -58,8 +59,8 @@ def tile_csdigatedsideinforesidual_w4_kernel(tc, y_bytes, y_scale, side, x, w_m_
             for q in range(4):
                 nc.sync.dma_start(out=tile[32 * q : 32 * q + 4, :].bitcast(I32), in_=dram[0, 4 * q : 4 * q + 4, :].bitcast(I32))
 
-        def load_half(tiles, view, h):
-            nc.sync.dma_start(out=tiles[h][:], in_=view[:, HALF * h : HALF * (h + 1), :])
+        def load_rows(tile, view, lo, hi):
+            nc.sync.dma_start(out=tile[:], in_=view[:, lo:hi, :])
 
         nc.gpsimd.memset(zeros[:].bitcast(I32), 0)
         make_identity(nc, ident[:])
@@ -68,20 +69,20 @@ def tile_csdigatedsideinforesidual_w4_kernel(tc, y_bytes, y_scale, side, x, w_m_
         nc.vector.memset(ones[:], 1.0)
         nc.scalar.activation(out=warm[:], in_=warm[:], func=ACT.Sigmoid)
 
-        load_half(y_raw, y_v, 0)
-        load_half(side_sb, side_v, 0)
         nc.sync.dma_start(out=ys_part[:], in_=y_scale.rearrange("o (p t) -> p (o t)", t=4))
+        load_rows(y_raw[0], y_v, 0, 4)
+        load_rows(side_sb[0], side_v, 0, 4)
         load_scales(wm_sc, w_m_scales)
         nc.sync.dma_start(out=wm[:], in_=w_m_words[0])
         nc.sync.dma_start(out=ws[:], in_=w_s_words[0])
         load_scales(ws_sc, w_s_scales)
-        load_half(y_raw, y_v, 1)
-        load_half(side_sb, side_v, 1)
+        load_rows(y_raw[1], y_v, 4, 8)
+        load_rows(side_sb[1], side_v, 4, 8)
         nc.sync.dma_start(out=g_part[:], in_=g.rearrange("(p t) -> p t", t=4))
-        load_half(x_sb, x_v, 0)
         load_scales(wo_sc, w_o_scales)
         nc.sync.dma_start(out=wo[:], in_=w_o_words[0])
-        load_half(x_sb, x_v, 1)
+        load_rows(x_sb[0], x_v, 0, 4)
+        load_rows(x_sb[1], x_v, 4, 8)
 
         def warm_up(n):
             bank = psum.tile([P, D], F32, tag="bank", name="warm_bank")
@@ -89,6 +90,31 @@ def tile_csdigatedsideinforesidual_w4_kernel(tc, y_bytes, y_scale, side, x, w_m_
                 nc.tensor.matmul(bank[:], lhsT=zeros[:, 0:P], rhs=zeros[:], start=True, stop=True)
 
         st = {}
+
+        def spread_scales():
+            bank = psum.tile([P, 4, P], F32, tag="bank", name="ysb")
+            for t in range(4):
+                nc.tensor.transpose(bank[:, t, :], ys_part[:, t : t + 1].to_broadcast([P, P]), ident[:])
+            nc.scalar.copy(out=ys_all[:].rearrange("p (n t) -> p n t", t=4), in_=bank[:].rearrange("p t n -> p n t"))
+
+        def yprod(i):
+            q, j = divmod(i, 2)
+            if j == 0:
+                st["yb", q] = work.tile([P, 2, D], BF16, tag="yb", name="yb", bufs=HALF, align_bytes=64)
+                st["grp", q] = work.tile([P, 2, 2 * P, 4], BF16, tag="grp", name="grp", bufs=HALF, align_bytes=64)
+            nc.vector.tensor_tensor(out=st["yb", q][:, j, :], in0=y_raw[i // HALF][:, i % HALF, :].bitcast(FP8), in1=ys_all[:], op=MULT)
+
+        def turn_scaled(q):
+            bank = psum.tile([P, 2, 2, P], F32, tag="bank", name="ty")
+            for j in range(2):
+                words = st["yb", q][:, j, :].bitcast(F32)
+                for u in range(2):
+                    nc.tensor.transpose(bank[:, u, j, :], words[:, u : D // 2 : 2], ident[:])
+            st["ty", q] = bank
+
+        def evac_scaled(q):
+            words = st["grp", q][:, 0].rearrange("p r t -> p (r t)").bitcast(F32)
+            nc.scalar.copy(out=words.rearrange("p (r u) -> p r u", u=2), in_=st["ty", q][:].rearrange("p u j r -> p (j r) u"))
 
         def widen(q):
             yb = work.tile([P, 2, 2, P, 2], BF16, tag="yb", name="yb", bufs=HALF, align_bytes=64)
@@ -105,25 +131,38 @@ def tile_csdigatedsideinforesidual_w4_kernel(tc, y_bytes, y_scale, side, x, w_m_
                     nc.tensor.transpose(bank[:, u, j, :], words[:, (2 * u + j) * P : (2 * u + j + 1) * P], ident[:])
             st["ty", q] = bank
 
+        def sort_side(q):
+            first = 2 * (q % 2)
+            words = side_sb[q // 2][:, first : first + 2, :].rearrange("p j k -> p (j k)").bitcast(F32)
+            out = work.tile([P, 2, 2 * P], F32, tag="sw", name="sw", bufs=HALF, align_bytes=64)
+            nc.vector.tensor_copy(out=out[:].rearrange("p u m -> p m u"), in_=words.rearrange("p (m u) -> p m u", u=2))
+            st["sw", q] = out
+
         def turn_side(q):
             bank = psum.tile([P, 2, 2, P], F32, tag="bank", name="ts")
             for j in range(2):
-                words = side_sb[q // 2][:, 2 * (q % 2) + j, :].bitcast(F32)
                 for u in range(2):
-                    nc.tensor.transpose(bank[:, u, j, :], words[:, u : D // 2 : 2], ident[:])
+                    if ("sw", q) in st:
+                        nc.tensor.transpose(bank[:, u, j, :], st["sw", q][:, u, j * P : (j + 1) * P], ident[:])
+                    else:
+                        nc.tensor.transpose(bank[:, u, j, :], side_sb[q // 2][:, 2 * (q % 2) + j, :].bitcast(F32)[:, u : D // 2 : 2], ident[:])
             st["ts", q] = bank
 
         def evac_side(q):
             words = st["grp", q][:, 1].rearrange("p r t -> p (r t)").bitcast(F32)
             nc.scalar.copy(out=words.rearrange("p (r u) -> p r u", u=2), in_=st["ts", q][:].rearrange("p u j r -> p (j r) u"))
 
-        def evac_y(q, lo=0, hi=2):
-            n = (hi - lo) * P
-            yt = st["ty", q][:].rearrange("p u j r -> p (u j r)").bitcast(BF16).rearrange("p (u r e) -> p r u e", u=2, e=2)
+        def evac_raw(q):
+            raw = work.tile([P, 2 * P, 4], BF16, tag="yt", name="yt", bufs=HALF, align_bytes=64)
+            words = raw[:].rearrange("p r t -> p (r t)").bitcast(F32)
+            nc.scalar.copy(out=words.rearrange("p (r u) -> p r u", u=2), in_=st["ty", q][:].rearrange("p u j r -> p (j r) u"))
+            st["yt", q] = raw
+
+        def scale_y(q, lo=0, hi=2):
             nc.vector.tensor_tensor(
-                out=st["grp", q][:, 0, lo * P : hi * P].rearrange("p r (u e) -> p r u e", e=2),
-                in0=yt[:, lo * P : hi * P],
-                in1=ys_part[:].rearrange("p (u e) -> p u e", e=2).unsqueeze(1).to_broadcast([P, n, 2, 2]),
+                out=st["grp", q][:, 0, lo * P : hi * P],
+                in0=st["yt", q][:, lo * P : hi * P],
+                in1=ys_part[:].unsqueeze(1).to_broadcast([P, (hi - lo) * P, 4]),
                 op=MULT,
             )
 
@@ -152,14 +191,14 @@ def tile_csdigatedsideinforesidual_w4_kernel(tc, y_bytes, y_scale, side, x, w_m_
             st["z", h, i] = bank
 
         def act(i, h):
-            name, func = (("sg", ACT.Sigmoid), ("th", ACT.Tanh))[h]
-            r = work.tile([P, 4, P], F32, tag=name, name=name, align_bytes=64)
-            nc.scalar.activation(out=r[:], in_=st["z", h, i][:].rearrange("p (m t) -> p t m", t=4), func=func)
-            st[name, i] = r
+            if ("gate", i) not in st:
+                st["gate", i] = work.tile([P, 2, 4, P], F32, tag="gate", name="gate", align_bytes=64)
+            func = (ACT.Sigmoid, ACT.Tanh)[h]
+            nc.scalar.activation(out=st["gate", i][:, h], in_=st["z", h, i][:].rearrange("p (m t) -> p t m", t=4), func=func)
 
         def uprod(i):
-            u = work.tile([P, 4, P], F32, tag="u", name="u", align_bytes=64)[:]
-            nc.vector.tensor_tensor(out=u, in0=st["sg", i][:], in1=st["th", i][:], op=MULT)
+            u = work.tile([P, 4, P], F32, tag="u", name="u", align_bytes=64)
+            nc.vector.tensor_tensor(out=u[:], in0=st["gate", i][:, 0], in1=st["gate", i][:, 1], op=MULT)
             st["u", i] = u
 
         def turn_u(i):
@@ -201,7 +240,7 @@ def tile_csdigatedsideinforesidual_w4_kernel(tc, y_bytes, y_scale, side, x, w_m_
         def scale_x(i):
             xs = work.tile([P, D], F32, tag="xs", name="xs", align_bytes=64)
             nc.scalar.activation(out=xs[:], in_=x_sb[i // HALF][:, i % HALF, :], func=ACT.Copy, scale=RSQRT2)
-            st["xs", i] = xs
+            st["xs", i] = xs[:]
 
         def skip(i):
             r = work.tile([P, D], F32, tag="sk", name="sk", align_bytes=64)
@@ -210,7 +249,7 @@ def tile_csdigatedsideinforesidual_w4_kernel(tc, y_bytes, y_scale, side, x, w_m_
 
         def xnew(i):
             r = work.tile([P, D], F32, tag="xn", name="xn", align_bytes=64)
-            nc.vector.scalar_tensor_tensor(out=r[:], in0=st["o", 0, i][:], scalar=RSQRT2, in1=st["xs", i][:], op0=MULT, op1=ADD)
+            nc.vector.scalar_tensor_tensor(out=r[:], in0=st["o", 0, i][:], scalar=RSQRT2, in1=st["xs", i], op0=MULT, op1=ADD)
             nc.sync.dma_start(out=xnew_v[:, i, :], in_=r[:])
 
         def both(stage, i):
@@ -227,59 +266,69 @@ def tile_csdigatedsideinforesidual_w4_kernel(tc, y_bytes, y_scale, side, x, w_m_
             mm_o(i, 1)
             mm_o(i, 0)
 
-        warm_up(5)
+        warm_up(3)
+        spread_scales()
+        warm_up(2)
         widen(0)
         widen(1)
+        sort_side(0)
+        sort_side(1)
         turn_y(0)
+        turn_y(1)
         turn_side(0)
         turn_side(1)
-        turn_y(1)
         warm_up(2)
-        evac_y(0, 0, 1)
+        evac_raw(0)
         evac_side(0)
-        evac_y(0, 1, 2)
+        evac_raw(1)
+        evac_side(1)
+        scale_y(0, 0, 1)
+        scale_y(0, 1, 2)
         quant(0, 0, 1)
         quant(0, 2, 4)
         quant(0, 1, 2)
-        evac_side(1)
-        evac_y(1)
-        widen(2)
-        quant(1)
+        scale_y(1)
+        yprod(4)
+        yprod(5)
         z(0)
         z(1)
         a(0)
         a(1)
         uprod(0)
-        widen(3)
+        quant(1)
         uprod(1)
         turn_side(2)
-        turn_y(2)
+        turn_scaled(2)
         turn_u(0)
         evac_side(2)
+        evac_scaled(2)
+        yprod(6)
         gain(0)
-        evac_y(2)
-        scale_x(0)
+        yprod(7)
         quant_u(0)
         quant(2)
         z(2)
         z(3)
         o(0)
+        scale_x(0)
         a(2)
         a(3)
         uprod(2)
-        turn_y(3)
+        turn_scaled(3)
         turn_side(3)
         turn_u(1)
         turn_u(2)
         skip(0)
-        uprod(3)
         xnew(0)
+        uprod(3)
         scale_x(1)
+        evac_scaled(3)
         evac_side(3)
-        evac_y(3)
         gain(1)
         gain(2)
         quant_u(1)
+        quant(3)
+        quant_u(2)
         z(4)
         z(5)
         o(1)
@@ -287,21 +336,18 @@ def tile_csdigatedsideinforesidual_w4_kernel(tc, y_bytes, y_scale, side, x, w_m_
         a(4)
         a(5)
         uprod(4)
-        quant(3)
-        quant_u(2)
         turn_u(3)
         turn_u(4)
         skip(1)
-        uprod(5)
         xnew(1)
+        uprod(5)
+        scale_x(3)
         gain(3)
         gain(4)
         quant_u(3)
         z(6)
         o(2)
         z(7)
-        scale_x(3)
-        scale_x(4)
         a(6)
         skip(2)
         a(7)
@@ -312,7 +358,7 @@ def tile_csdigatedsideinforesidual_w4_kernel(tc, y_bytes, y_scale, side, x, w_m_
         turn_u(5)
         turn_u(6)
         skip(3)
-        scale_x(5)
+        scale_x(4)
         xnew(3)
         uprod(7)
         gain(5)
@@ -321,13 +367,14 @@ def tile_csdigatedsideinforesidual_w4_kernel(tc, y_bytes, y_scale, side, x, w_m_
         gain(6)
         quant_u(5)
         skip(4)
+        scale_x(5)
         scale_x(6)
-        scale_x(7)
         xnew(4)
         quant_u(6)
         o(5)
         gain(7)
         skip(5)
+        scale_x(7)
         o(6)
         xnew(5)
         quant_u(7)

@@ -40,7 +40,7 @@ def tile_csdigatedsideinforesidual_w4_kernel(tc, y_bytes, y_scale, side, x, w_m_
 
         ys_part = keep.tile([P, 4], F32, name="ys_part")
         g_part = keep.tile([P, 4], BF16, name="g_part")
-        ys_all = keep.tile([P, D], F32, name="ys_all", align_bytes=64)
+        ys_all = keep.tile([P, 2, D], F32, name="ys_all", align_bytes=64)
         ones = keep.tile([P, 1], F32, name="ones")
         y_raw = [keep.tile([P, HALF, D], U8, name="y_raw%d" % h, align_bytes=64) for h in range(2)]
         side_sb = [keep.tile([P, HALF, E], BF16, name="side_sb%d" % h, align_bytes=64) for h in range(2)]
@@ -95,94 +95,85 @@ def tile_csdigatedsideinforesidual_w4_kernel(tc, y_bytes, y_scale, side, x, w_m_
             bank = psum.tile([P, 4, P], F32, tag="bank", name="ysb")
             for t in range(4):
                 nc.tensor.transpose(bank[:, t, :], ys_part[:, t : t + 1].to_broadcast([P, P]), ident[:])
-            nc.scalar.copy(out=ys_all[:].rearrange("p (n t) -> p n t", t=4), in_=bank[:].rearrange("p t n -> p n t"))
-
-        def yprod(i):
-            q, j = divmod(i, 2)
-            if j == 0:
-                st["yb", q] = work.tile([P, 2, D], BF16, tag="yb", name="yb", bufs=HALF, align_bytes=64)
-                st["grp", q] = work.tile([P, 2, 2 * P, 4], BF16, tag="grp", name="grp", bufs=HALF, align_bytes=64)
-            nc.vector.tensor_tensor(out=st["yb", q][:, j, :], in0=y_raw[i // HALF][:, i % HALF, :].bitcast(FP8), in1=ys_all[:], op=MULT)
-
-        def turn_scaled(q):
-            bank = psum.tile([P, 2, 2, P], F32, tag="bank", name="ty")
             for j in range(2):
-                words = st["yb", q][:, j, :].bitcast(F32)
+                nc.scalar.copy(out=ys_all[:, j].rearrange("p (n t) -> p n t", t=4), in_=bank[:].rearrange("p t n -> p n t"))
+
+        def pair_tile(name, i, shape, dtype):
+            if (name, i // 2) not in st:
+                st[name, i // 2] = work.tile([P, 2] + shape, dtype, tag=name, name=name, bufs=HALF, align_bytes=64)
+            return st[name, i // 2]
+
+        def rows(tiles, i, n):
+            return tiles[i // HALF][:, i % HALF : i % HALF + n, :]
+
+        def widen(i):
+            yb = work.tile([P, 2, P, 2], BF16, tag="yw", name="yw", bufs=2, align_bytes=64)
+            nc.vector.tensor_scalar(
+                out=yb[:].rearrange("p u m e -> p m u e"),
+                in0=y_raw[0][:, i, :].bitcast(FP8).rearrange("p (m u e) -> p m u e", u=2, e=2),
+                scalar1=ones[:],
+                scalar2=None,
+                op0=MULT,
+            )
+            st["yw", i] = yb
+
+        def yprod(i, n=1):
+            yb = pair_tile("yb", i, [D], BF16)
+            nc.vector.tensor_tensor(out=yb[:, i % 2 : i % 2 + n], in0=rows(y_raw, i, n).bitcast(FP8), in1=ys_all[:, 0:n], op=MULT)
+
+        def turn_y(i):
+            bank = psum.tile([P, 2, P], F32, tag="bank", name="ty")
+            words = st["yw", i][:].rearrange("p u m e -> p u (m e)").bitcast(F32)
+            for u in range(2):
+                nc.tensor.transpose(bank[:, u, :], words[:, u, :], ident[:])
+            st["ty", i] = bank
+
+        def turn_two(first, second):
+            bank = psum.tile([P, 2, 2, P], F32, tag="bank", name="tb")
+            for o, src in enumerate((first, second)):
                 for u in range(2):
-                    nc.tensor.transpose(bank[:, u, j, :], words[:, u : D // 2 : 2], ident[:])
-            st["ty", q] = bank
+                    nc.tensor.transpose(bank[:, o, u, :], src.bitcast(F32)[:, u : D // 2 : 2], ident[:])
+            return bank
 
-        def evac_scaled(q):
-            words = st["grp", q][:, 0].rearrange("p r t -> p (r t)").bitcast(F32)
-            nc.scalar.copy(out=words.rearrange("p (r u) -> p r u", u=2), in_=st["ty", q][:].rearrange("p u j r -> p (j r) u"))
+        def turn_sides():
+            st["ts"] = turn_two(side_sb[0][:, 0, :], side_sb[0][:, 1, :])
 
-        def widen(q):
-            yb = work.tile([P, 2, 2, P, 2], BF16, tag="yb", name="yb", bufs=HALF, align_bytes=64)
-            codes = y_raw[q // 2][:, 2 * (q % 2) : 2 * (q % 2) + 2, :].bitcast(FP8)
-            nc.vector.tensor_scalar(out=yb[:].rearrange("p u j m e -> p (j m) u e"), in0=codes.rearrange("p j (m u e) -> p (j m) u e", u=2, e=2), scalar1=ones[:], scalar2=None, op0=MULT)
-            st["yb", q] = yb
-            st["grp", q] = work.tile([P, 2, 2 * P, 4], BF16, tag="grp", name="grp", bufs=HALF, align_bytes=64)
+        def turn(i):
+            st["tb", i] = turn_two(st["yb", i // 2][:, i % 2, :], side_sb[i // HALF][:, i % HALF, :])
 
-        def turn_y(q):
-            bank = psum.tile([P, 2, 2, P], F32, tag="bank", name="ty")
-            words = st["yb", q][:].rearrange("p j u m e -> p (j u m e)").bitcast(F32)
-            for j in range(2):
-                for u in range(2):
-                    nc.tensor.transpose(bank[:, u, j, :], words[:, (2 * u + j) * P : (2 * u + j + 1) * P], ident[:])
-            st["ty", q] = bank
+        def grp_words(i):
+            grp = pair_tile("grp", i, [2, P, 4], BF16)
+            return grp[:].rearrange("p j o r t -> p (j o r t)").bitcast(F32).rearrange("p (j o r u) -> p j o r u", j=2, o=2, u=2)
 
-        def sort_side(q):
-            first = 2 * (q % 2)
-            words = side_sb[q // 2][:, first : first + 2, :].rearrange("p j k -> p (j k)").bitcast(F32)
-            out = work.tile([P, 2, 2 * P], F32, tag="sw", name="sw", bufs=HALF, align_bytes=64)
-            nc.vector.tensor_copy(out=out[:].rearrange("p u m -> p m u"), in_=words.rearrange("p (m u) -> p m u", u=2))
-            st["sw", q] = out
+        def evac_sides():
+            nc.scalar.copy(out=grp_words(0)[:, :, 1], in_=st["ts"][:].rearrange("p j u r -> p j r u"))
 
-        def turn_side(q):
-            bank = psum.tile([P, 2, 2, P], F32, tag="bank", name="ts")
-            for j in range(2):
-                for u in range(2):
-                    if ("sw", q) in st:
-                        nc.tensor.transpose(bank[:, u, j, :], st["sw", q][:, u, j * P : (j + 1) * P], ident[:])
-                    else:
-                        nc.tensor.transpose(bank[:, u, j, :], side_sb[q // 2][:, 2 * (q % 2) + j, :].bitcast(F32)[:, u : D // 2 : 2], ident[:])
-            st["ts", q] = bank
+        def evac(i):
+            nc.scalar.copy(out=grp_words(i)[:, i % 2], in_=st["tb", i][:].rearrange("p o u r -> p o r u"))
 
-        def evac_side(q):
-            words = st["grp", q][:, 1].rearrange("p r t -> p (r t)").bitcast(F32)
-            nc.scalar.copy(out=words.rearrange("p (r u) -> p r u", u=2), in_=st["ts", q][:].rearrange("p u j r -> p (j r) u"))
-
-        def evac_raw(q):
-            raw = work.tile([P, 2 * P, 4], BF16, tag="yt", name="yt", bufs=HALF, align_bytes=64)
-            words = raw[:].rearrange("p r t -> p (r t)").bitcast(F32)
-            nc.scalar.copy(out=words.rearrange("p (r u) -> p r u", u=2), in_=st["ty", q][:].rearrange("p u j r -> p (j r) u"))
-            st["yt", q] = raw
-
-        def scale_y(q, lo=0, hi=2):
+        def evac_y(i):
+            yt = st["ty", i][:].rearrange("p u r -> p (u r)").bitcast(BF16)
             nc.vector.tensor_tensor(
-                out=st["grp", q][:, 0, lo * P : hi * P],
-                in0=st["yt", q][:, lo * P : hi * P],
-                in1=ys_part[:].unsqueeze(1).to_broadcast([P, (hi - lo) * P, 4]),
+                out=pair_tile("grp", i, [2, P, 4], BF16)[:, i, 0].rearrange("p r (u e) -> p r u e", e=2),
+                in0=yt.rearrange("p (u r e) -> p r u e", u=2, e=2),
+                in1=ys_part[:].rearrange("p (u e) -> p u e", e=2).unsqueeze(1).to_broadcast([P, P, 2, 2]),
                 op=MULT,
             )
 
-        def quant(q, lo=0, hi=4):
-            if ("q", q) not in st:
-                codes = work.tile([P, 4 * P], U32, tag="codes", name="codes", bufs=HALF, align_bytes=64)
-                scales = work.tile([P, 4 * P], U8, tag="scales", name="scales", bufs=HALF, align_bytes=64)
-                st["q", q] = (codes, scales)
-            codes, scales = st["q", q]
-            grp = st["grp", q][:].rearrange("p o r t -> p (o r t)")
-            nc.vector.quantize_mx(out=codes[:, lo * P : hi * P].bitcast(FP8X4), scales=scales[:, lo * P : hi * P], in_=grp[:, lo * D : hi * D])
+        def quant(i, n=1):
+            codes = pair_tile("codes", i, [2 * P], U32)[:, i % 2 : i % 2 + n].rearrange("p j c -> p (j c)")
+            scales = pair_tile("scales", i, [2 * P], U8)[:, i % 2 : i % 2 + n].rearrange("p j c -> p (j c)")
+            grp = st["grp", i // 2][:, i % 2 : i % 2 + n].rearrange("p j o r t -> p (j o r t)")
+            nc.vector.quantize_mx(out=codes.bitcast(FP8X4), scales=scales, in_=grp)
 
         def mm_z(i, h):
-            codes, scales = st["q", i // 2]
+            codes, scales = st["codes", i // 2][:, i % 2], st["scales", i // 2][:, i % 2]
             bank = psum.tile([P, D], F32, tag="bank", name="zb")
             for o, (w, sc) in enumerate(((wm, wm_sc), (ws, ws_sc))):
                 nc.tensor.matmul_mx(
                     out=bank[:],
-                    lhsT=codes[:, (2 * o + i % 2) * P : (2 * o + i % 2 + 1) * P].bitcast(FP8X4),
-                    lhsT_scale=scales[:, (2 * o + i % 2) * P : (2 * o + i % 2 + 1) * P],
+                    lhsT=codes[:, o * P : (o + 1) * P].bitcast(FP8X4),
+                    lhsT_scale=scales[:, o * P : (o + 1) * P],
                     rhs=w[:, 2 * D * h : 2 * D * (h + 1)].bitcast(FP4X4),
                     rhs_scale=sc[:, D * h : D * (h + 1)],
                     start=(o == 0),
@@ -191,45 +182,41 @@ def tile_csdigatedsideinforesidual_w4_kernel(tc, y_bytes, y_scale, side, x, w_m_
             st["z", h, i] = bank
 
         def act(i, h):
-            if ("gate", i) not in st:
-                st["gate", i] = work.tile([P, 2, 4, P], F32, tag="gate", name="gate", align_bytes=64)
-            func = (ACT.Sigmoid, ACT.Tanh)[h]
-            nc.scalar.activation(out=st["gate", i][:, h], in_=st["z", h, i][:].rearrange("p (m t) -> p t m", t=4), func=func)
+            name, func = (("sg", ACT.Sigmoid), ("th", ACT.Tanh))[h]
+            r = pair_tile(name, i, [4, P], F32)
+            nc.scalar.activation(out=r[:, i % 2], in_=st["z", h, i][:].rearrange("p (m t) -> p t m", t=4), func=func)
 
-        def uprod(i):
-            u = work.tile([P, 4, P], F32, tag="u", name="u", align_bytes=64)
-            nc.vector.tensor_tensor(out=u[:], in0=st["gate", i][:, 0], in1=st["gate", i][:, 1], op=MULT)
-            st["u", i] = u
+        def uprod(i, n=1):
+            u = pair_tile("u", i, [4, P], F32)
+            both_tiles = slice(i % 2, i % 2 + n)
+            nc.vector.tensor_tensor(out=u[:, both_tiles], in0=st["sg", i // 2][:, both_tiles], in1=st["th", i // 2][:, both_tiles], op=MULT)
 
         def turn_u(i):
             bank = psum.tile([P, 4, P], F32, tag="bank", name="ut")
             for t in range(4):
-                nc.tensor.transpose(bank[:, t, :], st["u", i][:, t, :], ident[:])
+                nc.tensor.transpose(bank[:, t, :], st["u", i // 2][:, i % 2, t, :], ident[:])
             st["ut", i] = bank
 
         def gain(i):
-            ug = work.tile([P, P, 4], BF16, tag="ug", name="ug", align_bytes=64)
             nc.vector.tensor_tensor(
-                out=ug[:],
+                out=pair_tile("ug", i, [P, 4], BF16)[:, i % 2],
                 in0=st["ut", i][:].rearrange("p t r -> p r t"),
                 in1=g_part[:].unsqueeze(1).to_broadcast([P, P, 4]),
                 op=MULT,
             )
-            st["ug", i] = ug
 
-        def quant_u(i):
-            codes = work.tile([P, P], U32, tag="ucodes", name="ucodes", align_bytes=64)
-            scales = work.tile([P, P], U8, tag="uscales", name="uscales", align_bytes=64)
-            nc.vector.quantize_mx(out=codes[:].bitcast(FP8X4), scales=scales[:], in_=st["ug", i][:].rearrange("p r t -> p (r t)"))
-            st["uq", i] = (codes, scales)
+        def quant_u(i, n=1):
+            codes = pair_tile("ucodes", i, [P], U32)[:, i % 2 : i % 2 + n].rearrange("p j c -> p (j c)")
+            scales = pair_tile("uscales", i, [P], U8)[:, i % 2 : i % 2 + n].rearrange("p j c -> p (j c)")
+            ug = st["ug", i // 2][:, i % 2 : i % 2 + n].rearrange("p j r t -> p (j r t)")
+            nc.vector.quantize_mx(out=codes.bitcast(FP8X4), scales=scales, in_=ug)
 
         def mm_o(i, h):
-            codes, scales = st["uq", i]
             bank = psum.tile([P, D], F32, tag="bank", name="ob")
             nc.tensor.matmul_mx(
                 out=bank[:],
-                lhsT=codes[:].bitcast(FP8X4),
-                lhsT_scale=scales[:],
+                lhsT=st["ucodes", i // 2][:, i % 2].bitcast(FP8X4),
+                lhsT_scale=st["uscales", i // 2][:, i % 2],
                 rhs=wo[:, 2 * D * h : 2 * D * (h + 1)].bitcast(FP4X4),
                 rhs_scale=wo_sc[:, D * h : D * (h + 1)],
                 start=True,
@@ -237,10 +224,11 @@ def tile_csdigatedsideinforesidual_w4_kernel(tc, y_bytes, y_scale, side, x, w_m_
             )
             st["o", h, i] = bank
 
-        def scale_x(i):
-            xs = work.tile([P, D], F32, tag="xs", name="xs", align_bytes=64)
-            nc.scalar.activation(out=xs[:], in_=x_sb[i // HALF][:, i % HALF, :], func=ACT.Copy, scale=RSQRT2)
-            st["xs", i] = xs[:]
+        def scale_x(i, n=2):
+            nc.scalar.activation(out=pair_tile("xs", i, [D], F32)[:, i % 2 : i % 2 + n], in_=rows(x_sb, i, n), func=ACT.Copy, scale=RSQRT2)
+
+        def scale_x_vector(i, n=2):
+            nc.vector.tensor_scalar(out=pair_tile("xs", i, [D], F32)[:, i % 2 : i % 2 + n], in0=rows(x_sb, i, n), scalar1=RSQRT2, scalar2=None, op0=MULT)
 
         def skip(i):
             r = work.tile([P, D], F32, tag="sk", name="sk", align_bytes=64)
@@ -249,7 +237,7 @@ def tile_csdigatedsideinforesidual_w4_kernel(tc, y_bytes, y_scale, side, x, w_m_
 
         def xnew(i):
             r = work.tile([P, D], F32, tag="xn", name="xn", align_bytes=64)
-            nc.vector.scalar_tensor_tensor(out=r[:], in0=st["o", 0, i][:], scalar=RSQRT2, in1=st["xs", i], op0=MULT, op1=ADD)
+            nc.vector.scalar_tensor_tensor(out=r[:], in0=st["o", 0, i][:], scalar=RSQRT2, in1=st["xs", i // 2][:, i % 2], op0=MULT, op1=ADD)
             nc.sync.dma_start(out=xnew_v[:, i, :], in_=r[:])
 
         def both(stage, i):
@@ -271,113 +259,100 @@ def tile_csdigatedsideinforesidual_w4_kernel(tc, y_bytes, y_scale, side, x, w_m_
         warm_up(2)
         widen(0)
         widen(1)
-        sort_side(0)
-        sort_side(1)
+        yprod(2)
         turn_y(0)
+        turn_sides()
         turn_y(1)
-        turn_side(0)
-        turn_side(1)
+        evac_y(0)
+        yprod(3)
+        turn(2)
         warm_up(2)
-        evac_raw(0)
-        evac_side(0)
-        evac_raw(1)
-        evac_side(1)
-        scale_y(0, 0, 1)
-        scale_y(0, 1, 2)
-        quant(0, 0, 1)
-        quant(0, 2, 4)
-        quant(0, 1, 2)
-        scale_y(1)
-        yprod(4)
-        yprod(5)
+        turn(3)
+        evac_sides()
+        evac(2)
+        evac(3)
+        quant(0)
+        evac_y(1)
+        quant(1)
+        yprod(4, 2)
         z(0)
         z(1)
         a(0)
         a(1)
+        quant(2, 2)
         uprod(0)
-        quant(1)
+        yprod(6, 2)
         uprod(1)
-        turn_side(2)
-        turn_scaled(2)
+        turn(4)
+        turn(5)
         turn_u(0)
-        evac_side(2)
-        evac_scaled(2)
-        yprod(6)
-        gain(0)
-        yprod(7)
-        quant_u(0)
-        quant(2)
+        evac(4)
+        evac(5)
+        quant(4, 2)
         z(2)
         z(3)
-        o(0)
-        scale_x(0)
         a(2)
         a(3)
-        uprod(2)
-        turn_scaled(3)
-        turn_side(3)
+        gain(0)
+        scale_x_vector(0)
         turn_u(1)
-        turn_u(2)
-        skip(0)
-        xnew(0)
-        uprod(3)
-        scale_x(1)
-        evac_scaled(3)
-        evac_side(3)
+        turn(6)
+        turn(7)
+        evac(6)
+        evac(7)
         gain(1)
-        gain(2)
-        quant_u(1)
-        quant(3)
-        quant_u(2)
+        uprod(2, 2)
+        quant_u(0, 2)
+        quant(6, 2)
+        scale_x_vector(2)
         z(4)
         z(5)
-        o(1)
-        scale_x(2)
         a(4)
         a(5)
-        uprod(4)
+        turn_u(2)
         turn_u(3)
-        turn_u(4)
+        o(0)
+        o(1)
+        skip(0)
         skip(1)
-        xnew(1)
-        uprod(5)
-        scale_x(3)
+        gain(2)
         gain(3)
-        gain(4)
-        quant_u(3)
+        xnew(0)
+        uprod(4, 2)
+        quant_u(2, 2)
+        xnew(1)
         z(6)
-        o(2)
         z(7)
         a(6)
-        skip(2)
         a(7)
-        xnew(2)
-        quant_u(4)
         uprod(6)
-        o(3)
+        turn_u(4)
         turn_u(5)
-        turn_u(6)
-        skip(3)
-        scale_x(4)
-        xnew(3)
-        uprod(7)
+        gain(4)
         gain(5)
-        o(4)
+        uprod(7)
+        o(2)
+        o(3)
+        skip(2)
+        skip(3)
+        quant_u(4, 2)
+        xnew(2)
+        xnew(3)
+        scale_x(4)
+        turn_u(6)
         turn_u(7)
-        gain(6)
-        quant_u(5)
-        skip(4)
-        scale_x(5)
-        scale_x(6)
-        xnew(4)
-        quant_u(6)
+        o(4)
         o(5)
+        skip(4)
+        gain(6)
         gain(7)
         skip(5)
-        scale_x(7)
-        o(6)
-        xnew(5)
+        quant_u(6)
+        xnew(4)
         quant_u(7)
+        xnew(5)
+        scale_x(6)
+        o(6)
         skip(6)
         mm_o(7, 0)
         mm_o(7, 1)

@@ -43,7 +43,7 @@ def tile_csdigatedsideinforesidual_w4_kernel(tc, y_bytes, y_scale, side, x, w_m_
         ys_all = keep.tile([P, 2, D], F32, name="ys_all", align_bytes=64)
         ones = keep.tile([P, 1], F32, name="ones")
         y_raw = [keep.tile([P, HALF, D], U8, name="y_raw%d" % h, align_bytes=64) for h in range(2)]
-        side_sb = [keep.tile([P, HALF, E], BF16, name="side_sb%d" % h, align_bytes=64) for h in range(2)]
+        side_sb = [keep.tile([P, n, E], BF16, name="side_sb%d" % h, align_bytes=64) for h, n in enumerate((2, 2, HALF))]
         x_sb = [keep.tile([P, HALF, D], BF16, name="x_sb%d" % h, align_bytes=64) for h in range(2)]
         ident = keep.tile([P, P], F32, name="ident")
         zeros = keep.tile([P, D], BF16, name="zeros", align_bytes=64)
@@ -64,6 +64,7 @@ def tile_csdigatedsideinforesidual_w4_kernel(tc, y_bytes, y_scale, side, x, w_m_
 
         nc.gpsimd.memset(zeros[:].bitcast(I32), 0)
         make_identity(nc, ident[:])
+        nc.gpsimd.dma_start(out=side_sb[1][:], in_=side_v[:, 2:4, :])
         for t in (wm_sc, ws_sc, warm, wo_sc):
             nc.vector.memset(t[:].bitcast(I32), 0)
         nc.vector.memset(ones[:], 1.0)
@@ -71,13 +72,13 @@ def tile_csdigatedsideinforesidual_w4_kernel(tc, y_bytes, y_scale, side, x, w_m_
 
         nc.sync.dma_start(out=ys_part[:], in_=y_scale.rearrange("o (p t) -> p (o t)", t=4))
         load_rows(y_raw[0], y_v, 0, 4)
-        load_rows(side_sb[0], side_v, 0, 4)
+        load_rows(side_sb[0], side_v, 0, 2)
         load_scales(wm_sc, w_m_scales)
+        load_scales(ws_sc, w_s_scales)
         nc.sync.dma_start(out=wm[:], in_=w_m_words[0])
         nc.sync.dma_start(out=ws[:], in_=w_s_words[0])
-        load_scales(ws_sc, w_s_scales)
         load_rows(y_raw[1], y_v, 4, 8)
-        load_rows(side_sb[1], side_v, 4, 8)
+        load_rows(side_sb[2], side_v, 4, 8)
         nc.sync.dma_start(out=g_part[:], in_=g.rearrange("(p t) -> p t", t=4))
         load_scales(wo_sc, w_o_scales)
         nc.sync.dma_start(out=wo[:], in_=w_o_words[0])
@@ -139,7 +140,7 @@ def tile_csdigatedsideinforesidual_w4_kernel(tc, y_bytes, y_scale, side, x, w_m_
             st["ts"] = turn_two(side_sb[0][:, 0, :], side_sb[0][:, 1, :])
 
         def turn(i):
-            st["tb", i] = turn_two(st["yb", i // 2][:, i % 2, :], side_sb[i // HALF][:, i % HALF, :])
+            st["tb", i] = turn_two(st["yb", i // 2][:, i % 2, :], side_sb[min(i // 2, 2)][:, i - 2 * min(i // 2, 2), :])
 
         def grp_words(i):
             grp = pair_tile("grp", i, [2, P, 4], BF16)
@@ -265,8 +266,8 @@ def tile_csdigatedsideinforesidual_w4_kernel(tc, y_bytes, y_scale, side, x, w_m_
         turn_y(1)
         evac_y(0)
         yprod(3)
-        turn(2)
         warm_up(2)
+        turn(2)
         turn(3)
         evac_sides()
         evac(2)

@@ -167,20 +167,29 @@ def tile_csdigatedsideinforesidual_w4_kernel(tc, y_bytes, y_scale, side, x, w_m_
             grp = st["grp", i // 2][:, i % 2 : i % 2 + n].rearrange("p j o r t -> p (j o r t)")
             nc.vector.quantize_mx(out=codes.bitcast(FP8X4), scales=scales, in_=grp)
 
-        def mm_z(i, h):
+        def z_pass(i, h, o):
             codes, scales = st["codes", i // 2][:, i % 2], st["scales", i // 2][:, i % 2]
-            bank = psum.tile([P, D], F32, tag="bank", name="zb")
-            for o, (w, sc) in enumerate(((wm, wm_sc), (ws, ws_sc))):
-                nc.tensor.matmul_mx(
-                    out=bank[:],
-                    lhsT=codes[:, o * P : (o + 1) * P].bitcast(FP8X4),
-                    lhsT_scale=scales[:, o * P : (o + 1) * P],
-                    rhs=w[:, 2 * D * h : 2 * D * (h + 1)].bitcast(FP4X4),
-                    rhs_scale=sc[:, D * h : D * (h + 1)],
-                    start=(o == 0),
-                    stop=(o == 1),
-                )
-            st["z", h, i] = bank
+            w, sc = ((wm, wm_sc), (ws, ws_sc))[o]
+            if o == 0:
+                st["z", h, i] = psum.tile([P, D], F32, tag="bank", name="zb")
+            nc.tensor.matmul_mx(
+                out=st["z", h, i][:],
+                lhsT=codes[:, o * P : (o + 1) * P].bitcast(FP8X4),
+                lhsT_scale=scales[:, o * P : (o + 1) * P],
+                rhs=w[:, 2 * D * h : 2 * D * (h + 1)].bitcast(FP4X4),
+                rhs_scale=sc[:, D * h : D * (h + 1)],
+                start=(o == 0),
+                stop=(o == 1),
+            )
+
+        def mm_z(i, h):
+            z_pass(i, h, 0)
+            z_pass(i, h, 1)
+
+        def z_by_operand(i):
+            for o in range(2):
+                for h in range(2):
+                    z_pass(i, h, o)
 
         def act(i, h):
             name, func = (("sg", ACT.Sigmoid), ("th", ACT.Tanh))[h]
@@ -266,7 +275,7 @@ def tile_csdigatedsideinforesidual_w4_kernel(tc, y_bytes, y_scale, side, x, w_m_
         turn_y(1)
         evac_y(0)
         yprod(3)
-        warm_up(2)
+        warm_up(4)
         turn(2)
         turn(3)
         evac_sides()
@@ -276,7 +285,7 @@ def tile_csdigatedsideinforesidual_w4_kernel(tc, y_bytes, y_scale, side, x, w_m_
         evac_y(1)
         quant(1)
         yprod(4, 2)
-        z(0)
+        z_by_operand(0)
         z(1)
         a(0)
         a(1)
@@ -286,7 +295,6 @@ def tile_csdigatedsideinforesidual_w4_kernel(tc, y_bytes, y_scale, side, x, w_m_
         uprod(1)
         turn(4)
         turn(5)
-        turn_u(0)
         evac(4)
         evac(5)
         quant(4, 2)
@@ -294,17 +302,16 @@ def tile_csdigatedsideinforesidual_w4_kernel(tc, y_bytes, y_scale, side, x, w_m_
         z(3)
         a(2)
         a(3)
-        gain(0)
         scale_x_vector(0)
+        turn_u(0)
         turn_u(1)
         turn(6)
-        turn(7)
         evac(6)
-        evac(7)
+        gain(0)
         gain(1)
         uprod(2, 2)
         quant_u(0, 2)
-        quant(6, 2)
+        quant(6)
         scale_x_vector(2)
         z(4)
         z(5)
@@ -312,6 +319,8 @@ def tile_csdigatedsideinforesidual_w4_kernel(tc, y_bytes, y_scale, side, x, w_m_
         a(5)
         turn_u(2)
         turn_u(3)
+        turn(7)
+        evac(7)
         o(0)
         o(1)
         skip(0)
@@ -319,6 +328,7 @@ def tile_csdigatedsideinforesidual_w4_kernel(tc, y_bytes, y_scale, side, x, w_m_
         gain(2)
         gain(3)
         xnew(0)
+        quant(7)
         uprod(4, 2)
         quant_u(2, 2)
         xnew(1)

@@ -343,30 +343,30 @@ def tile_csdigatedsideinforesidual_w4_kernel(tc, y_bytes, y_scale, side, x, w_m_
         gain(5)
         uprod(7)
         o(2)
-        o(3)
         skip(2)
+        turn_u(6)
+        o(3)
         skip(3)
         quant_u(4, 2)
         xnew(2)
         xnew(3)
         scale_x(4)
-        turn_u(6)
         turn_u(7)
         o(4)
         o(5)
         skip(4)
         gain(6)
-        gain(7)
+        warm_up(2)
         skip(5)
-        quant_u(6)
         xnew(4)
-        quant_u(7)
-        xnew(5)
+        quant_u(6)
         scale_x(6)
+        gain(7)
         o(6)
+        xnew(5)
         skip(6)
-        mm_o(7, 0)
-        mm_o(7, 1)
+        quant_u(7)
+        o(7)
         xnew(6)
-        xnew(7)
         skip(7)
+        xnew(7)

@@ -99,9 +99,9 @@ def tile_csdigatedsideinforesidual_w4_kernel(tc, y_bytes, y_scale, side, x, w_m_
             for j in range(2):
                 nc.scalar.copy(out=ys_all[:, j].rearrange("p (n t) -> p n t", t=4), in_=bank[:].rearrange("p t n -> p n t"))
 
-        def pair_tile(name, i, shape, dtype):
+        def pair_tile(name, i, shape, dtype, reuse=None):
             if (name, i // 2) not in st:
-                st[name, i // 2] = work.tile([P, 2] + shape, dtype, tag=name, name=name, bufs=HALF, align_bytes=64)
+                st[name, i // 2] = work.tile([P, 2] + shape, dtype, tag=reuse or "%s%d" % (name, i // 2), name=name, bufs=1, align_bytes=64)
             return st[name, i // 2]
 
         def rows(tiles, i, n):
@@ -240,6 +240,9 @@ def tile_csdigatedsideinforesidual_w4_kernel(tc, y_bytes, y_scale, side, x, w_m_
         def scale_x_vector(i, n=2):
             nc.vector.tensor_scalar(out=pair_tile("xs", i, [D], F32)[:, i % 2 : i % 2 + n], in0=rows(x_sb, i, n), scalar1=RSQRT2, scalar2=None, op0=MULT)
 
+        def scale_x_gpsimd(i, reuse):
+            nc.gpsimd.tensor_scalar(out=pair_tile("xs", i, [D], F32, reuse)[:], in0=rows(x_sb, i, 2), scalar1=RSQRT2, scalar2=0.0, op0=MULT, op1=ADD)
+
         def skip(i):
             r = work.tile([P, D], F32, tag="sk", name="sk", align_bytes=64)
             nc.scalar.copy(out=r[:], in_=st["o", 1, i][:])
@@ -302,7 +305,7 @@ def tile_csdigatedsideinforesidual_w4_kernel(tc, y_bytes, y_scale, side, x, w_m_
         z(3)
         a(2)
         a(3)
-        scale_x_vector(0)
+        scale_x_gpsimd(0, "grp2")
         turn_u(0)
         turn_u(1)
         turn(6)
@@ -312,7 +315,7 @@ def tile_csdigatedsideinforesidual_w4_kernel(tc, y_bytes, y_scale, side, x, w_m_
         uprod(2, 2)
         quant_u(0, 2)
         quant(6)
-        scale_x_vector(2)
+        scale_x_gpsimd(2, "ug0")
         z(4)
         z(5)
         a(4)

@@ -62,13 +62,13 @@ def tile_csdigatedsideinforesidual_w4_kernel(tc, y_bytes, y_scale, side, x, w_m_
         def load_rows(tile, view, lo, hi):
             nc.sync.dma_start(out=tile[:], in_=view[:, lo:hi, :])
 
+        nc.vector.memset(ones[:], 1.0)
+        nc.scalar.activation(out=warm[:], in_=ones[:], func=ACT.Sigmoid)
         nc.gpsimd.memset(zeros[:].bitcast(I32), 0)
         make_identity(nc, ident[:])
         nc.gpsimd.dma_start(out=side_sb[1][:], in_=side_v[:, 2:4, :])
-        for t in (wm_sc, ws_sc, warm, wo_sc):
+        for t in (wm_sc, ws_sc, wo_sc):
             nc.vector.memset(t[:].bitcast(I32), 0)
-        nc.vector.memset(ones[:], 1.0)
-        nc.scalar.activation(out=warm[:], in_=warm[:], func=ACT.Sigmoid)
 
         nc.sync.dma_start(out=ys_part[:], in_=y_scale.rearrange("o (p t) -> p (o t)", t=4))
         load_rows(y_raw[0], y_v, 0, 4)
@@ -108,7 +108,7 @@ def tile_csdigatedsideinforesidual_w4_kernel(tc, y_bytes, y_scale, side, x, w_m_
             return tiles[i // HALF][:, i % HALF : i % HALF + n, :]
 
         def widen(i):
-            yb = work.tile([P, 2, P, 2], BF16, tag="yw", name="yw", bufs=2, align_bytes=64)
+            yb = work.tile([P, 2, P, 2], BF16, tag="yw", name="yw", bufs=3, align_bytes=64)
             nc.vector.tensor_scalar(
                 out=yb[:].rearrange("p u m e -> p m u e"),
                 in0=y_raw[0][:, i, :].bitcast(FP8).rearrange("p (m u e) -> p m u e", u=2, e=2),
@@ -139,6 +139,12 @@ def tile_csdigatedsideinforesidual_w4_kernel(tc, y_bytes, y_scale, side, x, w_m_
         def turn_sides():
             st["ts"] = turn_two(side_sb[0][:, 0, :], side_sb[0][:, 1, :])
 
+        def turn_side(i):
+            bank = psum.tile([P, 2, P], F32, tag="bank", name="ts")
+            for u in range(2):
+                nc.tensor.transpose(bank[:, u, :], side_sb[1][:, i % 2, :].bitcast(F32)[:, u : D // 2 : 2], ident[:])
+            nc.scalar.copy(out=grp_words(i)[:, i % 2, 1], in_=bank[:].rearrange("p u r -> p r u"))
+
         def turn(i):
             st["tb", i] = turn_two(st["yb", i // 2][:, i % 2, :], side_sb[min(i // 2, 2)][:, i - 2 * min(i // 2, 2), :])
 
@@ -155,7 +161,7 @@ def tile_csdigatedsideinforesidual_w4_kernel(tc, y_bytes, y_scale, side, x, w_m_
         def evac_y(i):
             yt = st["ty", i][:].rearrange("p u r -> p (u r)").bitcast(BF16)
             nc.vector.tensor_tensor(
-                out=pair_tile("grp", i, [2, P, 4], BF16)[:, i, 0].rearrange("p r (u e) -> p r u e", e=2),
+                out=pair_tile("grp", i, [2, P, 4], BF16)[:, i % 2, 0].rearrange("p r (u e) -> p r u e", e=2),
                 in0=yt.rearrange("p (u r e) -> p r u e", u=2, e=2),
                 in1=ys_part[:].rearrange("p (u e) -> p u e", e=2).unsqueeze(1).to_broadcast([P, P, 2, 2]),
                 op=MULT,
@@ -200,6 +206,10 @@ def tile_csdigatedsideinforesidual_w4_kernel(tc, y_bytes, y_scale, side, x, w_m_
             u = pair_tile("u", i, [4, P], F32)
             both_tiles = slice(i % 2, i % 2 + n)
             nc.vector.tensor_tensor(out=u[:, both_tiles], in0=st["sg", i // 2][:, both_tiles], in1=st["th", i // 2][:, both_tiles], op=MULT)
+
+        def uprod_gpsimd(i, reuse=None):
+            u = pair_tile("u", i, [4, P], F32, reuse)
+            nc.gpsimd.tensor_tensor(out=u[:, i % 2], in0=st["sg", i // 2][:, i % 2], in1=st["th", i // 2][:, i % 2], op=MULT)
 
         def turn_u(i):
             bank = psum.tile([P, 4, P], F32, tag="bank", name="ut")
@@ -267,25 +277,27 @@ def tile_csdigatedsideinforesidual_w4_kernel(tc, y_bytes, y_scale, side, x, w_m_
             mm_o(i, 1)
             mm_o(i, 0)
 
-        warm_up(3)
+        warm_up(2)
         spread_scales()
         warm_up(2)
         widen(0)
         widen(1)
-        yprod(2)
+        widen(2)
         turn_y(0)
         turn_sides()
         turn_y(1)
+        evac_sides()
         evac_y(0)
         yprod(3)
-        warm_up(4)
-        turn(2)
+        warm_up(2)
+        turn_y(2)
+        turn_side(2)
         turn(3)
-        evac_sides()
-        evac(2)
         evac(3)
-        quant(0)
+        warm_up(1)
         evac_y(1)
+        quant(0)
+        evac_y(2)
         quant(1)
         yprod(4, 2)
         z_by_operand(0)
@@ -306,6 +318,7 @@ def tile_csdigatedsideinforesidual_w4_kernel(tc, y_bytes, y_scale, side, x, w_m_
         a(2)
         a(3)
         scale_x_gpsimd(0, "grp2")
+        scale_x_vector(2)
         turn_u(0)
         turn_u(1)
         turn(6)
@@ -313,13 +326,14 @@ def tile_csdigatedsideinforesidual_w4_kernel(tc, y_bytes, y_scale, side, x, w_m_
         gain(0)
         gain(1)
         uprod(2, 2)
-        quant_u(0, 2)
         quant(6)
-        scale_x_gpsimd(2, "ug0")
+        quant_u(0, 2)
         z(4)
         z(5)
         a(4)
         a(5)
+        uprod_gpsimd(4, "ug0")
+        uprod_gpsimd(5)
         turn_u(2)
         turn_u(3)
         turn(7)
@@ -332,43 +346,42 @@ def tile_csdigatedsideinforesidual_w4_kernel(tc, y_bytes, y_scale, side, x, w_m_
         gain(3)
         xnew(0)
         quant(7)
-        uprod(4, 2)
         quant_u(2, 2)
+        scale_x_gpsimd(4, "ug1")
         xnew(1)
         z(6)
-        z(7)
         a(6)
-        a(7)
-        uprod(6)
         turn_u(4)
         turn_u(5)
+        z(7)
+        a(7)
         gain(4)
         gain(5)
-        uprod(7)
+        uprod(6)
         o(2)
-        skip(2)
-        turn_u(6)
         o(3)
-        skip(3)
         quant_u(4, 2)
         xnew(2)
-        xnew(3)
-        scale_x(4)
-        turn_u(7)
+        skip(2)
+        turn_u(6)
+        uprod(7)
+        skip(3)
         o(4)
         o(5)
-        skip(4)
         gain(6)
-        warm_up(2)
+        skip(4)
+        turn_u(7)
+        xnew(3)
         skip(5)
-        xnew(4)
         quant_u(6)
         scale_x(6)
         gain(7)
+        warm_up(1)
         o(6)
-        xnew(5)
-        skip(6)
+        xnew(4)
         quant_u(7)
+        skip(6)
+        xnew(5)
         o(7)
         xnew(6)
         skip(7)

@@ -332,8 +332,7 @@ def tile_csdigatedsideinforesidual_w4_kernel(tc, y_bytes, y_scale, side, x, w_m_
         z(5)
         a(4)
         a(5)
-        uprod_gpsimd(4, "ug0")
-        uprod_gpsimd(5)
+        uprod(4)
         turn_u(2)
         turn_u(3)
         turn(7)
@@ -344,25 +343,27 @@ def tile_csdigatedsideinforesidual_w4_kernel(tc, y_bytes, y_scale, side, x, w_m_
         skip(1)
         gain(2)
         gain(3)
-        xnew(0)
+        uprod(5)
         quant(7)
         quant_u(2, 2)
         scale_x_gpsimd(4, "ug1")
+        xnew(0)
         xnew(1)
         z(6)
         a(6)
         turn_u(4)
         turn_u(5)
+        o(2)
+        skip(2)
         z(7)
         a(7)
         gain(4)
         gain(5)
         uprod(6)
-        o(2)
+        xnew(2)
         o(3)
         quant_u(4, 2)
-        xnew(2)
-        skip(2)
+        xnew(3)
         turn_u(6)
         uprod(7)
         skip(3)
@@ -371,18 +372,17 @@ def tile_csdigatedsideinforesidual_w4_kernel(tc, y_bytes, y_scale, side, x, w_m_
         gain(6)
         skip(4)
         turn_u(7)
-        xnew(3)
+        xnew(4)
         skip(5)
         quant_u(6)
         scale_x(6)
         gain(7)
         warm_up(1)
         o(6)
-        xnew(4)
+        xnew(5)
         quant_u(7)
         skip(6)
-        xnew(5)
-        o(7)
         xnew(6)
+        o(7)
         skip(7)
         xnew(7)

@@ -29,7 +29,7 @@ def tile_csdigatedsideinforesidual_w4_kernel(tc, y_bytes, y_scale, side, x, w_m_
     with ExitStack() as ctx:
         keep = ctx.enter_context(tc.tile_pool(name="keep", bufs=1))
         work = ctx.enter_context(tc.tile_pool(name="work", bufs=TILES))
-        psum = ctx.enter_context(tc.psum_pool(name="psum", bufs=8))
+        psum = ctx.enter_context(tc.psum_pool(name="psum", bufs=1))
         ctx.enter_context(tc.manual_schedule())
 
         y_v = y_bytes.rearrange("(p i) k -> p i k", i=TILES)
@@ -42,9 +42,6 @@ def tile_csdigatedsideinforesidual_w4_kernel(tc, y_bytes, y_scale, side, x, w_m_
         g_part = keep.tile([P, 4], BF16, name="g_part")
         ys_all = keep.tile([P, 2, D], F32, name="ys_all", align_bytes=64)
         ones = keep.tile([P, 1], F32, name="ones")
-        y_raw = [keep.tile([P, HALF, D], U8, name="y_raw%d" % h, align_bytes=64) for h in range(2)]
-        side_sb = [keep.tile([P, n, E], BF16, name="side_sb%d" % h, align_bytes=64) for h, n in enumerate((2, 2, HALF))]
-        x_sb = [keep.tile([P, HALF, D], BF16, name="x_sb%d" % h, align_bytes=64) for h in range(2)]
         ident = keep.tile([P, P], F32, name="ident")
         zeros = keep.tile([P, D], BF16, name="zeros", align_bytes=64)
         warm = keep.tile([P, 1], F32, name="warm")
@@ -55,117 +52,125 @@ def tile_csdigatedsideinforesidual_w4_kernel(tc, y_bytes, y_scale, side, x, w_m_
         ws_sc = keep.tile([P, 2 * D], U8, name="ws_sc", align_bytes=64)
         wo_sc = keep.tile([P, 2 * D], U8, name="wo_sc", align_bytes=64)
 
+        st = {}
+        free_banks = list(range(8))
+
+        def take_bank(key, shape, readers=1):
+            b = free_banks.pop(0)
+            st[key] = psum.tile([P] + shape, F32, tag="bank%d" % b, name="bank")
+            st["held", key] = [b, readers]
+            return st[key]
+
+        def give_bank(key):
+            held = st["held", key]
+            held[1] = held[1] - 1
+            if held[1] == 0:
+                free_banks.append(held[0])
+
         def load_scales(tile, dram):
             for q in range(4):
                 nc.sync.dma_start(out=tile[32 * q : 32 * q + 4, :].bitcast(I32), in_=dram[0, 4 * q : 4 * q + 4, :].bitcast(I32))
 
-        def load_rows(tile, view, lo, hi):
+        def load_rows(name, lo, hi):
+            view, dtype = {"y": (y_v, U8), "side": (side_v, BF16), "x": (x_v, BF16)}[name]
+            tile = keep.tile([P, hi - lo, D], dtype, name="%s_in%d" % (name, lo), align_bytes=64)
             nc.sync.dma_start(out=tile[:], in_=view[:, lo:hi, :])
+            for i in range(lo, hi):
+                st[name, i] = (tile, i - lo)
 
-        nc.vector.memset(ones[:], 1.0)
-        nc.scalar.activation(out=warm[:], in_=ones[:], func=ACT.Sigmoid)
-        nc.gpsimd.memset(zeros[:].bitcast(I32), 0)
-        make_identity(nc, ident[:])
-        nc.gpsimd.dma_start(out=side_sb[1][:], in_=side_v[:, 2:4, :])
-        for t in (wm_sc, ws_sc, wo_sc):
-            nc.vector.memset(t[:].bitcast(I32), 0)
+        def rows(name, i, n=1):
+            tile, j = st[name, i]
+            return tile[:, j : j + n, :]
 
-        nc.sync.dma_start(out=ys_part[:], in_=y_scale.rearrange("o (p t) -> p (o t)", t=4))
-        load_rows(y_raw[0], y_v, 0, 4)
-        load_rows(side_sb[0], side_v, 0, 2)
-        load_scales(wm_sc, w_m_scales)
-        load_scales(ws_sc, w_s_scales)
-        nc.sync.dma_start(out=wm[:], in_=w_m_words[0])
-        nc.sync.dma_start(out=ws[:], in_=w_s_words[0])
-        load_rows(y_raw[1], y_v, 4, 8)
-        load_rows(side_sb[2], side_v, 4, 8)
-        nc.sync.dma_start(out=g_part[:], in_=g.rearrange("(p t) -> p t", t=4))
-        load_scales(wo_sc, w_o_scales)
-        nc.sync.dma_start(out=wo[:], in_=w_o_words[0])
-        load_rows(x_sb[0], x_v, 0, 4)
-        load_rows(x_sb[1], x_v, 4, 8)
+        def load_words(tile, dram):
+            nc.sync.dma_start(out=tile[:], in_=dram[0])
+
+        def load_y_scale():
+            nc.sync.dma_start(out=ys_part[:], in_=y_scale.rearrange("o (p t) -> p (o t)", t=4))
+
+        def load_gain():
+            nc.sync.dma_start(out=g_part[:], in_=g.rearrange("(p t) -> p t", t=4))
 
         def warm_up(n):
-            bank = psum.tile([P, D], F32, tag="bank", name="warm_bank")
+            bank = take_bank("warm", [D])
             for k in range(n):
                 nc.tensor.matmul(bank[:], lhsT=zeros[:, 0:P], rhs=zeros[:], start=True, stop=True)
+            give_bank("warm")
 
-        st = {}
-
-        def spread_scales():
-            bank = psum.tile([P, 4, P], F32, tag="bank", name="ysb")
+        def spread_scales(copies):
+            bank = take_bank("spread", [4, P], copies)
             for t in range(4):
                 nc.tensor.transpose(bank[:, t, :], ys_part[:, t : t + 1].to_broadcast([P, P]), ident[:])
-            for j in range(2):
-                nc.scalar.copy(out=ys_all[:, j].rearrange("p (n t) -> p n t", t=4), in_=bank[:].rearrange("p t n -> p n t"))
+
+        def evac_scales(j):
+            nc.scalar.copy(out=ys_all[:, j].rearrange("p (n t) -> p n t", t=4), in_=st["spread"][:].rearrange("p t n -> p n t"))
+            give_bank("spread")
 
         def pair_tile(name, i, shape, dtype, reuse=None):
             if (name, i // 2) not in st:
                 st[name, i // 2] = work.tile([P, 2] + shape, dtype, tag=reuse or "%s%d" % (name, i // 2), name=name, bufs=1, align_bytes=64)
             return st[name, i // 2]
 
-        def rows(tiles, i, n):
-            return tiles[i // HALF][:, i % HALF : i % HALF + n, :]
-
         def widen(i):
-            yb = work.tile([P, 2, P, 2], BF16, tag="yw", name="yw", bufs=3, align_bytes=64)
+            yw = pair_tile("yw", i, [2, P, 2], BF16)
             nc.vector.tensor_scalar(
-                out=yb[:].rearrange("p u m e -> p m u e"),
-                in0=y_raw[0][:, i, :].bitcast(FP8).rearrange("p (m u e) -> p m u e", u=2, e=2),
+                out=yw[:, i % 2].rearrange("p u m e -> p m u e"),
+                in0=rows("y", i)[:, 0].bitcast(FP8).rearrange("p (m u e) -> p m u e", u=2, e=2),
                 scalar1=ones[:],
                 scalar2=None,
                 op0=MULT,
             )
-            st["yw", i] = yb
+
+        def widen_scalar(i, n=1):
+            yb = pair_tile("yb", i, [D], BF16)
+            nc.scalar.activation(out=yb[:, i % 2 : i % 2 + n], in_=rows("y", i, n).bitcast(FP8), func=ACT.Copy)
 
         def yprod(i, n=1):
             yb = pair_tile("yb", i, [D], BF16)
-            nc.vector.tensor_tensor(out=yb[:, i % 2 : i % 2 + n], in0=rows(y_raw, i, n).bitcast(FP8), in1=ys_all[:, 0:n], op=MULT)
+            nc.vector.tensor_tensor(out=yb[:, i % 2 : i % 2 + n], in0=rows("y", i, n).bitcast(FP8), in1=ys_all[:, 0:n], op=MULT)
 
-        def turn_y(i):
-            bank = psum.tile([P, 2, P], F32, tag="bank", name="ty")
-            words = st["yw", i][:].rearrange("p u m e -> p u (m e)").bitcast(F32)
-            for u in range(2):
-                nc.tensor.transpose(bank[:, u, :], words[:, u, :], ident[:])
-            st["ty", i] = bank
+        def words_of(kind, i, u):
+            if kind == "w":
+                return st["yw", i // 2][:, i % 2].rearrange("p u m e -> p u (m e)").bitcast(F32)[:, u, :]
+            src = st["yb", i // 2][:, i % 2, :] if kind == "y" else rows("side", i)[:, 0]
+            return src.bitcast(F32)[:, u : D // 2 : 2]
 
-        def turn_two(first, second):
-            bank = psum.tile([P, 2, 2, P], F32, tag="bank", name="tb")
-            for o, src in enumerate((first, second)):
+        def turn(key, operands, readers=1):
+            bank = take_bank(key, [len(operands), 2, P], readers)
+            for o, (kind, i) in enumerate(operands):
                 for u in range(2):
-                    nc.tensor.transpose(bank[:, o, u, :], src.bitcast(F32)[:, u : D // 2 : 2], ident[:])
-            return bank
-
-        def turn_sides():
-            st["ts"] = turn_two(side_sb[0][:, 0, :], side_sb[0][:, 1, :])
-
-        def turn_side(i):
-            bank = psum.tile([P, 2, P], F32, tag="bank", name="ts")
-            for u in range(2):
-                nc.tensor.transpose(bank[:, u, :], side_sb[1][:, i % 2, :].bitcast(F32)[:, u : D // 2 : 2], ident[:])
-            nc.scalar.copy(out=grp_words(i)[:, i % 2, 1], in_=bank[:].rearrange("p u r -> p r u"))
-
-        def turn(i):
-            st["tb", i] = turn_two(st["yb", i // 2][:, i % 2, :], side_sb[min(i // 2, 2)][:, i - 2 * min(i // 2, 2), :])
+                    nc.tensor.transpose(bank[:, o, u, :], words_of(kind, i, u), ident[:])
 
         def grp_words(i):
             grp = pair_tile("grp", i, [2, P, 4], BF16)
             return grp[:].rearrange("p j o r t -> p (j o r t)").bitcast(F32).rearrange("p (j o r u) -> p j o r u", j=2, o=2, u=2)
 
-        def evac_sides():
-            nc.scalar.copy(out=grp_words(0)[:, :, 1], in_=st["ts"][:].rearrange("p j u r -> p j r u"))
+        def turn_tile(i):
+            turn(("tile", i), [("y", i), ("side", i)])
 
-        def evac(i):
-            nc.scalar.copy(out=grp_words(i)[:, i % 2], in_=st["tb", i][:].rearrange("p o u r -> p o r u"))
+        def evac_tile(i):
+            nc.scalar.copy(out=grp_words(i)[:, i % 2], in_=st["tile", i][:].rearrange("p o u r -> p o r u"))
+            give_bank(("tile", i))
+
+        def turn_sides(i, n):
+            turn(("sides", i), [("side", i + j) for j in range(n)])
+
+        def evac_sides(i, n):
+            nc.scalar.copy(out=grp_words(i)[:, i % 2 : i % 2 + n, 1], in_=st["sides", i][:].rearrange("p j u r -> p j r u"))
+            give_bank(("sides", i))
+
+        def turn_y(i, kind):
+            turn(("ty", i), [(kind, i)])
 
         def evac_y(i):
-            yt = st["ty", i][:].rearrange("p u r -> p (u r)").bitcast(BF16)
+            yt = st["ty", i][:].rearrange("p o u r -> p (o u r)").bitcast(BF16)
             nc.vector.tensor_tensor(
                 out=pair_tile("grp", i, [2, P, 4], BF16)[:, i % 2, 0].rearrange("p r (u e) -> p r u e", e=2),
                 in0=yt.rearrange("p (u r e) -> p r u e", u=2, e=2),
                 in1=ys_part[:].rearrange("p (u e) -> p u e", e=2).unsqueeze(1).to_broadcast([P, P, 2, 2]),
                 op=MULT,
             )
+            give_bank(("ty", i))
 
         def quant(i, n=1):
             codes = pair_tile("codes", i, [2 * P], U32)[:, i % 2 : i % 2 + n].rearrange("p j c -> p (j c)")
@@ -177,7 +182,7 @@ def tile_csdigatedsideinforesidual_w4_kernel(tc, y_bytes, y_scale, side, x, w_m_
             codes, scales = st["codes", i // 2][:, i % 2], st["scales", i // 2][:, i % 2]
             w, sc = ((wm, wm_sc), (ws, ws_sc))[o]
             if o == 0:
-                st["z", h, i] = psum.tile([P, D], F32, tag="bank", name="zb")
+                take_bank(("z", h, i), [D])
             nc.tensor.matmul_mx(
                 out=st["z", h, i][:],
                 lhsT=codes[:, o * P : (o + 1) * P].bitcast(FP8X4),
@@ -188,7 +193,7 @@ def tile_csdigatedsideinforesidual_w4_kernel(tc, y_bytes, y_scale, side, x, w_m_
                 stop=(o == 1),
             )
 
-        def mm_z(i, h):
+        def z_half(i, h):
             z_pass(i, h, 0)
             z_pass(i, h, 1)
 
@@ -201,21 +206,17 @@ def tile_csdigatedsideinforesidual_w4_kernel(tc, y_bytes, y_scale, side, x, w_m_
             name, func = (("sg", ACT.Sigmoid), ("th", ACT.Tanh))[h]
             r = pair_tile(name, i, [4, P], F32)
             nc.scalar.activation(out=r[:, i % 2], in_=st["z", h, i][:].rearrange("p (m t) -> p t m", t=4), func=func)
+            give_bank(("z", h, i))
 
         def uprod(i, n=1):
             u = pair_tile("u", i, [4, P], F32)
             both_tiles = slice(i % 2, i % 2 + n)
             nc.vector.tensor_tensor(out=u[:, both_tiles], in0=st["sg", i // 2][:, both_tiles], in1=st["th", i // 2][:, both_tiles], op=MULT)
 
-        def uprod_gpsimd(i, reuse=None):
-            u = pair_tile("u", i, [4, P], F32, reuse)
-            nc.gpsimd.tensor_tensor(out=u[:, i % 2], in0=st["sg", i // 2][:, i % 2], in1=st["th", i // 2][:, i % 2], op=MULT)
-
         def turn_u(i):
-            bank = psum.tile([P, 4, P], F32, tag="bank", name="ut")
+            bank = take_bank(("ut", i), [4, P])
             for t in range(4):
                 nc.tensor.transpose(bank[:, t, :], st["u", i // 2][:, i % 2, t, :], ident[:])
-            st["ut", i] = bank
 
         def gain(i):
             nc.vector.tensor_tensor(
@@ -224,6 +225,7 @@ def tile_csdigatedsideinforesidual_w4_kernel(tc, y_bytes, y_scale, side, x, w_m_
                 in1=g_part[:].unsqueeze(1).to_broadcast([P, P, 4]),
                 op=MULT,
             )
+            give_bank(("ut", i))
 
         def quant_u(i, n=1):
             codes = pair_tile("ucodes", i, [P], U32)[:, i % 2 : i % 2 + n].rearrange("p j c -> p (j c)")
@@ -231,8 +233,8 @@ def tile_csdigatedsideinforesidual_w4_kernel(tc, y_bytes, y_scale, side, x, w_m_
             ug = st["ug", i // 2][:, i % 2 : i % 2 + n].rearrange("p j r t -> p (j r t)")
             nc.vector.quantize_mx(out=codes.bitcast(FP8X4), scales=scales, in_=ug)
 
-        def mm_o(i, h):
-            bank = psum.tile([P, D], F32, tag="bank", name="ob")
+        def o_half(i, h):
+            bank = take_bank(("o", h, i), [D])
             nc.tensor.matmul_mx(
                 out=bank[:],
                 lhsT=st["ucodes", i // 2][:, i % 2].bitcast(FP8X4),
@@ -242,58 +244,73 @@ def tile_csdigatedsideinforesidual_w4_kernel(tc, y_bytes, y_scale, side, x, w_m_
                 start=True,
                 stop=True,
             )
-            st["o", h, i] = bank
 
-        def scale_x(i, n=2):
-            nc.scalar.activation(out=pair_tile("xs", i, [D], F32)[:, i % 2 : i % 2 + n], in_=rows(x_sb, i, n), func=ACT.Copy, scale=RSQRT2)
+        def scale_x_scalar(i, n=2):
+            nc.scalar.activation(out=pair_tile("xs", i, [D], F32)[:, i % 2 : i % 2 + n], in_=rows("x", i, n), func=ACT.Copy, scale=RSQRT2)
 
         def scale_x_vector(i, n=2):
-            nc.vector.tensor_scalar(out=pair_tile("xs", i, [D], F32)[:, i % 2 : i % 2 + n], in0=rows(x_sb, i, n), scalar1=RSQRT2, scalar2=None, op0=MULT)
+            nc.vector.tensor_scalar(out=pair_tile("xs", i, [D], F32)[:, i % 2 : i % 2 + n], in0=rows("x", i, n), scalar1=RSQRT2, scalar2=None, op0=MULT)
 
-        def scale_x_gpsimd(i, reuse):
-            nc.gpsimd.tensor_scalar(out=pair_tile("xs", i, [D], F32, reuse)[:], in0=rows(x_sb, i, 2), scalar1=RSQRT2, scalar2=0.0, op0=MULT, op1=ADD)
+        def scale_x_gpsimd(i, reuse=None):
+            nc.gpsimd.tensor_scalar(out=pair_tile("xs", i, [D], F32, reuse)[:], in0=rows("x", i, 2), scalar1=RSQRT2, scalar2=0.0, op0=MULT, op1=ADD)
 
         def skip(i):
             r = work.tile([P, D], F32, tag="sk", name="sk", align_bytes=64)
             nc.scalar.copy(out=r[:], in_=st["o", 1, i][:])
+            give_bank(("o", 1, i))
             nc.sync.dma_start(out=skip_v[:, i, :], in_=r[:])
 
         def xnew(i):
             r = work.tile([P, D], F32, tag="xn", name="xn", align_bytes=64)
             nc.vector.scalar_tensor_tensor(out=r[:], in0=st["o", 0, i][:], scalar=RSQRT2, in1=st["xs", i // 2][:, i % 2], op0=MULT, op1=ADD)
+            give_bank(("o", 0, i))
             nc.sync.dma_start(out=xnew_v[:, i, :], in_=r[:])
 
-        def both(stage, i):
-            stage(i, 0)
-            stage(i, 1)
+        def zero(tile):
+            nc.vector.memset(tile[:].bitcast(I32), 0)
 
-        def z(i):
-            both(mm_z, i)
-
-        def a(i):
-            both(act, i)
-
-        def o(i):
-            mm_o(i, 1)
-            mm_o(i, 0)
-
+        nc.vector.memset(ones[:], 1.0)
+        nc.scalar.activation(out=warm[:], in_=ones[:], func=ACT.Sigmoid)
+        nc.gpsimd.memset(zeros[:].bitcast(I32), 0)
+        make_identity(nc, ident[:])
+        zero(wm_sc)
+        zero(ws_sc)
+        zero(wo_sc)
+        load_y_scale()
+        load_rows("y", 0, 4)
+        load_rows("side", 0, 2)
+        load_rows("side", 2, 4)
+        load_scales(wm_sc, w_m_scales)
+        load_words(wm, w_m_words)
+        load_scales(ws_sc, w_s_scales)
+        load_words(ws, w_s_words)
+        load_rows("y", 4, 8)
+        load_rows("side", 4, 8)
+        load_gain()
+        load_scales(wo_sc, w_o_scales)
+        load_words(wo, w_o_words)
+        load_rows("x", 0, 4)
+        load_rows("x", 4, 8)
         warm_up(2)
-        spread_scales()
+        spread_scales(2)
+        evac_scales(0)
+        evac_scales(1)
         warm_up(2)
         widen(0)
         widen(1)
         widen(2)
-        turn_y(0)
-        turn_sides()
-        turn_y(1)
-        evac_sides()
+        turn_y(0, "w")
+        turn_sides(0, 2)
+        turn_y(1, "w")
+        evac_sides(0, 2)
         evac_y(0)
         yprod(3)
         warm_up(2)
-        turn_y(2)
-        turn_side(2)
-        turn(3)
-        evac(3)
+        turn_y(2, "w")
+        turn_sides(2, 1)
+        evac_sides(2, 1)
+        turn_tile(3)
+        evac_tile(3)
         warm_up(1)
         evac_y(1)
         quant(0)
@@ -301,44 +318,57 @@ def tile_csdigatedsideinforesidual_w4_kernel(tc, y_bytes, y_scale, side, x, w_m_
         quant(1)
         yprod(4, 2)
         z_by_operand(0)
-        z(1)
-        a(0)
-        a(1)
+        z_half(1, 0)
+        z_half(1, 1)
+        act(0, 0)
+        act(0, 1)
+        act(1, 0)
+        act(1, 1)
         quant(2, 2)
         uprod(0)
         yprod(6, 2)
         uprod(1)
-        turn(4)
-        turn(5)
-        evac(4)
-        evac(5)
+        turn_tile(4)
+        turn_tile(5)
+        evac_tile(4)
+        evac_tile(5)
         quant(4, 2)
-        z(2)
-        z(3)
-        a(2)
-        a(3)
+        z_half(2, 0)
+        z_half(2, 1)
+        z_half(3, 0)
+        z_half(3, 1)
+        act(2, 0)
+        act(2, 1)
+        act(3, 0)
+        act(3, 1)
         scale_x_gpsimd(0, "grp2")
         scale_x_vector(2)
         turn_u(0)
         turn_u(1)
-        turn(6)
-        evac(6)
+        turn_tile(6)
+        evac_tile(6)
         gain(0)
         gain(1)
         uprod(2, 2)
         quant(6)
         quant_u(0, 2)
-        z(4)
-        z(5)
-        a(4)
-        a(5)
+        z_half(4, 0)
+        z_half(4, 1)
+        z_half(5, 0)
+        z_half(5, 1)
+        act(4, 0)
+        act(4, 1)
+        act(5, 0)
+        act(5, 1)
         uprod(4)
         turn_u(2)
         turn_u(3)
-        turn(7)
-        evac(7)
-        o(0)
-        o(1)
+        turn_tile(7)
+        evac_tile(7)
+        o_half(0, 1)
+        o_half(0, 0)
+        o_half(1, 1)
+        o_half(1, 0)
         skip(0)
         skip(1)
         gain(2)
@@ -349,40 +379,50 @@ def tile_csdigatedsideinforesidual_w4_kernel(tc, y_bytes, y_scale, side, x, w_m_
         scale_x_gpsimd(4, "ug1")
         xnew(0)
         xnew(1)
-        z(6)
-        a(6)
+        z_half(6, 0)
+        z_half(6, 1)
+        act(6, 0)
+        act(6, 1)
         turn_u(4)
         turn_u(5)
-        o(2)
+        o_half(2, 1)
+        o_half(2, 0)
         skip(2)
-        z(7)
-        a(7)
+        z_half(7, 0)
+        z_half(7, 1)
+        act(7, 0)
+        act(7, 1)
         gain(4)
         gain(5)
         uprod(6)
         xnew(2)
-        o(3)
+        o_half(3, 1)
+        o_half(3, 0)
         quant_u(4, 2)
         xnew(3)
         turn_u(6)
         uprod(7)
         skip(3)
-        o(4)
-        o(5)
+        o_half(4, 1)
+        o_half(4, 0)
+        o_half(5, 1)
+        o_half(5, 0)
         gain(6)
         skip(4)
         turn_u(7)
         xnew(4)
         skip(5)
         quant_u(6)
-        scale_x(6)
+        scale_x_scalar(6, 2)
         gain(7)
         warm_up(1)
-        o(6)
+        o_half(6, 1)
+        o_half(6, 0)
         xnew(5)
         quant_u(7)
         skip(6)
         xnew(6)
-        o(7)
+        o_half(7, 1)
+        o_half(7, 0)
         skip(7)
         xnew(7)

@@ -22,6 +22,7 @@ P = 128
 TILES = N // P
 HALF = TILES // 2
 RSQRT2 = 0.5 ** 0.5
+BY_OPERAND = ()
 
 
 def tile_csdigatedsideinforesidual_w4_kernel(tc, y_bytes, y_scale, side, x, w_m_words, w_m_scales, w_s_words, w_s_scales, g, w_o_words, w_o_scales, out_0, out_1):
@@ -125,6 +126,18 @@ def tile_csdigatedsideinforesidual_w4_kernel(tc, y_bytes, y_scale, side, x, w_m_
             yb = pair_tile("yb", i, [D], BF16)
             nc.scalar.activation(out=yb[:, i % 2 : i % 2 + n], in_=rows("y", i, n).bitcast(FP8), func=ACT.Copy)
 
+        def widen_plain(i, n=1):
+            yb = pair_tile("yb", i, [D], BF16)
+            nc.vector.tensor_copy(out=yb[:, i % 2 : i % 2 + n], in_=rows("y", i, n).bitcast(FP8))
+
+        def widen_gpsimd(i, n=1):
+            yb = pair_tile("yb", i, [D], BF16)
+            nc.gpsimd.tensor_copy(out=yb[:, i % 2 : i % 2 + n], in_=rows("y", i, n).bitcast(FP8))
+
+        def scale_y(i, n=1):
+            turned = grp_slots(i)[:, slot(i, 0) : slot(i + n - 1, 0) + 1 : max(1, slot(1, 0) if i // 2 in BY_OPERAND else 2)]
+            nc.vector.tensor_tensor(out=turned, in0=turned, in1=ys_part[:].unsqueeze(1).unsqueeze(1).to_broadcast([P, n, P, 4]), op=MULT)
+
         def yprod(i, n=1):
             yb = pair_tile("yb", i, [D], BF16)
             nc.vector.tensor_tensor(out=yb[:, i % 2 : i % 2 + n], in0=rows("y", i, n).bitcast(FP8), in1=ys_all[:, 0:n], op=MULT)
@@ -143,10 +156,32 @@ def tile_csdigatedsideinforesidual_w4_kernel(tc, y_bytes, y_scale, side, x, w_m_
 
         def grp_words(i):
             grp = pair_tile("grp", i, [2, P, 4], BF16)
-            return grp[:].rearrange("p j o r t -> p (j o r t)").bitcast(F32).rearrange("p (j o r u) -> p j o r u", j=2, o=2, u=2)
+            pattern = "p (o j r u) -> p j o r u" if i // 2 in BY_OPERAND else "p (j o r u) -> p j o r u"
+            return grp[:].rearrange("p a b r t -> p (a b r t)").bitcast(F32).rearrange(pattern, j=2, o=2, u=2)
 
-        def turn_tile(i):
-            turn(("tile", i), [("y", i), ("side", i)])
+        def slot(i, o):
+            return 2 * o + i % 2 if i // 2 in BY_OPERAND else 2 * (i % 2) + o
+
+        def grp_slots(i):
+            return pair_tile("grp", i, [2, P, 4], BF16)[:].rearrange("p a b r t -> p (a b) r t")
+
+        def turn_ys(i, n):
+            turn(("ys", i), [("y", i + j) for j in range(n)])
+
+        def evac_ys(i, n):
+            nc.scalar.copy(out=grp_words(i)[:, i % 2 : i % 2 + n, 0], in_=st["ys", i][:].rearrange("p j u r -> p j r u"))
+            give_bank(("ys", i))
+
+        def quant_slots(i, first, n):
+            codes = pair_tile("codes", i, [2 * P], U32)[:].rearrange("p a c -> p (a c)")[:, first * P : (first + n) * P]
+            scales = pair_tile("scales", i, [2 * P], U8)[:].rearrange("p a c -> p (a c)")[:, first * P : (first + n) * P]
+            nc.vector.quantize_mx(out=codes.bitcast(FP8X4), scales=scales, in_=grp_slots(i)[:, first : first + n].rearrange("p a r t -> p (a r t)"))
+
+        def quant_operand(i, o, n=1):
+            quant_slots(i, slot(i, o), n)
+
+        def turn_tile(i, kind="y"):
+            turn(("tile", i), [(kind, i), ("side", i)])
 
         def evac_tile(i):
             nc.scalar.copy(out=grp_words(i)[:, i % 2], in_=st["tile", i][:].rearrange("p o u r -> p o r u"))
@@ -165,7 +200,7 @@ def tile_csdigatedsideinforesidual_w4_kernel(tc, y_bytes, y_scale, side, x, w_m_
         def evac_y(i):
             yt = st["ty", i][:].rearrange("p o u r -> p (o u r)").bitcast(BF16)
             nc.vector.tensor_tensor(
-                out=pair_tile("grp", i, [2, P, 4], BF16)[:, i % 2, 0].rearrange("p r (u e) -> p r u e", e=2),
+                out=grp_slots(i)[:, slot(i, 0)].rearrange("p r (u e) -> p r u e", e=2),
                 in0=yt.rearrange("p (u r e) -> p r u e", u=2, e=2),
                 in1=ys_part[:].rearrange("p (u e) -> p u e", e=2).unsqueeze(1).to_broadcast([P, P, 2, 2]),
                 op=MULT,
@@ -173,24 +208,22 @@ def tile_csdigatedsideinforesidual_w4_kernel(tc, y_bytes, y_scale, side, x, w_m_
             give_bank(("ty", i))
 
         def quant(i, n=1):
-            codes = pair_tile("codes", i, [2 * P], U32)[:, i % 2 : i % 2 + n].rearrange("p j c -> p (j c)")
-            scales = pair_tile("scales", i, [2 * P], U8)[:, i % 2 : i % 2 + n].rearrange("p j c -> p (j c)")
-            grp = st["grp", i // 2][:, i % 2 : i % 2 + n].rearrange("p j o r t -> p (j o r t)")
-            nc.vector.quantize_mx(out=codes.bitcast(FP8X4), scales=scales, in_=grp)
+            quant_slots(i, 2 * (i % 2), 2 * n)
 
         def z_pass(i, h, o):
-            codes, scales = st["codes", i // 2][:, i % 2], st["scales", i // 2][:, i % 2]
+            codes, scales = [st[name, i // 2][:].rearrange("p a c -> p (a c)")[:, slot(i, o) * P : (slot(i, o) + 1) * P] for name in ("codes", "scales")]
             w, sc = ((wm, wm_sc), (ws, ws_sc))[o]
-            if o == 0:
+            first = ("z", h, i) not in st
+            if first:
                 take_bank(("z", h, i), [D])
             nc.tensor.matmul_mx(
                 out=st["z", h, i][:],
-                lhsT=codes[:, o * P : (o + 1) * P].bitcast(FP8X4),
-                lhsT_scale=scales[:, o * P : (o + 1) * P],
+                lhsT=codes.bitcast(FP8X4),
+                lhsT_scale=scales,
                 rhs=w[:, 2 * D * h : 2 * D * (h + 1)].bitcast(FP4X4),
                 rhs_scale=sc[:, D * h : D * (h + 1)],
-                start=(o == 0),
-                stop=(o == 1),
+                start=first,
+                stop=not first,
             )
 
         def z_half(i, h):
@@ -245,6 +278,51 @@ def tile_csdigatedsideinforesidual_w4_kernel(tc, y_bytes, y_scale, side, x, w_m_
                 stop=True,
             )
 
+        def o_part(i, h, c):
+            bank = take_bank(("o", h, i, c), [D // 2])
+            lo = D * h + D // 2 * c
+            nc.tensor.matmul_mx(
+                out=bank[:],
+                lhsT=st["ucodes", i // 2][:, i % 2].bitcast(FP8X4),
+                lhsT_scale=st["uscales", i // 2][:, i % 2],
+                rhs=wo[:, 2 * lo : 2 * lo + D].bitcast(FP4X4),
+                rhs_scale=wo_sc[:, lo : lo + D // 2],
+                start=True,
+                stop=True,
+            )
+
+        def skip_part(i, c):
+            cols = slice(D // 2 * c, D // 2 * (c + 1))
+            r = work.tile([P, D // 2], F32, tag="skp", name="skp", bufs=4, align_bytes=64)
+            nc.scalar.copy(out=r[:], in_=st["o", 1, i, c][:])
+            give_bank(("o", 1, i, c))
+            nc.sync.dma_start(out=skip_v[:, i, cols], in_=r[:])
+
+        def xnew_part(i, c):
+            cols = slice(D // 2 * c, D // 2 * (c + 1))
+            r = work.tile([P, D // 2], F32, tag="xnp", name="xnp", bufs=4, align_bytes=64)
+            nc.vector.scalar_tensor_tensor(out=r[:], in0=st["o", 0, i, c][:], scalar=RSQRT2, in1=st["xs", i // 2][:, i % 2, cols], op0=MULT, op1=ADD)
+            give_bank(("o", 0, i, c))
+            nc.sync.dma_start(out=xnew_v[:, i, cols], in_=r[:])
+
+        def act_part(i, h, c):
+            name, func = (("sg", ACT.Sigmoid), ("th", ACT.Tanh))[h]
+            r = pair_tile(name, i, [4, P], F32)
+            nc.scalar.activation(out=r[:, i % 2, 2 * c : 2 * c + 2], in_=st["z", h, i][:].rearrange("p (m t) -> p t m", t=4)[:, 2 * c : 2 * c + 2], func=func)
+            if c == 1:
+                give_bank(("z", h, i))
+
+        def uprod_part(i, c):
+            u = pair_tile("u", i, [4, P], F32)
+            planes = slice(2 * c, 2 * c + 2)
+            nc.vector.tensor_tensor(out=u[:, i % 2, planes], in0=st["sg", i // 2][:, i % 2, planes], in1=st["th", i // 2][:, i % 2, planes], op=MULT)
+
+        def turn_u_part(i, c):
+            if c == 0:
+                take_bank(("ut", i), [4, P])
+            for t in range(2 * c, 2 * c + 2):
+                nc.tensor.transpose(st["ut", i][:, t, :], st["u", i // 2][:, i % 2, t, :], ident[:])
+
         def scale_x_scalar(i, n=2):
             nc.scalar.activation(out=pair_tile("xs", i, [D], F32)[:, i % 2 : i % 2 + n], in_=rows("x", i, n), func=ACT.Copy, scale=RSQRT2)
 
@@ -298,23 +376,20 @@ def tile_csdigatedsideinforesidual_w4_kernel(tc, y_bytes, y_scale, side, x, w_m_
         warm_up(2)
         widen(0)
         widen(1)
-        widen(2)
         turn_y(0, "w")
         turn_sides(0, 2)
         turn_y(1, "w")
         evac_sides(0, 2)
+        yprod(2)
         evac_y(0)
         yprod(3)
-        warm_up(2)
-        turn_y(2, "w")
-        turn_sides(2, 1)
-        evac_sides(2, 1)
+        warm_up(3)
+        turn_tile(2)
         turn_tile(3)
+        evac_tile(2)
         evac_tile(3)
-        warm_up(1)
-        evac_y(1)
         quant(0)
-        evac_y(2)
+        evac_y(1)
         quant(1)
         yprod(4, 2)
         z_by_operand(0)
@@ -325,9 +400,10 @@ def tile_csdigatedsideinforesidual_w4_kernel(tc, y_bytes, y_scale, side, x, w_m_
         act(1, 0)
         act(1, 1)
         quant(2, 2)
-        uprod(0)
         yprod(6, 2)
+        uprod(0)
         uprod(1)
+        scale_x_vector(0)
         turn_tile(4)
         turn_tile(5)
         evac_tile(4)
@@ -341,8 +417,6 @@ def tile_csdigatedsideinforesidual_w4_kernel(tc, y_bytes, y_scale, side, x, w_m_
         act(2, 1)
         act(3, 0)
         act(3, 1)
-        scale_x_gpsimd(0, "grp2")
-        scale_x_vector(2)
         turn_u(0)
         turn_u(1)
         turn_tile(6)
@@ -350,8 +424,8 @@ def tile_csdigatedsideinforesidual_w4_kernel(tc, y_bytes, y_scale, side, x, w_m_
         gain(0)
         gain(1)
         uprod(2, 2)
-        quant(6)
         quant_u(0, 2)
+        quant(6)
         z_half(4, 0)
         z_half(4, 1)
         z_half(5, 0)
@@ -365,64 +439,71 @@ def tile_csdigatedsideinforesidual_w4_kernel(tc, y_bytes, y_scale, side, x, w_m_
         turn_u(3)
         turn_tile(7)
         evac_tile(7)
-        o_half(0, 1)
-        o_half(0, 0)
-        o_half(1, 1)
-        o_half(1, 0)
-        skip(0)
-        skip(1)
         gain(2)
         gain(3)
         uprod(5)
-        quant(7)
         quant_u(2, 2)
-        scale_x_gpsimd(4, "ug1")
-        xnew(0)
-        xnew(1)
+        quant(7)
+        scale_x_gpsimd(2, "grp3")
         z_half(6, 0)
-        z_half(6, 1)
+        o_half(0, 1)
+        o_half(0, 0)
+        o_half(1, 1)
+        skip(0)
+        skip(1)
         act(6, 0)
-        act(6, 1)
+        xnew(0)
         turn_u(4)
         turn_u(5)
-        o_half(2, 1)
-        o_half(2, 0)
-        skip(2)
-        z_half(7, 0)
-        z_half(7, 1)
-        act(7, 0)
-        act(7, 1)
         gain(4)
         gain(5)
-        uprod(6)
-        xnew(2)
+        z_half(6, 1)
+        o_half(1, 0)
+        o_half(2, 1)
+        o_half(2, 0)
         o_half(3, 1)
         o_half(3, 0)
+        z_half(7, 0)
+        z_half(7, 1)
+        act(6, 1)
+        skip(2)
+        skip(3)
+        xnew(1)
+        uprod(6)
         quant_u(4, 2)
+        scale_x_gpsimd(4, "ug2")
+        xnew(2)
         xnew(3)
         turn_u(6)
-        uprod(7)
-        skip(3)
+        gain(6)
+        act(7, 0)
+        act_part(7, 1, 0)
+        act_part(7, 1, 1)
         o_half(4, 1)
         o_half(4, 0)
         o_half(5, 1)
         o_half(5, 0)
-        gain(6)
         skip(4)
-        turn_u(7)
-        xnew(4)
         skip(5)
-        quant_u(6)
         scale_x_scalar(6, 2)
-        gain(7)
-        warm_up(1)
+        uprod_part(7, 0)
+        uprod_part(7, 1)
+        quant_u(6)
+        turn_u_part(7, 0)
+        turn_u_part(7, 1)
+        xnew(4)
         o_half(6, 1)
         o_half(6, 0)
+        skip(6)
+        gain(7)
         xnew(5)
         quant_u(7)
-        skip(6)
         xnew(6)
-        o_half(7, 1)
-        o_half(7, 0)
-        skip(7)
-        xnew(7)
+        o_part(7, 0, 0)
+        o_part(7, 1, 0)
+        o_part(7, 0, 1)
+        o_part(7, 1, 1)
+        xnew_part(7, 0)
+        skip_part(7, 0)
+        xnew_part(7, 1)
+        skip_part(7, 1)

@@ -68,14 +68,14 @@ def tile_csdigatedsideinforesidual_w4_kernel(tc, y_bytes, y_scale, side, x, w_m_
             if held[1] == 0:
                 free_banks.append(held[0])
 
-        def load_scales(tile, dram):
+        def load_scales(tile, dram, queue=nc.sync):
             for q in range(4):
-                nc.sync.dma_start(out=tile[32 * q : 32 * q + 4, :].bitcast(I32), in_=dram[0, 4 * q : 4 * q + 4, :].bitcast(I32))
+                queue.dma_start(out=tile[32 * q : 32 * q + 4, :].bitcast(I32), in_=dram[0, 4 * q : 4 * q + 4, :].bitcast(I32))
 
-        def load_rows(name, lo, hi):
+        def load_rows(name, lo, hi, queue=nc.sync):
             view, dtype = {"y": (y_v, U8), "side": (side_v, BF16), "x": (x_v, BF16)}[name]
             tile = keep.tile([P, hi - lo, D], dtype, name="%s_in%d" % (name, lo), align_bytes=64)
-            nc.sync.dma_start(out=tile[:], in_=view[:, lo:hi, :])
+            queue.dma_start(out=tile[:], in_=view[:, lo:hi, :])
             for i in range(lo, hi):
                 st[name, i] = (tile, i - lo)
 
@@ -85,6 +85,13 @@ def tile_csdigatedsideinforesidual_w4_kernel(tc, y_bytes, y_scale, side, x, w_m_
 
         def load_words(tile, dram):
             nc.sync.dma_start(out=tile[:], in_=dram[0])
+
+        def load_words_gpsimd(tile, dram):
+            nc.gpsimd.dma_start(out=tile[:].bitcast(I32), in_=dram[0].bitcast(I32))
+
+        def load_scale_rows(tile, dram):
+            for r in range(4):
+                nc.sync.dma_start(out=tile[r:P:32, :].bitcast(I32), in_=dram[0, r:16:4, :].bitcast(I32))
 
         def load_y_scale():
             nc.sync.dma_start(out=ys_part[:], in_=y_scale.rearrange("o (p t) -> p (o t)", t=4))
@@ -102,6 +109,16 @@ def tile_csdigatedsideinforesidual_w4_kernel(tc, y_bytes, y_scale, side, x, w_m_
             bank = take_bank("spread", [4, P], copies)
             for t in range(4):
                 nc.tensor.transpose(bank[:, t, :], ys_part[:, t : t + 1].to_broadcast([P, P]), ident[:])
+
+        def spread_scales_plain(readers):
+            bank = take_bank("plain", [P, 4], readers)
+            for t in range(4):
+                nc.tensor.transpose(bank[:, :, t], ys_part[:, t : t + 1].to_broadcast([P, P]), ident[:])
+
+        def scale_wide(i):
+            wide = st["wide", i // 2][:, i % 2]
+            nc.vector.tensor_tensor(out=pair_tile("yb", i, [D], BF16)[:, i % 2], in0=wide, in1=st["plain"][:].rearrange("p n t -> p (n t)"), op=MULT)
+            give_bank("plain")
 
         def evac_scales(j):
             nc.scalar.copy(out=ys_all[:, j].rearrange("p (n t) -> p n t", t=4), in_=st["spread"][:].rearrange("p t n -> p n t"))
@@ -127,7 +144,7 @@ def tile_csdigatedsideinforesidual_w4_kernel(tc, y_bytes, y_scale, side, x, w_m_
             nc.scalar.activation(out=yb[:, i % 2 : i % 2 + n], in_=rows("y", i, n).bitcast(FP8), func=ACT.Copy)
 
         def widen_plain(i, n=1):
-            yb = pair_tile("yb", i, [D], BF16)
+            yb = pair_tile("wide", i, [D], BF16)
             nc.vector.tensor_copy(out=yb[:, i % 2 : i % 2 + n], in_=rows("y", i, n).bitcast(FP8))
 
         def widen_gpsimd(i, n=1):
@@ -344,6 +361,20 @@ def tile_csdigatedsideinforesidual_w4_kernel(tc, y_bytes, y_scale, side, x, w_m_
             give_bank(("o", 0, i))
             nc.sync.dma_start(out=xnew_v[:, i, :], in_=r[:])
 
+        def skip_pair(i):
+            r = pair_tile("sk", i, [D], F32)
+            nc.scalar.copy(out=r[:, i % 2], in_=st["o", 1, i][:])
+            give_bank(("o", 1, i))
+            if i % 2:
+                nc.sync.dma_start(out=skip_v[:, i - 1 : i + 1, :], in_=r[:])
+
+        def xnew_pair(i):
+            r = pair_tile("xn", i, [D], F32)
+            nc.vector.scalar_tensor_tensor(out=r[:, i % 2], in0=st["o", 0, i][:], scalar=RSQRT2, in1=st["xs", i // 2][:, i % 2], op0=MULT, op1=ADD)
+            give_bank(("o", 0, i))
+            if i % 2:
+                nc.sync.dma_start(out=xnew_v[:, i - 1 : i + 1, :], in_=r[:])
+
         def zero(tile):
             nc.vector.memset(tile[:].bitcast(I32), 0)
 
@@ -499,11 +530,7 @@ def tile_csdigatedsideinforesidual_w4_kernel(tc, y_bytes, y_scale, side, x, w_m_
         xnew(5)
         quant_u(7)
         xnew(6)
-        o_part(7, 0, 0)
-        o_part(7, 1, 0)
-        o_part(7, 0, 1)
-        o_part(7, 1, 1)
-        xnew_part(7, 0)
-        skip_part(7, 0)
-        xnew_part(7, 1)
-        skip_part(7, 1)
+        o_half(7, 0)
+        o_half(7, 1)
+        xnew(7)
+        skip(7)

@@ -20,7 +20,6 @@ ACT = mybir.ActivationFunctionType
 
 P = 128
 TILES = N // P
-HALF = TILES // 2
 RSQRT2 = 0.5 ** 0.5
 BY_OPERAND = ()
 
@@ -41,7 +40,6 @@ def tile_csdigatedsideinforesidual_w4_kernel(tc, y_bytes, y_scale, side, x, w_m_
 
         ys_part = keep.tile([P, 4], F32, name="ys_part")
         g_part = keep.tile([P, 4], BF16, name="g_part")
-        ys_all = keep.tile([P, 2, D], F32, name="ys_all", align_bytes=64)
         ones = keep.tile([P, 1], F32, name="ones")
         ident = keep.tile([P, P], F32, name="ident")
         zeros = keep.tile([P, D], BF16, name="zeros", align_bytes=64)
@@ -51,6 +49,7 @@ def tile_csdigatedsideinforesidual_w4_kernel(tc, y_bytes, y_scale, side, x, w_m_
         wo = keep.tile([P, 4 * D], U8, name="wo", align_bytes=64)
         wm_sc = keep.tile([P, 2 * D], U8, name="wm_sc", align_bytes=64)
         ws_sc = keep.tile([P, 2 * D], U8, name="ws_sc", align_bytes=64)
+        ys_sorted = keep.tile([P, 2, P, 2], F32, name="ys_sorted", align_bytes=64)
         wo_sc = keep.tile([P, 2 * D], U8, name="wo_sc", align_bytes=64)
 
         st = {}
@@ -86,12 +85,18 @@ def tile_csdigatedsideinforesidual_w4_kernel(tc, y_bytes, y_scale, side, x, w_m_
         def load_words(tile, dram):
             nc.sync.dma_start(out=tile[:], in_=dram[0])
 
-        def load_words_gpsimd(tile, dram):
-            nc.gpsimd.dma_start(out=tile[:].bitcast(I32), in_=dram[0].bitcast(I32))
+        def spread_sorted(copies):
+            bank = take_bank("spread", [2, P, 2], copies)
+            for t in range(4):
+                nc.tensor.transpose(bank[:, t // 2, :, t % 2], ys_part[:, t : t + 1].to_broadcast([P, P]), ident[:])
 
-        def load_scale_rows(tile, dram):
-            for r in range(4):
-                nc.sync.dma_start(out=tile[r:P:32, :].bitcast(I32), in_=dram[0, r:16:4, :].bitcast(I32))
+        def keep_scales():
+            nc.scalar.copy(out=ys_sorted[:], in_=st["spread"][:])
+            give_bank("spread")
+
+        def yprod(i):
+            yb = pair_tile("yb", i, [2, P, 2], BF16)
+            nc.vector.tensor_tensor(out=yb[:, i % 2], in0=rows("y", i)[:, 0].bitcast(FP8).rearrange("p (m u e) -> p u m e", u=2, e=2), in1=ys_sorted[:], op=MULT)
 
         def load_y_scale():
             nc.sync.dma_start(out=ys_part[:], in_=y_scale.rearrange("o (p t) -> p (o t)", t=4))
@@ -105,63 +110,16 @@ def tile_csdigatedsideinforesidual_w4_kernel(tc, y_bytes, y_scale, side, x, w_m_
                 nc.tensor.matmul(bank[:], lhsT=zeros[:, 0:P], rhs=zeros[:], start=True, stop=True)
             give_bank("warm")
 
-        def spread_scales(copies):
-            bank = take_bank("spread", [4, P], copies)
-            for t in range(4):
-                nc.tensor.transpose(bank[:, t, :], ys_part[:, t : t + 1].to_broadcast([P, P]), ident[:])
-
-        def spread_scales_plain(readers):
-            bank = take_bank("plain", [P, 4], readers)
-            for t in range(4):
-                nc.tensor.transpose(bank[:, :, t], ys_part[:, t : t + 1].to_broadcast([P, P]), ident[:])
-
-        def scale_wide(i):
-            wide = st["wide", i // 2][:, i % 2]
-            nc.vector.tensor_tensor(out=pair_tile("yb", i, [D], BF16)[:, i % 2], in0=wide, in1=st["plain"][:].rearrange("p n t -> p (n t)"), op=MULT)
-            give_bank("plain")
-
-        def evac_scales(j):
-            nc.scalar.copy(out=ys_all[:, j].rearrange("p (n t) -> p n t", t=4), in_=st["spread"][:].rearrange("p t n -> p n t"))
-            give_bank("spread")
-
         def pair_tile(name, i, shape, dtype, reuse=None):
             if (name, i // 2) not in st:
                 st[name, i // 2] = work.tile([P, 2] + shape, dtype, tag=reuse or "%s%d" % (name, i // 2), name=name, bufs=1, align_bytes=64)
             return st[name, i // 2]
 
-        def widen(i):
-            yw = pair_tile("yw", i, [2, P, 2], BF16)
-            nc.vector.tensor_scalar(
-                out=yw[:, i % 2].rearrange("p u m e -> p m u e"),
-                in0=rows("y", i)[:, 0].bitcast(FP8).rearrange("p (m u e) -> p m u e", u=2, e=2),
-                scalar1=ones[:],
-                scalar2=None,
-                op0=MULT,
-            )
-
-        def widen_scalar(i, n=1):
-            yb = pair_tile("yb", i, [D], BF16)
-            nc.scalar.activation(out=yb[:, i % 2 : i % 2 + n], in_=rows("y", i, n).bitcast(FP8), func=ACT.Copy)
-
-        def widen_plain(i, n=1):
-            yb = pair_tile("wide", i, [D], BF16)
-            nc.vector.tensor_copy(out=yb[:, i % 2 : i % 2 + n], in_=rows("y", i, n).bitcast(FP8))
-
-        def widen_gpsimd(i, n=1):
-            yb = pair_tile("yb", i, [D], BF16)
-            nc.gpsimd.tensor_copy(out=yb[:, i % 2 : i % 2 + n], in_=rows("y", i, n).bitcast(FP8))
-
-        def scale_y(i, n=1):
-            turned = grp_slots(i)[:, slot(i, 0) : slot(i + n - 1, 0) + 1 : max(1, slot(1, 0) if i // 2 in BY_OPERAND else 2)]
-            nc.vector.tensor_tensor(out=turned, in0=turned, in1=ys_part[:].unsqueeze(1).unsqueeze(1).to_broadcast([P, n, P, 4]), op=MULT)
-
-        def yprod(i, n=1):
-            yb = pair_tile("yb", i, [D], BF16)
-            nc.vector.tensor_tensor(out=yb[:, i % 2 : i % 2 + n], in0=rows("y", i, n).bitcast(FP8), in1=ys_all[:, 0:n], op=MULT)
-
         def words_of(kind, i, u):
             if kind == "w":
                 return st["yw", i // 2][:, i % 2].rearrange("p u m e -> p u (m e)").bitcast(F32)[:, u, :]
+            if kind == "s":
+                return st["yb", i // 2][:, i % 2].rearrange("p u m e -> p u (m e)").bitcast(F32)[:, u, :]
             src = st["yb", i // 2][:, i % 2, :] if kind == "y" else rows("side", i)[:, 0]
             return src.bitcast(F32)[:, u : D // 2 : 2]
 
@@ -182,20 +140,10 @@ def tile_csdigatedsideinforesidual_w4_kernel(tc, y_bytes, y_scale, side, x, w_m_
         def grp_slots(i):
             return pair_tile("grp", i, [2, P, 4], BF16)[:].rearrange("p a b r t -> p (a b) r t")
 
-        def turn_ys(i, n):
-            turn(("ys", i), [("y", i + j) for j in range(n)])
-
-        def evac_ys(i, n):
-            nc.scalar.copy(out=grp_words(i)[:, i % 2 : i % 2 + n, 0], in_=st["ys", i][:].rearrange("p j u r -> p j r u"))
-            give_bank(("ys", i))
-
         def quant_slots(i, first, n):
             codes = pair_tile("codes", i, [2 * P], U32)[:].rearrange("p a c -> p (a c)")[:, first * P : (first + n) * P]
             scales = pair_tile("scales", i, [2 * P], U8)[:].rearrange("p a c -> p (a c)")[:, first * P : (first + n) * P]
             nc.vector.quantize_mx(out=codes.bitcast(FP8X4), scales=scales, in_=grp_slots(i)[:, first : first + n].rearrange("p a r t -> p (a r t)"))
-
-        def quant_operand(i, o, n=1):
-            quant_slots(i, slot(i, o), n)
 
         def turn_tile(i, kind="y"):
             turn(("tile", i), [(kind, i), ("side", i)])
@@ -203,26 +151,6 @@ def tile_csdigatedsideinforesidual_w4_kernel(tc, y_bytes, y_scale, side, x, w_m_
         def evac_tile(i):
             nc.scalar.copy(out=grp_words(i)[:, i % 2], in_=st["tile", i][:].rearrange("p o u r -> p o r u"))
             give_bank(("tile", i))
-
-        def turn_sides(i, n):
-            turn(("sides", i), [("side", i + j) for j in range(n)])
-
-        def evac_sides(i, n):
-            nc.scalar.copy(out=grp_words(i)[:, i % 2 : i % 2 + n, 1], in_=st["sides", i][:].rearrange("p j u r -> p j r u"))
-            give_bank(("sides", i))
-
-        def turn_y(i, kind):
-            turn(("ty", i), [(kind, i)])
-
-        def evac_y(i):
-            yt = st["ty", i][:].rearrange("p o u r -> p (o u r)").bitcast(BF16)
-            nc.vector.tensor_tensor(
-                out=grp_slots(i)[:, slot(i, 0)].rearrange("p r (u e) -> p r u e", e=2),
-                in0=yt.rearrange("p (u r e) -> p r u e", u=2, e=2),
-                in1=ys_part[:].rearrange("p (u e) -> p u e", e=2).unsqueeze(1).to_broadcast([P, P, 2, 2]),
-                op=MULT,
-            )
-            give_bank(("ty", i))
 
         def quant(i, n=1):
             quant_slots(i, 2 * (i % 2), 2 * n)
@@ -295,33 +223,6 @@ def tile_csdigatedsideinforesidual_w4_kernel(tc, y_bytes, y_scale, side, x, w_m_
                 stop=True,
             )
 
-        def o_part(i, h, c):
-            bank = take_bank(("o", h, i, c), [D // 2])
-            lo = D * h + D // 2 * c
-            nc.tensor.matmul_mx(
-                out=bank[:],
-                lhsT=st["ucodes", i // 2][:, i % 2].bitcast(FP8X4),
-                lhsT_scale=st["uscales", i // 2][:, i % 2],
-                rhs=wo[:, 2 * lo : 2 * lo + D].bitcast(FP4X4),
-                rhs_scale=wo_sc[:, lo : lo + D // 2],
-                start=True,
-                stop=True,
-            )
-
-        def skip_part(i, c):
-            cols = slice(D // 2 * c, D // 2 * (c + 1))
-            r = work.tile([P, D // 2], F32, tag="skp", name="skp", bufs=4, align_bytes=64)
-            nc.scalar.copy(out=r[:], in_=st["o", 1, i, c][:])
-            give_bank(("o", 1, i, c))
-            nc.sync.dma_start(out=skip_v[:, i, cols], in_=r[:])
-
-        def xnew_part(i, c):
-            cols = slice(D // 2 * c, D // 2 * (c + 1))
-            r = work.tile([P, D // 2], F32, tag="xnp", name="xnp", bufs=4, align_bytes=64)
-            nc.vector.scalar_tensor_tensor(out=r[:], in0=st["o", 0, i, c][:], scalar=RSQRT2, in1=st["xs", i // 2][:, i % 2, cols], op0=MULT, op1=ADD)
-            give_bank(("o", 0, i, c))
-            nc.sync.dma_start(out=xnew_v[:, i, cols], in_=r[:])
-
         def act_part(i, h, c):
             name, func = (("sg", ACT.Sigmoid), ("th", ACT.Tanh))[h]
             r = pair_tile(name, i, [4, P], F32)
@@ -343,11 +244,8 @@ def tile_csdigatedsideinforesidual_w4_kernel(tc, y_bytes, y_scale, side, x, w_m_
         def scale_x_scalar(i, n=2):
             nc.scalar.activation(out=pair_tile("xs", i, [D], F32)[:, i % 2 : i % 2 + n], in_=rows("x", i, n), func=ACT.Copy, scale=RSQRT2)
 
-        def scale_x_vector(i, n=2):
-            nc.vector.tensor_scalar(out=pair_tile("xs", i, [D], F32)[:, i % 2 : i % 2 + n], in0=rows("x", i, n), scalar1=RSQRT2, scalar2=None, op0=MULT)
-
-        def scale_x_gpsimd(i, reuse=None):
-            nc.gpsimd.tensor_scalar(out=pair_tile("xs", i, [D], F32, reuse)[:], in0=rows("x", i, 2), scalar1=RSQRT2, scalar2=0.0, op0=MULT, op1=ADD)
+        def scale_x_gpsimd(i, n=2, reuse=None):
+            nc.gpsimd.tensor_scalar(out=pair_tile("xs", i, [D], F32, reuse)[:, i % 2 : i % 2 + n], in0=rows("x", i, n), scalar1=RSQRT2, scalar2=0.0, op0=MULT, op1=ADD)
 
         def skip(i):
             r = work.tile([P, D], F32, tag="sk", name="sk", align_bytes=64)
@@ -361,19 +259,38 @@ def tile_csdigatedsideinforesidual_w4_kernel(tc, y_bytes, y_scale, side, x, w_m_
             give_bank(("o", 0, i))
             nc.sync.dma_start(out=xnew_v[:, i, :], in_=r[:])
 
-        def skip_pair(i):
-            r = pair_tile("sk", i, [D], F32)
-            nc.scalar.copy(out=r[:, i % 2], in_=st["o", 1, i][:])
-            give_bank(("o", 1, i))
-            if i % 2:
-                nc.sync.dma_start(out=skip_v[:, i - 1 : i + 1, :], in_=r[:])
+        def widen(i):
+            yw = pair_tile("yw", i, [2, P, 2], BF16)
+            nc.vector.tensor_scalar(
+                out=yw[:, i % 2].rearrange("p u m e -> p m u e"),
+                in0=rows("y", i)[:, 0].bitcast(FP8).rearrange("p (m u e) -> p m u e", u=2, e=2),
+                scalar1=ones[:],
+                scalar2=None,
+                op0=MULT,
+            )
 
-        def xnew_pair(i):
-            r = pair_tile("xn", i, [D], F32)
-            nc.vector.scalar_tensor_tensor(out=r[:, i % 2], in0=st["o", 0, i][:], scalar=RSQRT2, in1=st["xs", i // 2][:, i % 2], op0=MULT, op1=ADD)
-            give_bank(("o", 0, i))
-            if i % 2:
-                nc.sync.dma_start(out=xnew_v[:, i - 1 : i + 1, :], in_=r[:])
+        def turn_sides(i, n):
+            turn(("sides", i), [("side", i + j) for j in range(n)])
+
+        def evac_sides(i, n):
+            nc.scalar.copy(out=grp_words(i)[:, i % 2 : i % 2 + n, 1], in_=st["sides", i][:].rearrange("p j u r -> p j r u"))
+            give_bank(("sides", i))
+
+        def turn_y(i, kind):
+            turn(("ty", i), [(kind, i)])
+
+        def evac_y(i):
+            yt = st["ty", i][:].rearrange("p o u r -> p (o u r)").bitcast(BF16)
+            nc.vector.tensor_tensor(
+                out=grp_slots(i)[:, slot(i, 0)].rearrange("p r (u e) -> p r u e", e=2),
+                in0=yt.rearrange("p (u r e) -> p r u e", u=2, e=2),
+                in1=ys_part[:].rearrange("p (u e) -> p u e", e=2).unsqueeze(1).to_broadcast([P, P, 2, 2]),
+                op=MULT,
+            )
+            give_bank(("ty", i))
+
+        def scale_x_vector(i, n=2):
+            nc.vector.tensor_scalar(out=pair_tile("xs", i, [D], F32)[:, i % 2 : i % 2 + n], in0=rows("x", i, n), scalar1=RSQRT2, scalar2=None, op0=MULT)
 
         def zero(tile):
             nc.vector.memset(tile[:].bitcast(I32), 0)
@@ -401,9 +318,8 @@ def tile_csdigatedsideinforesidual_w4_kernel(tc, y_bytes, y_scale, side, x, w_m_
         load_rows("x", 0, 4)
         load_rows("x", 4, 8)
         warm_up(2)
-        spread_scales(2)
-        evac_scales(0)
-        evac_scales(1)
+        spread_sorted(1)
+        keep_scales()
         warm_up(2)
         widen(0)
         widen(1)
@@ -415,14 +331,15 @@ def tile_csdigatedsideinforesidual_w4_kernel(tc, y_bytes, y_scale, side, x, w_m_
         evac_y(0)
         yprod(3)
         warm_up(3)
-        turn_tile(2)
-        turn_tile(3)
+        turn_tile(2, "s")
+        turn_tile(3, "s")
         evac_tile(2)
         evac_tile(3)
         quant(0)
         evac_y(1)
         quant(1)
-        yprod(4, 2)
+        yprod(4)
+        yprod(5)
         z_by_operand(0)
         z_half(1, 0)
         z_half(1, 1)
@@ -431,12 +348,13 @@ def tile_csdigatedsideinforesidual_w4_kernel(tc, y_bytes, y_scale, side, x, w_m_
         act(1, 0)
         act(1, 1)
         quant(2, 2)
-        yprod(6, 2)
+        yprod(6)
+        yprod(7)
         uprod(0)
         uprod(1)
         scale_x_vector(0)
-        turn_tile(4)
-        turn_tile(5)
+        turn_tile(4, "s")
+        turn_tile(5, "s")
         evac_tile(4)
         evac_tile(5)
         quant(4, 2)
@@ -450,7 +368,7 @@ def tile_csdigatedsideinforesidual_w4_kernel(tc, y_bytes, y_scale, side, x, w_m_
         act(3, 1)
         turn_u(0)
         turn_u(1)
-        turn_tile(6)
+        turn_tile(6, "s")
         evac_tile(6)
         gain(0)
         gain(1)
@@ -468,14 +386,14 @@ def tile_csdigatedsideinforesidual_w4_kernel(tc, y_bytes, y_scale, side, x, w_m_
         uprod(4)
         turn_u(2)
         turn_u(3)
-        turn_tile(7)
+        turn_tile(7, "s")
         evac_tile(7)
         gain(2)
         gain(3)
         uprod(5)
         quant_u(2, 2)
         quant(7)
-        scale_x_gpsimd(2, "grp3")
+        scale_x_gpsimd(2, 2, "grp3")
         z_half(6, 0)
         o_half(0, 1)
         o_half(0, 0)
@@ -502,7 +420,7 @@ def tile_csdigatedsideinforesidual_w4_kernel(tc, y_bytes, y_scale, side, x, w_m_
         xnew(1)
         uprod(6)
         quant_u(4, 2)
-        scale_x_gpsimd(4, "ug2")
+        scale_x_gpsimd(4, 2, "ug2")
         xnew(2)
         xnew(3)
         turn_u(6)

@@ -193,8 +193,9 @@ def tile_csdigatedsideinforesidual_w4_kernel(tc, y_bytes, y_scale, side, x, w_m_
 
         def turn_u(i):
             bank = take_bank(("ut", i), [4, P])
+            u = st["u", i // 2][:, i % 2]
             for t in range(4):
-                nc.tensor.transpose(bank[:, t, :], st["u", i // 2][:, i % 2, t, :], ident[:])
+                nc.tensor.transpose(bank[:, t, :], u[:, t, :], ident[:])
 
         def gain(i):
             nc.vector.tensor_tensor(
@@ -297,7 +298,7 @@ def tile_csdigatedsideinforesidual_w4_kernel(tc, y_bytes, y_scale, side, x, w_m_
 
         nc.vector.memset(ones[:], 1.0)
         nc.scalar.activation(out=warm[:], in_=ones[:], func=ACT.Sigmoid)
-        nc.gpsimd.memset(zeros[:].bitcast(I32), 0)
+        nc.vector.memset(zeros[:].bitcast(I32), 0)
         make_identity(nc, ident[:])
         zero(wm_sc)
         zero(ws_sc)

@@ -120,12 +120,12 @@ def tile_csdigatedsideinforesidual_w4_kernel(tc, y_bytes, y_scale, side, x, w_m_
                 return st["yw", i // 2][:, i % 2].rearrange("p u m e -> p u (m e)").bitcast(F32)[:, u, :]
             if kind == "s":
                 return st["yb", i // 2][:, i % 2].rearrange("p u m e -> p u (m e)").bitcast(F32)[:, u, :]
-            src = st["yb", i // 2][:, i % 2, :] if kind == "y" else rows("side", i)[:, 0]
+            src = st["yb", i // 2][:, i % 2].rearrange("p u m e -> p (u m e)") if kind == "y" else rows("side", i)[:, 0]
             return src.bitcast(F32)[:, u : D // 2 : 2]
 
         def turn(key, operands, readers=1):
             bank = take_bank(key, [len(operands), 2, P], readers)
-            for o, (kind, i) in enumerate(operands):
+            for o, (kind, i) in reversed(list(enumerate(operands))):
                 for u in range(2):
                     nc.tensor.transpose(bank[:, o, u, :], words_of(kind, i, u), ident[:])
 
@@ -148,8 +148,8 @@ def tile_csdigatedsideinforesidual_w4_kernel(tc, y_bytes, y_scale, side, x, w_m_
         def turn_tile(i, kind="y"):
             turn(("tile", i), [(kind, i), ("side", i)])
 
-        def evac_tile(i):
-            nc.scalar.copy(out=grp_words(i)[:, i % 2], in_=st["tile", i][:].rearrange("p o u r -> p o r u"))
+        def evac_tile(i, copy=nc.scalar.copy):
+            copy(out=grp_words(i)[:, i % 2], in_=st["tile", i][:].rearrange("p o u r -> p o r u"))
             give_bank(("tile", i))
 
         def quant(i, n=1):
@@ -243,10 +243,16 @@ def tile_csdigatedsideinforesidual_w4_kernel(tc, y_bytes, y_scale, side, x, w_m_
                 nc.tensor.transpose(st["ut", i][:, t, :], st["u", i // 2][:, i % 2, t, :], ident[:])
 
         def scale_x_scalar(i, n=2):
-            nc.scalar.activation(out=pair_tile("xs", i, [D], F32)[:, i % 2 : i % 2 + n], in_=rows("x", i, n), func=ACT.Copy, scale=RSQRT2)
+            xs = work.tile([P, n, D], F32, tag="xs%d" % i, name="xs", bufs=1, align_bytes=64)
+            nc.scalar.activation(out=xs[:], in_=rows("x", i, n), func=ACT.Copy, scale=RSQRT2)
+            for j in range(n):
+                st["xs_of", i + j] = xs[:, j]
 
-        def scale_x_gpsimd(i, n=2, reuse=None):
-            nc.gpsimd.tensor_scalar(out=pair_tile("xs", i, [D], F32, reuse)[:, i % 2 : i % 2 + n], in0=rows("x", i, n), scalar1=RSQRT2, scalar2=0.0, op0=MULT, op1=ADD)
+        def scale_x_gpsimd(i, n, reuse):
+            xs = work.tile([P, n, D], F32, tag=reuse, name="xs", bufs=1, align_bytes=64)
+            nc.gpsimd.tensor_scalar(out=xs[:], in0=rows("x", i, n), scalar1=RSQRT2, scalar2=0.0, op0=MULT, op1=ADD)
+            for j in range(n):
+                st["xs_of", i + j] = xs[:, j]
 
         def skip(i):
             r = work.tile([P, D], F32, tag="sk", name="sk", align_bytes=64)
@@ -256,7 +262,7 @@ def tile_csdigatedsideinforesidual_w4_kernel(tc, y_bytes, y_scale, side, x, w_m_
 
         def xnew(i):
             r = work.tile([P, D], F32, tag="xn", name="xn", align_bytes=64)
-            nc.vector.scalar_tensor_tensor(out=r[:], in0=st["o", 0, i][:], scalar=RSQRT2, in1=st["xs", i // 2][:, i % 2], op0=MULT, op1=ADD)
+            nc.vector.scalar_tensor_tensor(out=r[:], in0=st["o", 0, i][:], scalar=RSQRT2, in1=st["xs_of", i], op0=MULT, op1=ADD)
             give_bank(("o", 0, i))
             nc.sync.dma_start(out=xnew_v[:, i, :], in_=r[:])
 
@@ -271,7 +277,10 @@ def tile_csdigatedsideinforesidual_w4_kernel(tc, y_bytes, y_scale, side, x, w_m_
             )
 
         def turn_sides(i, n):
-            turn(("sides", i), [("side", i + j) for j in range(n)])
+            bank = take_bank(("sides", i), [n, 2, P])
+            for j in range(n):
+                for u in range(2):
+                    nc.tensor.transpose(bank[:, j, u, :], words_of("side", i + j, u), ident[:])
 
         def evac_sides(i, n):
             nc.scalar.copy(out=grp_words(i)[:, i % 2 : i % 2 + n, 1], in_=st["sides", i][:].rearrange("p j u r -> p j r u"))
@@ -291,7 +300,10 @@ def tile_csdigatedsideinforesidual_w4_kernel(tc, y_bytes, y_scale, side, x, w_m_
             give_bank(("ty", i))
 
         def scale_x_vector(i, n=2):
-            nc.vector.tensor_scalar(out=pair_tile("xs", i, [D], F32)[:, i % 2 : i % 2 + n], in0=rows("x", i, n), scalar1=RSQRT2, scalar2=None, op0=MULT)
+            xs = work.tile([P, n, D], F32, tag="xs%d" % i, name="xs", bufs=1, align_bytes=64)
+            nc.vector.tensor_scalar(out=xs[:], in0=rows("x", i, n), scalar1=RSQRT2, scalar2=None, op0=MULT)
+            for j in range(n):
+                st["xs_of", i + j] = xs[:, j]
 
         def zero(tile):
             nc.vector.memset(tile[:].bitcast(I32), 0)
@@ -306,17 +318,17 @@ def tile_csdigatedsideinforesidual_w4_kernel(tc, y_bytes, y_scale, side, x, w_m_
         load_y_scale()
         load_rows("y", 0, 4)
         load_rows("side", 0, 2)
-        load_rows("side", 2, 4)
         load_scales(wm_sc, w_m_scales)
+        load_rows("side", 2, 4)
         load_words(wm, w_m_words)
         load_scales(ws_sc, w_s_scales)
         load_words(ws, w_s_words)
         load_rows("y", 4, 8)
         load_rows("side", 4, 8)
         load_gain()
-        load_scales(wo_sc, w_o_scales)
-        load_words(wo, w_o_words)
         load_rows("x", 0, 4)
+        load_words(wo, w_o_words)
+        load_scales(wo_sc, w_o_scales)
         load_rows("x", 4, 8)
         warm_up(2)
         spread_sorted(1)
@@ -331,7 +343,7 @@ def tile_csdigatedsideinforesidual_w4_kernel(tc, y_bytes, y_scale, side, x, w_m_
         yprod(2)
         evac_y(0)
         yprod(3)
-        warm_up(3)
+        warm_up(2)
         turn_tile(2, "s")
         turn_tile(3, "s")
         evac_tile(2)

from contextlib import ExitStack

import concourse.mybir as mybir
from concourse.masks import make_identity

N, D, E = 1024, 512, 512
FLOPS = 2 * N * (D + E + D) * 2 * D

F32 = mybir.dt.float32
BF16 = mybir.dt.bfloat16
U8 = mybir.dt.uint8
U32 = mybir.dt.uint32
I32 = mybir.dt.int32
FP8 = mybir.dt.float8_e4m3fn
FP8X4 = mybir.dt.float8_e4m3fn_x4
FP4X4 = mybir.dt.float4_e2m1fn_x4
MULT = mybir.AluOpType.mult
ADD = mybir.AluOpType.add
ACT = mybir.ActivationFunctionType

P = 128
TILES = N // P
RSQRT2 = 0.5 ** 0.5
BY_OPERAND = ()


def tile_csdigatedsideinforesidual_w4_kernel(tc, y_bytes, y_scale, side, x, w_m_words, w_m_scales, w_s_words, w_s_scales, g, w_o_words, w_o_scales, out_0, out_1):
    nc = tc.nc
    with ExitStack() as ctx:
        keep = ctx.enter_context(tc.tile_pool(name="keep", bufs=1))
        work = ctx.enter_context(tc.tile_pool(name="work", bufs=TILES))
        psum = ctx.enter_context(tc.psum_pool(name="psum", bufs=1))
        ctx.enter_context(tc.manual_schedule())

        y_v = y_bytes.rearrange("(p i) k -> p i k", i=TILES)
        side_v = side.rearrange("(p i) k -> p i k", i=TILES)
        x_v = x.rearrange("(p i) k -> p i k", i=TILES)
        xnew_v = out_0.rearrange("(p i) k -> p i k", i=TILES)
        skip_v = out_1.rearrange("(p i) k -> p i k", i=TILES)

        ys_part = keep.tile([P, 4], F32, name="ys_part")
        g_part = keep.tile([P, 4], BF16, name="g_part")
        ones = keep.tile([P, 1], F32, name="ones")
        ident = keep.tile([P, P], F32, name="ident")
        zeros = keep.tile([P, D], BF16, name="zeros", align_bytes=64)
        warm = keep.tile([P, 1], F32, name="warm")
        wm = keep.tile([P, 4 * D], U8, name="wm", align_bytes=64)
        ws = keep.tile([P, 4 * D], U8, name="ws", align_bytes=64)
        wo = keep.tile([P, 4 * D], U8, name="wo", align_bytes=64)
        wm_sc = keep.tile([P, 2 * D], U8, name="wm_sc", align_bytes=64)
        ws_sc = keep.tile([P, 2 * D], U8, name="ws_sc", align_bytes=64)
        ys_sorted = keep.tile([P, 2, P, 2], F32, name="ys_sorted", align_bytes=64)
        wo_sc = keep.tile([P, 2 * D], U8, name="wo_sc", align_bytes=64)

        st = {}
        free_banks = list(range(8))

        def take_bank(key, shape, readers=1):
            b = free_banks.pop(0)
            st[key] = psum.tile([P] + shape, F32, tag="bank%d" % b, name="bank")
            st["held", key] = [b, readers]
            return st[key]

        def give_bank(key):
            held = st["held", key]
            held[1] = held[1] - 1
            if held[1] == 0:
                free_banks.append(held[0])

        def load_scales(tile, dram, queue=nc.sync):
            for q in range(4):
                queue.dma_start(out=tile[32 * q : 32 * q + 4, :].bitcast(I32), in_=dram[0, 4 * q : 4 * q + 4, :].bitcast(I32))

        def load_rows(name, lo, hi, queue=nc.sync):
            view, dtype = {"y": (y_v, U8), "side": (side_v, BF16), "x": (x_v, BF16)}[name]
            tile = keep.tile([P, hi - lo, D], dtype, name="%s_in%d" % (name, lo), align_bytes=64)
            queue.dma_start(out=tile[:], in_=view[:, lo:hi, :])
            for i in range(lo, hi):
                st[name, i] = (tile, i - lo)

        def rows(name, i, n=1):
            tile, j = st[name, i]
            return tile[:, j : j + n, :]

        def load_words(tile, dram):
            nc.sync.dma_start(out=tile[:], in_=dram[0])

        def spread_sorted(copies):
            bank = take_bank("spread", [2, P, 2], copies)
            for t in range(4):
                nc.tensor.transpose(bank[:, t // 2, :, t % 2], ys_part[:, t : t + 1].to_broadcast([P, P]), ident[:])

        def keep_scales():
            nc.scalar.copy(out=ys_sorted[:], in_=st["spread"][:])
            give_bank("spread")

        def yprod(i):
            yb = pair_tile("yb", i, [2, P, 2], BF16)
            nc.vector.tensor_tensor(out=yb[:, i % 2], in0=rows("y", i)[:, 0].bitcast(FP8).rearrange("p (m u e) -> p u m e", u=2, e=2), in1=ys_sorted[:], op=MULT)

        def load_y_scale():
            nc.sync.dma_start(out=ys_part[:], in_=y_scale.rearrange("o (p t) -> p (o t)", t=4))

        def load_gain():
            nc.sync.dma_start(out=g_part[:], in_=g.rearrange("(p t) -> p t", t=4))

        def warm_up(n):
            bank = take_bank("warm", [D])
            for k in range(n):
                nc.tensor.matmul(bank[:], lhsT=zeros[:, 0:P], rhs=zeros[:], start=True, stop=True)
            give_bank("warm")

        def pair_tile(name, i, shape, dtype, reuse=None):
            if (name, i // 2) not in st:
                st[name, i // 2] = work.tile([P, 2] + shape, dtype, tag=reuse or "%s%d" % (name, i // 2), name=name, bufs=1, align_bytes=64)
            return st[name, i // 2]

        def words_of(kind, i, u):
            if kind == "w":
                return st["yw", i // 2][:, i % 2].rearrange("p u m e -> p u (m e)").bitcast(F32)[:, u, :]
            if kind == "s":
                return st["yb", i // 2][:, i % 2].rearrange("p u m e -> p u (m e)").bitcast(F32)[:, u, :]
            src = st["yb", i // 2][:, i % 2].rearrange("p u m e -> p (u m e)") if kind == "y" else rows("side", i)[:, 0]
            return src.bitcast(F32)[:, u : D // 2 : 2]

        def turn(key, operands, readers=1):
            bank = take_bank(key, [len(operands), 2, P], readers)
            for o, (kind, i) in reversed(list(enumerate(operands))):
                for u in range(2):
                    nc.tensor.transpose(bank[:, o, u, :], words_of(kind, i, u), ident[:])

        def grp_words(i):
            grp = pair_tile("grp", i, [2, P, 4], BF16)
            pattern = "p (o j r u) -> p j o r u" if i // 2 in BY_OPERAND else "p (j o r u) -> p j o r u"
            return grp[:].rearrange("p a b r t -> p (a b r t)").bitcast(F32).rearrange(pattern, j=2, o=2, u=2)

        def slot(i, o):
            return 2 * o + i % 2 if i // 2 in BY_OPERAND else 2 * (i % 2) + o

        def grp_slots(i):
            return pair_tile("grp", i, [2, P, 4], BF16)[:].rearrange("p a b r t -> p (a b) r t")

        def quant_slots(i, first, n):
            codes = pair_tile("codes", i, [2 * P], U32)[:].rearrange("p a c -> p (a c)")[:, first * P : (first + n) * P]
            scales = pair_tile("scales", i, [2 * P], U8)[:].rearrange("p a c -> p (a c)")[:, first * P : (first + n) * P]
            nc.vector.quantize_mx(out=codes.bitcast(FP8X4), scales=scales, in_=grp_slots(i)[:, first : first + n].rearrange("p a r t -> p (a r t)"))

        def turn_tile(i, kind="y"):
            turn(("tile", i), [(kind, i), ("side", i)])

        def evac_tile(i, copy=nc.scalar.copy):
            copy(out=grp_words(i)[:, i % 2], in_=st["tile", i][:].rearrange("p o u r -> p o r u"))
            give_bank(("tile", i))

        def quant(i, n=1):
            quant_slots(i, 2 * (i % 2), 2 * n)

        def z_pass(i, h, o):
            codes, scales = [st[name, i // 2][:].rearrange("p a c -> p (a c)")[:, slot(i, o) * P : (slot(i, o) + 1) * P] for name in ("codes", "scales")]
            w, sc = ((wm, wm_sc), (ws, ws_sc))[o]
            first = ("z", h, i) not in st
            if first:
                take_bank(("z", h, i), [D])
            nc.tensor.matmul_mx(
                out=st["z", h, i][:],
                lhsT=codes.bitcast(FP8X4),
                lhsT_scale=scales,
                rhs=w[:, 2 * D * h : 2 * D * (h + 1)].bitcast(FP4X4),
                rhs_scale=sc[:, D * h : D * (h + 1)],
                start=first,
                stop=not first,
            )

        def z_half(i, h):
            z_pass(i, h, 0)
            z_pass(i, h, 1)

        def z_by_operand(i):
            for o in range(2):
                for h in range(2):
                    z_pass(i, h, o)

        def act(i, h):
            name, func = (("sg", ACT.Sigmoid), ("th", ACT.Tanh))[h]
            r = pair_tile(name, i, [4, P], F32)
            nc.scalar.activation(out=r[:, i % 2], in_=st["z", h, i][:].rearrange("p (m t) -> p t m", t=4), func=func)
            give_bank(("z", h, i))

        def uprod(i, n=1):
            u = pair_tile("u", i, [4, P], F32)
            both_tiles = slice(i % 2, i % 2 + n)
            nc.vector.tensor_tensor(out=u[:, both_tiles], in0=st["sg", i // 2][:, both_tiles], in1=st["th", i // 2][:, both_tiles], op=MULT)

        def turn_u(i):
            bank = take_bank(("ut", i), [4, P])
            u = st["u", i // 2][:, i % 2]
            for t in range(4):
                nc.tensor.transpose(bank[:, t, :], u[:, t, :], ident[:])

        def gain(i):
            nc.vector.tensor_tensor(
                out=pair_tile("ug", i, [P, 4], BF16)[:, i % 2],
                in0=st["ut", i][:].rearrange("p t r -> p r t"),
                in1=g_part[:].unsqueeze(1).to_broadcast([P, P, 4]),
                op=MULT,
            )
            give_bank(("ut", i))

        def quant_u(i, n=1):
            codes = pair_tile("ucodes", i, [P], U32)[:, i % 2 : i % 2 + n].rearrange("p j c -> p (j c)")
            scales = pair_tile("uscales", i, [P], U8)[:, i % 2 : i % 2 + n].rearrange("p j c -> p (j c)")
            ug = st["ug", i // 2][:, i % 2 : i % 2 + n].rearrange("p j r t -> p (j r t)")
            nc.vector.quantize_mx(out=codes.bitcast(FP8X4), scales=scales, in_=ug)

        def o_half(i, h):
            bank = take_bank(("o", h, i), [D])
            nc.tensor.matmul_mx(
                out=bank[:],
                lhsT=st["ucodes", i // 2][:, i % 2].bitcast(FP8X4),
                lhsT_scale=st["uscales", i // 2][:, i % 2],
                rhs=wo[:, 2 * D * h : 2 * D * (h + 1)].bitcast(FP4X4),
                rhs_scale=wo_sc[:, D * h : D * (h + 1)],
                start=True,
                stop=True,
            )

        def act_part(i, h, c):
            name, func = (("sg", ACT.Sigmoid), ("th", ACT.Tanh))[h]
            r = pair_tile(name, i, [4, P], F32)
            nc.scalar.activation(out=r[:, i % 2, 2 * c : 2 * c + 2], in_=st["z", h, i][:].rearrange("p (m t) -> p t m", t=4)[:, 2 * c : 2 * c + 2], func=func)
            if c == 1:
                give_bank(("z", h, i))

        def uprod_part(i, c):
            u = pair_tile("u", i, [4, P], F32)
            planes = slice(2 * c, 2 * c + 2)
            nc.vector.tensor_tensor(out=u[:, i % 2, planes], in0=st["sg", i // 2][:, i % 2, planes], in1=st["th", i // 2][:, i % 2, planes], op=MULT)

        def turn_u_part(i, c):
            if c == 0:
                take_bank(("ut", i), [4, P])
            for t in range(2 * c, 2 * c + 2):
                nc.tensor.transpose(st["ut", i][:, t, :], st["u", i // 2][:, i % 2, t, :], ident[:])

        def scale_x_scalar(i, n=2):
            xs = work.tile([P, n, D], F32, tag="xs%d" % i, name="xs", bufs=1, align_bytes=64)
            nc.scalar.activation(out=xs[:], in_=rows("x", i, n), func=ACT.Copy, scale=RSQRT2)
            for j in range(n):
                st["xs_of", i + j] = xs[:, j]

        def scale_x_gpsimd(i, n, reuse):
            xs = work.tile([P, n, D], F32, tag=reuse, name="xs", bufs=1, align_bytes=64)
            nc.gpsimd.tensor_scalar(out=xs[:], in0=rows("x", i, n), scalar1=RSQRT2, scalar2=0.0, op0=MULT, op1=ADD)
            for j in range(n):
                st["xs_of", i + j] = xs[:, j]

        def skip(i):
            r = work.tile([P, D], F32, tag="sk", name="sk", align_bytes=64)
            nc.scalar.copy(out=r[:], in_=st["o", 1, i][:])
            give_bank(("o", 1, i))
            nc.sync.dma_start(out=skip_v[:, i, :], in_=r[:])

        def xnew(i):
            r = work.tile([P, D], F32, tag="xn", name="xn", align_bytes=64)
            nc.vector.scalar_tensor_tensor(out=r[:], in0=st["o", 0, i][:], scalar=RSQRT2, in1=st["xs_of", i], op0=MULT, op1=ADD)
            give_bank(("o", 0, i))
            nc.sync.dma_start(out=xnew_v[:, i, :], in_=r[:])

        def widen(i):
            yw = pair_tile("yw", i, [2, P, 2], BF16)
            nc.vector.tensor_scalar(
                out=yw[:, i % 2].rearrange("p u m e -> p m u e"),
                in0=rows("y", i)[:, 0].bitcast(FP8).rearrange("p (m u e) -> p m u e", u=2, e=2),
                scalar1=ones[:],
                scalar2=None,
                op0=MULT,
            )

        def turn_sides(i, n):
            bank = take_bank(("sides", i), [n, 2, P])
            for j in range(n):
                for u in range(2):
                    nc.tensor.transpose(bank[:, j, u, :], words_of("side", i + j, u), ident[:])

        def evac_sides(i, n):
            nc.scalar.copy(out=grp_words(i)[:, i % 2 : i % 2 + n, 1], in_=st["sides", i][:].rearrange("p j u r -> p j r u"))
            give_bank(("sides", i))

        def turn_y(i, kind):
            turn(("ty", i), [(kind, i)])

        def evac_y(i):
            yt = st["ty", i][:].rearrange("p o u r -> p (o u r)").bitcast(BF16)
            nc.vector.tensor_tensor(
                out=grp_slots(i)[:, slot(i, 0)].rearrange("p r (u e) -> p r u e", e=2),
                in0=yt.rearrange("p (u r e) -> p r u e", u=2, e=2),
                in1=ys_part[:].rearrange("p (u e) -> p u e", e=2).unsqueeze(1).to_broadcast([P, P, 2, 2]),
                op=MULT,
            )
            give_bank(("ty", i))

        def scale_x_vector(i, n=2):
            xs = work.tile([P, n, D], F32, tag="xs%d" % i, name="xs", bufs=1, align_bytes=64)
            nc.vector.tensor_scalar(out=xs[:], in0=rows("x", i, n), scalar1=RSQRT2, scalar2=None, op0=MULT)
            for j in range(n):
                st["xs_of", i + j] = xs[:, j]

        def zero(tile):
            nc.vector.memset(tile[:].bitcast(I32), 0)

        nc.vector.memset(ones[:], 1.0)
        nc.scalar.activation(out=warm[:], in_=ones[:], func=ACT.Sigmoid)
        nc.vector.memset(zeros[:].bitcast(I32), 0)
        make_identity(nc, ident[:])
        zero(wm_sc)
        zero(ws_sc)
        zero(wo_sc)
        load_y_scale()
        load_rows("y", 0, 4)
        load_rows("side", 0, 2)
        load_scales(wm_sc, w_m_scales)
        load_rows("side", 2, 4)
        load_words(wm, w_m_words)
        load_scales(ws_sc, w_s_scales)
        load_words(ws, w_s_words)
        load_rows("y", 4, 8)
        load_rows("side", 4, 8)
        load_gain()
        load_rows("x", 0, 4)
        load_words(wo, w_o_words)
        load_scales(wo_sc, w_o_scales)
        load_rows("x", 4, 8)
        warm_up(2)
        spread_sorted(1)
        keep_scales()
        warm_up(2)
        widen(0)
        widen(1)
        turn_y(0, "w")
        turn_sides(0, 2)
        turn_y(1, "w")
        evac_sides(0, 2)
        yprod(2)
        evac_y(0)
        yprod(3)
        warm_up(2)
        turn_tile(2, "s")
        turn_tile(3, "s")
        evac_tile(2)
        evac_tile(3)
        quant(0)
        evac_y(1)
        quant(1)
        yprod(4)
        yprod(5)
        z_by_operand(0)
        z_half(1, 0)
        z_half(1, 1)
        act(0, 0)
        act(0, 1)
        act(1, 0)
        act(1, 1)
        quant(2, 2)
        yprod(6)
        yprod(7)
        uprod(0)
        uprod(1)
        scale_x_vector(0)
        turn_tile(4, "s")
        turn_tile(5, "s")
        evac_tile(4)
        evac_tile(5)
        quant(4, 2)
        z_half(2, 0)
        z_half(2, 1)
        z_half(3, 0)
        z_half(3, 1)
        act(2, 0)
        act(2, 1)
        act(3, 0)
        act(3, 1)
        turn_u(0)
        turn_u(1)
        turn_tile(6, "s")
        evac_tile(6)
        gain(0)
        gain(1)
        uprod(2, 2)
        quant_u(0, 2)
        quant(6)
        z_half(4, 0)
        z_half(4, 1)
        z_half(5, 0)
        z_half(5, 1)
        act(4, 0)
        act(4, 1)
        act(5, 0)
        act(5, 1)
        uprod(4)
        turn_u(2)
        turn_u(3)
        turn_tile(7, "s")
        evac_tile(7)
        gain(2)
        gain(3)
        uprod(5)
        quant_u(2, 2)
        quant(7)
        scale_x_gpsimd(2, 2, "grp3")
        z_half(6, 0)
        o_half(0, 1)
        o_half(0, 0)
        o_half(1, 1)
        skip(0)
        skip(1)
        act(6, 0)
        xnew(0)
        turn_u(4)
        turn_u(5)
        gain(4)
        gain(5)
        z_half(6, 1)
        o_half(1, 0)
        o_half(2, 1)
        o_half(2, 0)
        o_half(3, 1)
        o_half(3, 0)
        z_half(7, 0)
        z_half(7, 1)
        act(6, 1)
        skip(2)
        skip(3)
        xnew(1)
        uprod(6)
        quant_u(4, 2)
        scale_x_gpsimd(4, 2, "ug2")
        xnew(2)
        xnew(3)
        turn_u(6)
        gain(6)
        act(7, 0)
        act_part(7, 1, 0)
        act_part(7, 1, 1)
        o_half(4, 1)
        o_half(4, 0)
        o_half(5, 1)
        o_half(5, 0)
        skip(4)
        skip(5)
        scale_x_scalar(6, 2)
        uprod_part(7, 0)
        uprod_part(7, 1)
        quant_u(6)
        turn_u_part(7, 0)
        turn_u_part(7, 1)
        xnew(4)
        o_half(6, 1)
        o_half(6, 0)
        skip(6)
        gain(7)
        xnew(5)
        quant_u(7)
        xnew(6)
        o_half(7, 0)
        o_half(7, 1)
        xnew(7)
        skip(7)
